import numpy as np, ml_dtypes
CORES = [40,41,42,43,44,45,46,47]
N = 8
BF = ml_dtypes.bfloat16
def gentries(a):
    return np.ascontiguousarray(a.reshape(8, 16, -1).transpose(0, 2, 1)).reshape(8, -1)
def gtable(e):
    e = np.asarray(e); return np.ascontiguousarray(e.reshape(8, -1, 16).transpose(0, 2, 1)).reshape(128, -1).astype(np.int32)
V, B, P, T, RO = 1024, 2768, 256, 48, 2
C, M, GH = V + P * RO, B + P * RO, (N - 1) * T
I, SEV = B - GH, 176
THETA, DELTA = (465, 580), (7, 9)
def wire(rng, bias, edge=False, crowd=None, hole=None, full=()):
    en = np.zeros((N, 8, 2, B), np.int64); bl = np.full((N, 8, 16, V), -1, np.int64); snd = np.zeros((N, 8, N - 1, T), np.int64)
    for q in range(N):
        for g in range(8):
            if crowd is not None and crowd[g] >= 0:
                s = (rng.permutation(V)[:, None] * 16 + np.arange(16)).reshape(-1)
                a, z, w = s[:I].copy(), np.roll(s[I:2 * I], crowd[g]), s[2 * I:2 * I + GH].copy()
            else:
                key = rng.random((V, 16)) + bias[q, g][:, None]
                if hole is not None: key = key + 99.0 * (np.arange(16)[None, :] == hole[q, g][:, None])
                s = np.argsort(key.reshape(-1))[:2 * I + GH]; s = s[rng.permutation(2 * I + GH)]
                a, z, w = s[:I].copy(), s[I:2 * I].copy(), s[2 * I:].copy()
                if g in full:
                    s = s[np.argsort(bias[q, g][s // 16] >= 0, kind="stable")]; w, a, z = s[:GH].copy(), s[GH:GH + I].copy(), s[GH + I:].copy()
                    m = rng.random(I) < 0.5; a, z = np.where(m, z, a), np.where(m, a, z)
                for i in np.flatnonzero(a // 16 == z // 16):
                    if a[i] // 16 == z[i] // 16:
                        j = np.flatnonzero((z // 16 != a[i] // 16) & (a // 16 != z[i] // 16)); j = int(j[rng.integers(0, len(j))])
                        zi, zj = int(z[i]), int(z[j]); z[i] = zj; z[j] = zi
            if edge: o = np.concatenate([GH // 2 + rng.permutation(I), rng.permutation(np.concatenate([np.arange(GH // 2), np.arange(GH // 2 + I, B)]))])
            else: o = rng.permutation(B)
            k, tw = o[:I], o[I:]
            en[q, g, 0, k] = a // 16; en[q, g, 1, k] = z // 16
            bl[q, g, a % 16, a // 16] = k; bl[q, g, z % 16, z // 16] = k; bl[q, g, w % 16, w // 16] = tw
            snd[q, g] = tw.reshape(N - 1, T); far = C + np.arange(GH); first = (q + 1 + np.arange(GH) // T) % N > q
            en[q, g, 0, tw] = np.where(first, w // 16, far); en[q, g, 1, tw] = np.where(first, far, w // 16)
    return en, bl, snd
def cells(rng, s, swing):
    lead, n = s.shape[:-1], s.shape[-1]; base = (s >> 4)[..., None, :]
    x = base + (np.argsort(rng.random(lead + (16, n)), axis=-2) < (s & 15)[..., None, :])
    room = np.clip(np.minimum(base, 62 - base), 0, swing)
    z = (rng.random(lead + (8, n)) * (room + 1)).astype(np.int64) * (1 - 2 * rng.integers(0, 2, lead + (8, n)))
    x[..., 0::2, :] += z; x[..., 1::2, :] -= z
    return x
def twin(y, snd):
    for q in range(N):
        for d in range(1, N):
            r = (q + d) % N
            if q < r:
                for g in range(8): y[r, g][:, snd[r, g, N - 1 - d]] = y[q, g][:, snd[q, g, d - 1]]
    return y
def xsums(rng): return np.clip(rng.integers(100, 901, (N, 8, V)) + rng.integers(-260, 65, (N, 8, 1)), 0, 1008)
def ysums(rng, share): return np.where(rng.random((N, 8, B)) < share, SEV + (rng.integers(0, 640, (N, 8, B)) * rng.random((N, 8, B))).astype(np.int64), rng.integers(0, SEV, (N, 8, B)))
def pack(x, y, en, bl, snd):
    return {"x0": np.ascontiguousarray(x.reshape(N, 128, V)).astype(np.float32).astype(BF), "y0": np.ascontiguousarray(y.reshape(N, 128, B)).astype(np.float32).astype(BF),
            "bl0": np.ascontiguousarray(bl.reshape(N, 128, V)).astype(np.int32), "en0": np.ascontiguousarray(en.reshape(N, 16, B)).astype(np.int32), "snd": np.stack([gtable(a.reshape(8, -1)) for a in snd])}
def setup_inputs(rng):
    en, bl, snd = wire(rng, 0.6 * rng.random((N, 8, V)))
    return pack(cells(rng, xsums(rng), 12), twin(cells(rng, ysums(rng, 0.92), 12), snd), en, bl, snd)
def setup_inputs_spread(rng):
    en, bl, snd = wire(rng, 2.0 * rng.random((N, 8, V)))
    ex = rng.choice(np.array([0.3, 0.7, 1.0, 2.0, 4.0]), (N, 8, 1, V)); ey = rng.choice(np.array([0.2, 1.0, 3.0, 6.0]), (N, 8, 1, B))
    x = np.minimum((64 * rng.random((N, 8, 16, V)) ** ex).astype(np.int64), 63); y = np.minimum((64 * rng.random((N, 8, 16, B)) ** ey).astype(np.int64), 63)
    return pack(x, twin(y, snd), en, bl, snd)
def setup_inputs_ends(rng):
    en, bl, snd = wire(rng, np.zeros((N, 8, 1)) - np.abs(2 * np.arange(V) - (V - 1)) * 9.0 / V, edge=True)
    pat = np.argsort(rng.random((8, 16)), axis=1) < 8; gi = np.arange(8)[None, :, None]
    kinds = np.stack([np.ones((8, 16), bool), pat, ~pat, np.zeros((8, 16), bool)]).astype(np.int64) * 63
    key = rng.random((N, 8, V)); key[..., 0] = -1.0; key[..., V - 1] = -2.0
    go = np.where(gi % 2 == 0, key < 0.75, np.argsort(np.argsort(key, axis=2), axis=2) < P)
    kx = rng.integers(0, 3, (N, 8, V)); kx[..., 0] = 0; kx[..., V - 1] = 0
    x = kinds[np.where(go, kx, 3), gi].transpose(0, 1, 3, 2)
    ky = rng.choice(5, (N, 8, B), p=[0.2, 0.35, 0.2, 0.1, 0.15]); ky[:, 7] = np.where(ky[:, 7] >= 3, 1, ky[:, 7])
    y = np.ascontiguousarray(kinds[np.minimum(ky, 3), gi].transpose(0, 1, 3, 2))
    y = np.where((ky == 4)[:, :, None, :], 63 * rng.integers(0, 2, y.shape), y)
    return pack(x, twin(y, snd), en, bl, snd)
def setup_inputs_corners(rng):
    bias = rng.choice(np.array([-9.0, 0.0, 9.0]), (N, 8, V), p=[0.25, 0.55, 0.2]); bias[..., 0] = -9.0; bias[..., V - 1] = -9.0
    hole = np.where(rng.random((N, 8, V)) < 0.6, 15, rng.integers(0, 16, (N, 8, V))); hole = np.where((bias < 0) & (rng.random((N, 8, V)) < 0.6), hole, -1); hole[..., 0] = -1; hole[..., V - 1] = -1
    en, bl, snd = wire(rng, bias, hole=hole)
    s = rng.choice(np.array([SEV, SEV - 1, SEV + 1, 1008, 0]), (N, 8, B), p=[0.3, 0.2, 0.2, 0.15, 0.15]); s = np.where(rng.random((N, 8, B)) < 0.5, s, ysums(rng, 0.9))
    y = cells(rng, s, 12); y[:, 3] = 22; y[:, 5] = 52; y = twin(y, snd)
    thr = THETA[0] + (np.add.reduce((np.add.reduce(y, axis=2) >= SEV).astype(np.int64), axis=2) & 31)[:, :, None]
    n = rng.choice(np.array([0, 1, P - 1, P, P + 1, V]), (N, 8)); n[:, 3] = P; n[:, 5] = P + 1; n[0] = (0, 1, P - 1, P, P + 1, P + 1, V, P)
    hot = np.argsort(rng.random((N, 8, V)), axis=2) < n[:, :, None]
    up = np.where(rng.random((N, 8, V)) < 0.5, thr, thr + (rng.random((N, 8, V)) * (1009 - thr)).astype(np.int64))
    down = np.where(rng.random((N, 8, V)) < 0.5, thr - 1, (rng.random((N, 8, V)) * thr).astype(np.int64))
    x = cells(rng, np.where(hot, up, down), 12); x[:, 3] = np.where(hot[:, 3], 63, 0)[:, None, :]; x[:, 5] = np.where(hot[:, 5], 32, 0)[:, None, :]
    return pack(x, y, en, bl, snd)
def setup_inputs_crowd(rng):
    go = np.argsort(rng.random((N, 8, V)), axis=2) < P; two = [2, 7]
    bias = np.zeros((N, 8, V)); bias[:, two] = np.where(go[:, two], -9.0, 0.0)
    en, bl, snd = wire(rng, bias, crowd=(0, 1, -1, 0, 1, 0, 1, -1), full=(2, 7))
    s = xsums(rng); s[:, :2] = rng.integers(510, 1009, (N, 2, V)); s[:, 3] = rng.integers(510, 1009, (N, V)); s[np.arange(N), 3, rng.integers(0, V, N)] = rng.integers(0, 400, N)
    s[:, 5:7] = THETA[0] + np.array([B & 31, (B - 1) & 31])[None, :, None] + rng.choice(np.array([-40, -1, 0, 1, 40]), (N, 2, V), p=[0.1, 0.4, 0.3, 0.1, 0.1])
    t = ysums(rng, 0.9); live = ysums(rng, 2.0)
    for g in (0, 1, 3, 4, 5, 6): t[:, g] = live[:, g]
    y = cells(rng, t, 12); y[:, two] = rng.integers(52, 64, (N, 2, 16, B)); y = twin(y, snd)
    for q in range(N):
        for g in (1, 4, 6): y[q, g][:, int(rng.choice(np.setdiff1d(np.arange(B), snd[q, g].reshape(-1))))] = 10
        go[q, 2, int(rng.choice(np.flatnonzero(go[q, 2])))] = False
    x = cells(rng, s, 12); x[:, two] = np.where(go[:, two][:, :, None, :], rng.integers(32, 41, (N, 2, 16, V)), rng.integers(0, 8, (N, 2, 16, V)))
    return pack(x, y, en, bl, snd)
def check_inputs(d):
    bad = []
    for k, lo, hi in (("x0", 0, 63), ("y0", 0, 63), ("bl0", -1, B - 1), ("en0", 0, C + GH - 1), ("snd", 0, B - 1)):
        a = np.asarray(d[k]).astype(np.float64)
        if not (np.min(a) >= lo and np.max(a) <= hi and np.all(a == np.floor(a))): bad.append("range of " + k)
    if bad: return bad
    en = d["en0"].astype(np.int64).reshape(N, 8, 2, B); bl = d["bl0"].astype(np.int64).reshape(N, 8, 16, V)
    sl = np.stack([gentries(a) for a in d["snd"]]).astype(np.int64); y = d["y0"].astype(np.float32).reshape(N, 8, 16, B)
    for q in range(N):
        for g in range(8):
            s, e = sl[q, g], en[q, g]; tw = np.zeros(B, bool); tw[s] = True
            if len(np.unique(s)) < GH: bad.append("twins of snd differ")
            if np.any(e[:, ~tw] >= V) or np.any(e[0, ~tw] == e[1, ~tw]): bad.append("ends of en0 on one rank")
            first = (q + 1 + np.arange(GH) // T) % N > q; own = np.where(first, e[0, s], e[1, s]); far = np.where(first, e[1, s], e[0, s])
            if np.any(own >= V) or np.any(far != C + np.arange(GH)): bad.append("ends of en0 of twins")
            r, c = np.nonzero(bl[q, g] >= 0); have = np.sort(bl[q, g][r, c] * V + c)
            want = np.sort((np.arange(B)[None, :] * V + e)[e < V])
            if len(have) != len(want) or np.any(have != want): bad.append("slots of bl0")
        for k in range(1, N):
            r = (q + k) % N
            for g in range(8):
                if np.any(y[q, g][:, sl[q, g].reshape(N - 1, T)[k - 1]] != y[r, g][:, sl[r, g].reshape(N - 1, T)[N - 1 - k]]): bad.append("y0 of twins alike")
    return sorted(set(bad))
def reference(x0, y0, bl0, en0, snd):
    x = np.zeros((N, 8, 16, C), np.int32); x[..., :V] = x0.astype(np.float32).astype(np.int32).reshape(N, 8, 16, V)
    y = np.zeros((N, 8, 16, M), np.int32); y[..., :B] = y0.astype(np.float32).astype(np.int32).reshape(N, 8, 16, B)
    bits = y[..., :1024] & 7
    exists = np.zeros((N, 8, C), bool); exists[..., :V] = True
    bl = np.full((N, 8, 16, C), -1, np.int64); bl[..., :V] = bl0.reshape(N, 8, 16, V)
    en = np.zeros((N, 8, 2, M), np.int64); en[..., :B] = en0.reshape(N, 8, 2, B)
    sl = np.stack([gentries(a) for a in snd]).astype(np.int64).reshape(N, 8, N - 1, T)
    take = np.take_along_axis
    for t in range(RO):
        live = np.add.reduce(y, axis=2) >= SEV
        count = np.add.reduce(live.astype(np.int64), axis=2)
        cand = np.add.reduce(x, axis=2) >= THETA[t] + (count & 31)[:, :, None]
        place = np.add.accumulate(cand.astype(np.int64), axis=2) - cand
        div = cand & (place < P)
        low = np.where(div[:, :, None], np.maximum(x - DELTA[t], 0), x); high = np.where(div[:, :, None], np.minimum(x + DELTA[t], 63), x)
        own = [[take(en[q, :, 0 if q < (q + d) % N else 1], sl[q, :, d - 1], 1) for d in range(1, N)] for q in range(N)]
        for q in range(N):
            wl, wh, wd = [low[q]], [high[q]], [div[q]]
            for d in range(1, N):
                r = (q + d) % N; c = own[r][N - 1 - d]
                wl.append(take(low[r], c[:, None, :], 2)); wh.append(take(high[r], c[:, None, :], 2)); wd.append(take(div[r], c, 1))
            wl, wh, wd = np.concatenate(wl, axis=2), np.concatenate(wh, axis=2), np.concatenate(wd, axis=1)
            e = en[q].copy(); a = [take(w, e[:, 0][:, None, :], 2) for w in (wl, wh)]; z = [take(w, e[:, 1][:, None, :], 2) for w in (wl, wh)]
            score = np.stack([np.add.reduce(np.abs(2 * y[q] - a[i] - z[j]), axis=1) for i in (0, 1) for j in (0, 1)])
            best = np.argmin(score, axis=0); pole = np.stack([best >> 1, best & 1], axis=1)
            touched = live[q] & (take(wd, e[:, 0], 1) | take(wd, e[:, 1], 1))
            gap = np.abs(np.where((pole[:, 0] == 1)[:, None], a[1], a[0]) - np.where((pole[:, 1] == 1)[:, None], z[1], z[0]))
            yn = np.where(touched[:, None], (y[q] + gap) >> 1, y[q]); stays_live = np.add.reduce(yn, axis=1) >= SEV
            move = touched[:, None] & (e < C) & (pole == 1); ne = np.where(move, V + P * t + take(place[q][:, None, :], np.minimum(e, C - 1), 2), e)
            for g in range(8):
                v = np.flatnonzero(div[q, g]); n = V + P * t + np.arange(len(v)); old = bl[q, g][:, v]; b = np.maximum(old, 0)
                keep = (old >= 0) & stays_live[g][b]; side = np.where(e[g, 0][b] == v[None, :], pole[g, 0][b], pole[g, 1][b])
                tv = np.where(keep & (side == 0), old, -1); tn = np.where(keep & (side == 1), old, -1)
                k = np.flatnonzero(np.any(tv < 0, axis=0) & np.any(tn < 0, axis=0)); nb = B + P * t + k
                rv, rn = np.argmax(tv < 0, axis=0)[k], np.argmax(tn < 0, axis=0)[k]
                tv[rv, k] = nb; tn[rn, k] = nb
                bl[q, g][:, v] = tv; bl[q, g][:, n] = tn
                yn[g][:, nb] = high[q, g][:, v[k]] - low[q, g][:, v[k]]; ne[g, 0, nb] = v[k]; ne[g, 1, nb] = n[k]
                x[q, g][:, v] = low[q, g][:, v]; x[q, g][:, n] = high[q, g][:, v]; exists[q, g, n] = True
            y[q] = yn; en[q] = ne
        if t + 1 < RO:
            x = np.where(exists[:, :, None], np.minimum(np.maximum(x + np.take(bits, (np.arange(C) + 331 * t) & 1023, axis=3) - 3, 0), 63), x)
    return {"yx": x.reshape(N, 128, C).astype(np.float32).astype(BF), "yy": y.reshape(N, 128, M).astype(np.float32).astype(BF),
            "yl": bl.reshape(N, 128, C).astype(np.float32), "ye": en.reshape(N, 16, M).astype(np.float32)}

@@ -1,0 +1,742 @@
+import numpy as np
+from concourse.bass import DstId, RemoteDMATransfer
+from concourse.mybir import AluOpType as A, AxisListType as AX, ActivationFunctionType as F
+
+V, B, P, C, GH = 1024, 2768, 256, 1536, 336
+THETA, DELTA = (465, 580), (7, 9)
+CW = C + GH
+LO, HZ, HA, Y0, Y1, WEND = 16, 16 + CW, 16 + 2 * CW, 16 + 3 * CW, 16 + 3 * CW + B, 16 + 3 * CW + B + B + P
+KB = 173
+MAG = 1.5 * 2 ** 23
+
+bf, f4, i4, u2 = "bfloat16", "float32", "int32", "uint16"
+SB = {
+    "win": ([WEND], bf), "lw": ([2 * CW], bf), "hif": ([C], bf), "lof": ([1280], bf), "yn": ([B], bf), "xa": ([1280], bf), "xb": ([1280], bf),
+    "yo": ([16, KB], bf), "yon": ([512], bf), "bli": ([V], i4), "bl": ([C], f4), "ylo": ([C], f4),
+    "eni": ([2, 176], i4), "e0": ([384], f4), "e1": ([384], f4), "e2": ([384], f4), "eu": ([384], u2), "ofs": ([384], u2),
+    "sni": ([24], i4), "snf": ([96], f4), "snu": ([48], u2), "mk": ([GH], f4), "gm": ([GH], f4), "ow": ([42], u2),
+    "sb0": ([672], bf), "sb1": ([672], bf), "land0": ([7, 96], bf), "land1": ([7, 96], bf), "fh": ([GH], bf),
+    "tu": ([2048], bf), "t00": ([2048], bf), "t01": ([2048], bf), "wa": ([2048], bf),
+    "a00": ([2048], bf), "a01": ([2048], bf), "a10": ([2048], bf), "a11": ([2048], bf),
+    "ga": ([2048], bf), "dd": ([2048], bf), "hh": ([2048], bf), "ah": ([2048], bf),
+    "kb": ([128], f4), "mm": ([128], f4), "pp": ([384], bf), "ut": ([64], bf), "oa": ([64], f4), "zq": ([64], bf), "pla": ([64], bf),
+    "lv": ([192], bf), "kk": ([3, 192], bf), "zi": ([3, 192], bf), "info": ([3328], bf), "gs": ([4096], bf),
+    "jb": ([192], f4), "jb1": ([192], f4), "jc": ([80], f4), "ids": ([1280], f4), "dlw": ([C], f4), "dum": ([P], f4),
+    "cs": ([20], f4), "ci": ([8], i4), "cand": ([80], bf), "cum": ([80], bf), "inc": ([80], f4), "dv": ([80], bf), "dv1": ([80], bf), "dv2": ([80], bf),
+    "so": ([80], f4), "sou": ([80], u2), "one": ([80], bf), "dl": ([16], f4), "dlu": ([16], u2), "mw": ([16], f4), "nw": ([16], f4),
+    "hd": ([P], bf), "wd": ([P], bf), "bta": ([P], bf), "btz": ([P], bf), "inv": ([P], bf), "dvs": ([P], f4), "dvu": ([P], u2),
+    "s1": ([P], f4), "s2": ([P], f4), "tt": ([512], f4), "tv": ([P], f4), "em": ([512], bf), "made": ([P], bf), "ii": ([P], bf), "nbc": ([P], f4),
+    "prm": ([16], u2), "prf": ([16], f4), "tr": ([32], f4), "trt": ([32], f4), "d1": ([V], bf), "d2": ([V], bf), "c127": ([64], bf),
+    "xi": ([256], f4), "gi": ([128], f4), "wt": ([16, 128], bf), "bm": ([5, 144], bf), "bmf": ([144], f4), "idf": ([128], f4),
+    "xs": ([80], f4), "pn": ([P], bf), "mt": ([19, 128], bf), "tb": ([16], f4), "pw": ([16], f4), "pw2": ([16], f4), "ones": ([2048], bf),
+}
+SCRATCH = {k: ("sbuf", [128] + s, d) for k, (s, d) in SB.items()}
+for _k in range(8):
+    SCRATCH["ps%d" % _k] = ("psum", [128, 512], "float32")
+NDMA = 48
+SEMAPHORES = ["qv", "qa", "qp", "qg", "arr0", "arr1", "out0", "out1"] + ["d%d" % k for k in range(NDMA)]
+HOP = 120.0
+TRIES = 60
+PLAIN = ((1, 0, 0), (1, 0, 0))
+
+
+def rank_program(g, core, T, topo):
+    q = T.rank_of(core)
+    if q is None:
+        return
+    N = len(T.cores)
+    ops = []
+    queue = {"v": g.vector, "a": g.scalar, "p": g.tensor, "g": g, "s": g.sync}
+
+    def R(name, *ix, part=None):
+        shape = SCRATCH[name][1][1:]
+        ix = list(ix) + [slice(None)] * (len(shape) - len(ix))
+        lo = hi = 0
+        n = 1
+        for d, i in enumerate(ix):
+            st = 1
+            for s in shape[d + 1:]:
+                st *= s
+            rg = range(shape[d])[i] if isinstance(i, slice) else range(i, i + 1)
+            lo += rg[0] * st
+            hi += rg[-1] * st
+            n *= len(rg)
+        ap = T[name][tuple([part if part is not None else slice(None)] + ix)]
+        return (ap, name, lo, hi + 1, n, 2 if SCRATCH[name][2] in (bf, u2) else 4)
+
+    def S(name, a, b, st=1, part=None):
+        return R(name, slice(a, b, st), part=part)
+
+    def IND(w, o):
+        return (w[0].indirect(o[0]), w[1], w[2], w[3], 16 * o[4], w[5], o)
+
+    def op(eng, fn, cost, rd, wr, lat=0.0, kind="c"):
+        rd = [x for x in rd if isinstance(x, tuple)]
+        rd = rd + [x[6] for x in rd + wr if len(x) > 6]
+        ops.append({"e": eng, "fn": fn, "cost": cost, "lat": lat, "kind": kind,
+                    "tr": [x[1:4] for x in rd], "tw": [x[1:4] for x in wr],
+                    "rd": [x[1:4] for x in rd],
+                    "wr": [x[1:4] for x in wr] + [("bank" + x[1], 0, 1) for x in rd + wr if x[1].startswith("ps")]})
+
+    def ap(x):
+        return x[0] if isinstance(x, tuple) else x
+
+    def vcost(o, i, two=False):
+        if len(o) > 6:
+            return 60 + 3.8 * o[4]
+        if len(i) > 6:
+            return 60 + 1.6 * o[4]
+        return 30 + max(64, o[4] * (2 if two else 0.5 if o[5] == 2 and i[5] == 2 else 1))
+
+    def ts(o, i, s1, o0, s2=None, o1=None):
+        if o1 is None:
+            op("v", lambda e: e.tensor_scalar(o[0], i[0], ap(s1), None, o0), vcost(o, i), [i, s1], [o])
+        else:
+            op("v", lambda e: e.tensor_scalar(o[0], i[0], ap(s1), ap(s2), o0, o1), vcost(o, i), [i, s1, s2], [o])
+
+    def tt(o, a, b, f):
+        two = not (a[1].startswith("ps") or b[1].startswith("ps"))
+        op("v", lambda e: e.tensor_tensor(o[0], a[0], b[0], f), vcost(o, a, two) if two else 30 + max(64, o[4]), [a, b], [o])
+
+    def cp(o, i):
+        op("v", lambda e: e.tensor_copy(o[0], i[0]), vcost(o, i), [i], [o])
+
+    def ms(o, c):
+        op("v", lambda e: e.memset(o[0], c), vcost(o, o), [], [o])
+
+    def act(o, i, f=F.Identity, bias=0.0, scale=1.0):
+        op("a", lambda e: e.activation(o[0], i[0], f, bias=ap(bias), scale=ap(scale)),
+           70 + o[4] * (1.6 if len(i) > 6 else 1.0), [i, bias, scale], [o])
+
+    def mm(items, start=True, stop=True):
+        def fn(e):
+            r = None
+            for k, (o, l, x) in enumerate(items):
+                r = e.matmul(o[0], l[0], x[0], start and k == 0, stop and k == len(items) - 1)
+            return r
+        cost = sum(max(64, x[4]) * (2.0 if x[5] == 4 else 0.5) for o, l, x in items)
+        op("p", fn, cost, [x for o, l, x in items] + [l for o, l, x in items], [o for o, l, x in items])
+
+    def iota(o, pat, base, cm, small=True):
+        if small:
+            op("g", lambda e: e.iota(o[0], pat, base, cm, allow_small_or_imprecise_dtypes=True), 150 + 2 * o[4], [], [o])
+        else:
+            op("g", lambda e: e.iota(o[0], pat, base, cm), 150 + 2 * o[4], [], [o])
+
+    def dma(o, i, eng="s", lat=2200.0, tag=None):
+        w = [(o[0], o[1], o[2] - 8, o[3] + 8)] if isinstance(o, tuple) else []
+        op(eng, lambda e: e.dma_start(ap(o), ap(i)), 80, [i], w, lat=lat, kind="d")
+        ops[-1]["tag"] = tag
+
+    def M(k):
+        return R("mt", k)
+    ID, NI, I255, I8, NIH, IA, IZ, IN0, IN1, I256, N2048, IBIG, ONES, TRI, TF = [M(k) for k in range(15)]
+    NI8, NTF, ON17 = M(16), M(17), M(18)
+
+    def W(kind, r):
+        if kind == "f":
+            return S("bmf", 15 - r, 143 - r)
+        return R("bm", kind, slice(15 - r, 143 - r))
+    P8, N8, WP, WN, WS = 0, 1, 2, 3, 4
+
+    def col(k):
+        return S("cs", k, k + 1)
+    PC, FC, GC, G15, PWC, RC, MA, MZ, WSC, TH, NPW = [col(k) for k in range(11)]
+
+    def ps(k, a=0, b=512, st=1):
+        return S("ps%d" % k, a, b, st)
+
+    dma(S("yn", 0, B // 2), T.y0[:, 0:B // 2], lat=2600.0, tag="y")
+    dma(S("yn", B // 2, B), T.y0[:, B // 2:B], eng="a", lat=3200.0, tag="y")
+    dma(S("xa", 0, V), T.x0[:, :], lat=3600.0)
+    dma(S("sni", 0, 21), T.snd[:, :], lat=3000.0)
+    for h in range(2):
+        dma(R("eni", h, slice(0, KB)), T.en0[h::2, :], eng="sa"[h], lat=3400.0, tag="e")
+
+    iota(R("xi"), [[1, 256]], 0, 0)
+    iota(S("ci", 0, 1), [[0, 1]], 0, 1, small=False)
+    iota(R("gi"), [[1, 8], [0, 16]], 0, 0)
+    ms(R("ones"), 1.0)
+    op("g", lambda e: e.affine_select(T.wt[:], T.ones[:], [[-1, 16], [-16, 8], [0, 16]], A.is_equal, 0.0, 0, 1), 4300, [R("ones")], [R("wt")])
+    cp(PC, S("ci", 0, 1))
+    ts(S("ci", 1, 2), S("ci", 0, 1), 15, A.bitwise_and)
+    ts(S("ci", 2, 3), S("ci", 0, 1), 4, A.arith_shift_right)
+    cp(S("cs", 1, 3), S("ci", 1, 3))
+    ts(G15, GC, 16.0, A.mult, 15.0, A.add)
+    x144 = S("xi", 0, 144)
+    ts(R("bm", P8), x144, G15, A.is_equal, 8.0, A.mult)
+    ts(ONES, R("gi"), GC, A.is_equal)
+    ts(ID, S("xi", 0, 128), PC, A.is_equal)
+    ts(TRI, S("xi", 0, 128), PC, A.is_gt)
+    tt(TRI, TRI, ONES, A.mult)
+    ts(R("bmf"), x144, G15, A.is_equal)
+    ts(R("tb"), S("xi", 0, 16), FC, A.is_equal)
+    ts(R("jc"), S("xi", 0, 80), 16.0, A.mult, FC, A.add)
+    ts(R("jb"), S("xi", 0, 192), 16.0, A.mult, FC, A.add)
+    ts(R("nw"), S("jc", 0, 16), float(V), A.add)
+    ts(R("jc"), R("jc"), 256.0, A.add)
+    ts(R("jb1"), R("jb"), float(Y1 - LO), A.add)
+    ts(R("jb"), R("jb"), float(Y0 - LO), A.add)
+    ms(R("one"), 1.0)
+    ms(R("c127"), -127.5)
+    for m, c in ((NI, -1.0), (I255, 255 / 512), (I8, 0.125), (NI8, -0.125), (NIH, -0.5), (IA, 2.0 * CW), (IZ, 1.0 * CW), (IN0, 1024.0), (IN1, 1280.0),
+                 (I256, 1 / 256), (N2048, -2048.0), (IBIG, 131072.0)):
+        act(m, ID, scale=c)
+    act(R("idf"), ID)
+    act(R("bm", N8), R("bm", P8), scale=-1.0)
+    ts(TF, TRI, -4096.0, A.mult)
+    act(M(15), ID, scale=65536.0)
+    tt(TF, TF, M(15), A.add)
+    act(NTF, TF, scale=-1.0)
+    act(ON17, ONES, scale=17.0)
+    ms(R("pw2"), 2.0)
+    ms(R("prf"), 0.0)
+    op("v", lambda e: e.tensor_tensor_scan(T.pw[:], T.pw2[:], T.prf[:], 0.5, A.mult, A.add), 100, [R("pw2"), R("prf")], [R("pw")])
+    tt(R("pw"), R("pw"), R("tb"), A.mult)
+    op("v", lambda e: e.tensor_reduce(PWC[0], T.pw[:], AX.X, A.add), 100, [R("pw")], [PWC])
+    ts(MA, FC, 7.5, A.is_lt, 0.25, A.mult)
+    ts(MZ, FC, 7.5, A.is_gt, 0.25, A.mult)
+    ts(col(11), MZ, 32.0, A.mult, -4.0, A.add)
+    tt(NPW, PWC, col(11), A.mult)
+    ts(R("bm", WP), x144, G15, A.is_equal, NPW, A.mult)
+    act(R("bm", WN), R("bm", WP), scale=-1.0)
+    ts(col(12), MZ, 1020.0, A.mult, 1.0, A.add)
+    ms(R("pw2"), 0.5)
+    op("v", lambda e: e.tensor_tensor_scan(T.pw[:], T.pw2[:], T.prf[:], 1.0, A.mult, A.add), 100, [R("pw2"), R("prf")], [R("pw")])
+    tt(R("pw"), R("pw"), R("tb"), A.mult)
+    op("v", lambda e: e.tensor_reduce(RC[0], T.pw[:], AX.X, A.add), 100, [R("pw")], [RC])
+    tt(RC, RC, col(12), A.mult)
+    ts(R("s1"), R("xi"), RC, A.mult, -0.5 + 2.0 ** -10, A.add)
+    ts(R("s2"), R("s1"), MAG, A.add, -MAG, A.add)
+    tt(R("s1"), R("s1"), R("s2"), A.subtract)
+    ts(R("bta"), R("s1"), 0.0, A.is_gt, MA, A.mult)
+    ts(R("btz"), R("s1"), 0.0, A.is_gt, MZ, A.mult)
+    ts(col(13), S("tb", 1, 2), 2048.0, A.mult, S("tb", 0, 1), A.add)
+    ts(WSC, S("tb", 2, 3), 2.0 ** 22, A.mult, col(13), A.add)
+    ts(R("bm", WS), x144, G15, A.is_equal, WSC, A.mult)
+    act(R("ii"), R("xi"), bias=-128.0)
+    act(R("dum"), R("xi"), bias=1280.0)
+    ts(col(14), FC, 16.0, A.mult)
+    ts(R("prm"), S("xi", 0, 16), col(14), A.add)
+    z = lambda a, b: S("ones", 0, b - a)
+    ms(S("win", 0, 16), 0.0)
+    for name, a, b in (("win", LO + V, LO + C), ("lw", V, CW), ("lw", CW + V, CW + C), ("hif", V, C), ("bl", V, C)):
+        act(S(name, a, b), z(a, b), scale=0.0)
+    ms(R("e0"), 0.0)
+    ms(R("e1"), 0.0)
+
+    for h in range(2):
+        cp(S("e0", 192 * h, 192 * h + KB), R("eni", h, slice(0, KB)))
+        cp(S("eu", 192 * h, 192 * h + KB), R("eni", h, slice(0, KB)))
+    mm([(ps(7, 0, KB), W(P8, r), S("yn", KB * r, KB * r + KB)) for r in range(7)], stop=False)
+    mm([(ps(7, 0, KB), W(P8, r), S("yn", KB * r, KB * r + KB)) for r in range(7, 16)], start=False)
+    ts(S("lv", 0, KB), ps(7, 0, KB), 1407.5, A.is_gt)
+    dma(R("bli"), T.bl0[:, :], lat=3000.0)
+    ops[-1]["rd"].append(S("lv", 0, KB)[1:4])
+    for r in range(16):
+        o, i = S("win", Y0 + r, Y0 + B, 16), S("yn", KB * r, KB * r + KB)
+        (cp if r % 2 else act)(o, i)
+        ops[-1]["tag"] = "weave"
+    ts(S("bl", 0, V), R("bli"), 1.0, A.add)
+    sn = lambda k: S("snf", 24 * k, 24 * k + 21)
+    ts(sn(0), S("sni", 0, 21), 1.0 / KB, A.mult, -0.5 + 0.5 / KB, A.add)
+    ts(sn(1), sn(0), MAG, A.add, -MAG, A.add)
+    cp(S("snu", 24, 45), sn(1))
+    ts(sn(2), sn(1), -float(KB), A.mult)
+    tt(sn(2), sn(2), S("sni", 0, 21), A.add)
+    nlow = 3 * (N - 1 - q)
+    if nlow > 0:
+        cp(S("snu", 0, nlow), S("snf", 48, 48 + nlow))
+    if nlow < 21:
+        ts(S("snu", nlow, 21), S("snf", 48 + nlow, 69), 192.0, A.add)
+    cp(R("mk"), IND(R("tb"), S("snu", 24, 45)))
+    act(R("d1"), S("yn", 0, V), bias=-3.5)
+    ts(R("d2"), R("d1"), MAG * 8, A.add, -MAG * 8, A.add)
+
+    def reduce(o, i):
+        op("v", lambda e: e.tensor_reduce(o[0], i[0], AX.X, A.add), 30 + max(64, i[4]), [i], [o])
+
+    def own_cells(t):
+        tt(R("gm"), IND(R("e%d" % t), S("snu", 0, 21)), R("mk"), A.mult)
+        pb = 2 if t == 0 else 5
+        mm([(ps(pb, 0, 21), W("f", r), S("gm", r, GH, 16)) for r in range(16)])
+        for k in range(3):
+            cp(S("ow", k, 42, 6), ps(pb, k, 21, 3))
+            ts(S("ow", 3 + k, 42, 6), ps(pb, k, 21, 3), float(CW), A.add)
+
+    def banks_of(t):
+        rb = 8 if t == 0 else 6
+        return [(r0, min(16, r0 + rb)) for r0 in range(0, 16, rb)]
+
+    def cell_sums(t):
+        X, K, Ct, dl = "xa" if t == 0 else "xb", 64 + 16 * t, V + P * t, float(DELTA[t])
+        ts(S("hif", 0, Ct), S(X, 0, Ct), dl, A.add, 63.0, A.min)
+        ts(S("lof", 0, Ct), S(X, 0, Ct), -dl, A.add, 0.0, A.max)
+        mm([(ps(6, 64, 64 + K), W(P8, r), S(X, K * r, K * r + K)) for r in range(16)])
+        act(S("xs", 0, K), ps(6, 64, 64 + K))
+
+    def cell_preload(t):
+        X, K = "xa" if t == 0 else "xb", 64 + 16 * t
+        for k, (r0, r1) in enumerate(banks_of(t)):
+            w = (r1 - r0) * K
+            mm([(ps(k, 0, w), NIH, S(X, K * r0, K * r1))], stop=False)
+            mm([(ps(3 + k, 0, w), I8, S("hif", K * r0, K * r1)), (ps(3 + k, 0, w), NI8, S("lof", K * r0, K * r1))], stop=False)
+
+    def old_live():
+        mm([(ps(7, 0, KB), ONES, S("lv", 0, KB))])
+        reduce(col(15), ps(7, 0, KB))
+
+    own_cells(0)
+    cell_sums(0)
+    cell_preload(0)
+    old_live()
+    late = []
+    for t in range(2):
+        Ct, K, NC = V + P * t, 64 + 16 * t, KB + 16 * t
+        n0, dl = V + P * t, float(DELTA[t])
+        E, En = "e%d" % t, "e%d" % (t + 1)
+        YB = Y0 if t == 0 else Y1
+        if t == 0:
+            cp(S("ci", 4, 5), col(15))
+        else:
+            ts(S("ci", 4, 5), col(16), 0.5, A.mult, col(15), A.add)
+        ts(S("ci", 5, 6), S("ci", 4, 5), 31, A.bitwise_and)
+        ts(TH, S("ci", 5, 6), 8.0, A.mult, 8.0 * THETA[t] - 0.5, A.add)
+        ts(S("cand", 0, K), S("xs", 0, K), TH, A.is_gt)
+        op("v", lambda e, K=K: e.tensor_tensor_scan(T.cum[:, 0:K], T.one[:, 0:K], T.cand[:, 0:K], 0.0, A.mult, A.add), 100,
+           [R("one"), R("cand")], [R("cum")])
+        ts(S("dv2", 0, K), S("xs", 0, K), TH, A.is_gt, dl / 2, A.mult)
+        off = ps(7, 300, 301)
+        mm([(off, TRI, S("cum", K - 1, K))])
+        ts(S("dv1", 0, K), S("cum", 0, K), off, A.add, 256.5, A.is_lt)
+        tt(S("dv", 0, K), S("dv1", 0, K), S("dv2", 0, K), A.mult)
+        for k, (r0, r1) in enumerate(banks_of(t)):
+            w = (r1 - r0) * K
+            for kk_ in (k, 3 + k):
+                mm([(ps(kk_, K * (r - r0), K * (r - r0 + 1)), R("wt", r), S("dv", 0, K)) for r in range(r0, r1)], start=False)
+            ts(S("lw", K * r0, K * r1), ps(k, 0, w), -1.0, A.mult, 0.0, A.max)
+            act(S("lw", CW + K * r0, CW + K * r1), ps(3 + k, 0, w), F.Relu, bias=-2.0 * dl, scale=4.0)
+        sb, land = "sb%d" % t, "land%d" % t
+        cp(S(sb, 0, 320), IND(S("lw", 0, CW + C), S("ow", 0, 20)))
+        act(S(sb, 320, 672), IND(S("lw", 0, CW + C), S("ow", 20, 42)))
+
+        def send(e, t=t, sb=sb, land=land):
+            trs = []
+            for d in range(1, N):
+                dst = T.cores[(q + d) % N]
+                rid, pid, _ = topo.addr(dst)
+                en = topo.engines(core, dst)
+                mask = (1 << en[2 * (d - 1)]) | (1 << en[2 * (d - 1) + 1])
+                trs.append(RemoteDMATransfer(dst_ids=[DstId(rid=rid, pnc=pid)], dma_engine_mask=mask, remote_sem=T.sem["arr%d" % t],
+                                             src=T[sb][:, 96 * (d - 1):96 * d], dst=T[land][:, N - 1 - d, :]))
+            e.remote_dma_fused(trs, local_sem=T.sem["out%d" % t])
+        op("g", send, 300, [R(sb)], [R(land)], lat=3000.0, kind="r%d" % t)
+        ts(S("inc", 0, K), S("cum", 0, K), off, A.add, -1.0, A.add)
+        if t == 1:
+            late[0]()
+        cp(S("lw", C, CW), R(land, slice(None), slice(0, 48)))
+        act(S("lw", CW + C, 2 * CW), R(land, slice(None), slice(48, 96)))
+        act(S("win", LO, LO + Ct), S("lw", 0, Ct), scale=2.0)
+        ts(S("win", LO + C, LO + CW), S("lw", C, CW), 2.0, A.mult)
+        mm([(ps(5, 0, GH), ID, S("lw", C, CW)), (ps(5, 0, GH), ID, S("lw", CW + C, 2 * CW))])
+        act(S("win", HA + C, HA + CW), ps(5, 0, GH), scale=2.0)
+        ts(S("win", HZ + C, HZ + CW), S("win", HA + C, HA + CW), 1.0, A.mult)
+        iota(S("ids", 0, Ct), [[1, K], [K, 16]], 0, 0)
+        if t == 0:
+            for nm, a, b, v in (("win", HA, HA + C, 0), ("win", HZ, HZ + C, 0), ("info", 0, 3328, 1)):
+                iota(S(nm, a, b), [[0, b - a]], v, 0)
+                ops[-1]["rd"].append(R(land)[1:4])
+        ts(S("so", 0, K), S("dv", 0, K), 1.0, A.is_lt, 4096.0, A.mult)
+        tt(S("so", 0, K), S("so", 0, K), S("inc", 0, K), A.add)
+        tt(S("so", 0, K), S("so", 0, K), S("jc", 0, K), A.min)
+        cp(S("sou", 0, K), S("so", 0, K))
+        act(S("dlw", 0, P), R("dum"))
+        for a in range(0, K, 16):
+            cp(IND(R("dlw"), S("sou", a, a + 16)), S("ids", 16 * a, 16 * a + 256))
+            ops[-1]["rd"].append(R(sb)[1:4])
+        DL = S("dlw", 0, P)
+        mm([(ps(7, 0, 16), W("f", r), S("dlw", r, P, 16)) for r in range(16)])
+        ts(R("dl"), ps(7, 0, 16), 1 / 16, A.mult)
+        cp(R("dlu"), R("dl"))
+        act(R("hd"), IND(R("hif"), R("dlu")))
+        act(R("wd"), IND(S("lw", CW, CW + C), R("dlu")), scale=2.0)
+        act(R("dvs"), IND(R("bl"), R("dlu")))
+        cp(R("dvu"), R("dvs"))
+        tt(IND(S("win", HA, HA + C), R("dlu")), R("hd"), R("bta"), A.add)
+        tt(IND(S("win", HZ, HZ + C), R("dlu")), R("hd"), R("btz"), A.add)
+        ts(R("inv"), DL, 1279.5, A.is_gt, -1024.0, A.mult)
+        act(R("nbc"), R("xi"), bias=float(B + P * t + 1 - 4096 * 48))
+        for k in range(3):
+            ts(R("kk", k, slice(0, NC)), S("lv", 0, NC), k + 1 - 8192.0, A.mult, 8192.0, A.add)
+        if t == 1:
+            dma(T.yx[:, 0:Ct], S("win", LO, LO + Ct))
+            dma(T.yx[:, Ct:C], R("hd"))
+            act(S("ylo", 0, Ct), S("bl", 0, Ct), bias=-1.0)
+
+        chunks = [(0, 64), (64, 128), (128, NC)] if t == 0 else [(0, 64), (128, NC), (64, 128)]
+        loh, wh = S("lw", 0, CW), S("lw", CW, 2 * CW)
+        awin, zwin = S("win", LO, Y1 if t == 0 else WEND), S("win", 0, HA)
+
+        def units(c0, c1):
+            return [(a, min(c1, a + 32)) for a in range(c0, c1, 32)]
+
+        def phase1(k):
+            c0, c1 = chunks[k]
+            n, o = c1 - c0, 1024 * (k % 2) - 16 * c0
+            U = lambda nm, a, b: S(nm, o + 16 * a, o + 16 * b)
+            for a, b in units(c0, c1):
+                tt(U("tu", a, b), IND(loh, S("eu", a, b)), S("win", YB + 16 * a, YB + 16 * b), A.subtract)
+                act(U("wa", a, b), IND(wh, S("eu", a, b)))
+            for a, b in units(c0, c1):
+                tt(U("t00", a, b), IND(loh, S("eu", 192 + a, 192 + b)), U("tu", a, b), A.add)
+            plain = PLAIN[t][k]
+            for a, b in units(c0, c1):
+                if plain:
+                    act(U("t01", a, b), IND(wh, S("eu", 192 + a, 192 + b)))
+                else:
+                    tt(U("t01", a, b), IND(wh, S("eu", 192 + a, 192 + b)), U("t00", a, b), A.add)
+            for a, b in units(c0, c1):
+                w = 16 * (b - a)
+                p0, p1 = ps((2 * (a // 32)) % 3, 0, w), ps((2 * (a // 32) + 1) % 3, 0, w)
+                act(U("a00", a, b), U("t00", a, b), F.Abs)
+                mm([(p0, ID, U("t00", a, b)), (p0, ID, U("wa", a, b))])
+                act(U("a10", a, b), p0, F.Abs)
+                if plain:
+                    mm([(p1, ID, U("t00", a, b)), (p1, ID, U("t01", a, b))])
+                    act(U("a01", a, b), p1, F.Abs)
+                    mm([(p0, ID, U("t00", a, b)), (p0, ID, U("wa", a, b)), (p0, ID, U("t01", a, b))])
+                    p1 = p0
+                else:
+                    act(U("a01", a, b), U("t01", a, b), F.Abs)
+                    mm([(p1, ID, U("t01", a, b)), (p1, ID, U("wa", a, b))])
+                act(U("a11", a, b), p1, F.Abs)
+            Z = lambda nm, r: S(nm, o + 16 * c0 + r, o + 16 * c1, 16)
+            kk = lambda x: R("kk", x, slice(c0, c1))
+            reg = lambda x: ps(5, 64 * x, 64 * x + n)
+            lin = ((P8, "wa"), (P8, "t01")) if plain else ((P8, "wa"), (N8, "t00"), (P8, "t01"))
+            mm([(reg(4), NI, kk(0))] + [(reg(4), W(w_, r), Z(nm, r)) for w_, nm in lin for r in range(16)])
+            mm([(reg(0), W(P8, r), Z("a00", r)) for r in range(16)])
+            mm([(reg(3), ID, kk(1))] + [(reg(3), W(P8, r), Z("a10", r)) for r in range(16)])
+            mm([(reg(2), ID, kk(0))] + [(reg(2), W(P8, r), Z("a01", r)) for r in range(16)])
+            mm([(reg(1), ID, kk(2))] + [(reg(1), W(P8, r), Z("a11", r)) for r in range(16)])
+
+        def decide(k):
+            c0, c1 = chunks[k]
+            n = c1 - c0
+            reg = lambda x: ps(5, 64 * x, 64 * x + n)
+            k01, k10 = S("kb", 0, n), S("kb", 64, 64 + n)
+            act(k01, reg(2))
+            act(k10, reg(3))
+            ts(S("ut", 0, n), reg(4), 0.5, A.is_lt, 16384.0, A.mult)
+            tt(S("mm", 0, n), reg(1), k10, A.min)
+            tt(S("mm", 64, 64 + n), reg(1), k01, A.min)
+            tt(reg(5), reg(0), k01, A.min)
+            tt(reg(6), reg(0), k10, A.min)
+            pa, pz = S("pp", c0, c1), S("pp", 192 + c0, 192 + c1)
+            tt(pa, reg(5), S("mm", 0, n), A.is_gt)
+            tt(pz, reg(6), S("mm", 64, 64 + n), A.is_gt)
+            oa, oz = ps(6, 0, n), ps(6, 64, 64 + n)
+            mm([(oa, R("idf"), S(E, c0, c1)), (oa, ID, S("ut", 0, n)), (oa, IA, pa)])
+            mm([(oz, R("idf"), S(E, 192 + c0, 192 + c1)), (oz, NI, S("ut", 0, n)), (oz, IZ, pz)])
+            tt(S("oa", 0, n), oa, S("jb" if t == 0 else "jb1", c0, c1), A.min)
+            ts(S("ofs", 192 + c0, 192 + c1), oz, 16.0, A.add)
+            cp(S("ofs", c0, c1), S("oa", 0, n))
+
+        def phase2(k):
+            c0, c1 = chunks[k]
+            o = 1024 * (k % 2) - 16 * c0
+            U = lambda nm, a, b: S(nm, o + 16 * a, o + 16 * b)
+            for a, b in units(c0, c1):
+                act(U("ga", a, b), IND(awin, S("ofs", a, b)))
+                tt(U("dd", a, b), IND(zwin, S("ofs", 192 + a, 192 + b)), U("ga", a, b), A.subtract)
+            for a, b in units(c0, c1):
+                ts(U("hh", a, b), U("dd", a, b), MAG, A.add, -MAG, A.add)
+                act(U("ah", a, b), U("hh", a, b), F.Abs)
+            n = c1 - c0
+            Z = lambda nm, r, cb=c1: S(nm, o + 16 * c0 + r, o + 16 * cb, 16)
+            pl, ys = ps(7, 128, 128 + n), ps(6, 192, 192 + n)
+            mm([(pl, W(w_, r), Z(nm, r)) for w_, nm in ((WP, "dd"), (WN, "hh")) for r in range(16)] + [(pl, ID, S("c127", 0, n))])
+            if t == 0:
+                for a, b in units(c0, c1):
+                    pb, w = 3 + (a // 32) % 2, 16 * (b - a)
+                    mm([(ps(pb, 0, w), I255, S("win", Y0 + 16 * a, Y0 + 16 * b)), (ps(pb, 0, w), I255, U("ah", a, b))])
+                    ts(S("win", Y1 + 16 * a, Y1 + 16 * b), ps(pb, 0, w), MAG, A.add, -MAG, A.add)
+                mm([(ys, W(P8, r), S("win", Y1 + 16 * c0 + r, Y1 + 16 * c1, 16)) for r in range(16)])
+            else:
+                cb = min(c1, KB)
+                m = cb - c0
+                for hf in range(2):
+                    for r in range(8 * hf, 8 * hf + 8):
+                        oo = ps(3 + hf, m * (r % 8), m * (r % 8 + 1))
+                        mm([(oo, I255, S("win", Y1 + 16 * c0 + r, Y1 + 16 * cb, 16)), (oo, I255, Z("ah", r, cb))])
+                    ts(R("yo", slice(8 * hf, 8 * hf + 8), slice(c0, cb)), ps(3 + hf, 0, 8 * m), MAG, A.add, -MAG, A.add)
+                if cb < c1:
+                    mm([(ps(2, 0, P), I255, S("win", Y1 + B, Y1 + B + P)), (ps(2, 0, P), I255, U("ah", cb, c1))])
+                    ts(S("yon", 0, P), ps(2, 0, P), MAG, A.add, -MAG, A.add)
+                mm([(ps(6, 192, 192 + m), W(P8, r), R("yo", r, slice(c0, cb))) for r in range(16)])
+                if cb < c1:
+                    mm([(ps(6, 192 + m, 192 + n), W(P8, r), S("yon", r, P, 16)) for r in range(16)])
+
+        def post(k):
+            c0, c1 = chunks[k]
+            n = c1 - c0
+            pl, ys = ps(7, 128, 128 + n), ps(6, 192, 192 + n)
+            zq, pla = S("zq", 0, n), S("pla", 0, n)
+            ts(zq, pl, MAG * 256, A.add, -MAG * 256, A.add)
+            tt(pla, pl, zq, A.subtract)
+            ts(R("zi", 2, slice(c0, c1)), ys, 1407.5, A.is_lt)
+            if t == 0:
+                ts(S("lv", c0, c1), ys, 1407.5, A.is_gt)
+            ra, rz = ps(7, 256, 256 + n), ps(7, 320, 320 + n)
+            IN = IN0 if t == 0 else IN1
+            mm([(ra, NI, S("c127", 0, n)), (ra, IN, S("pp", c0, c1)), (ra, ID, pla)])
+            mm([(rz, IN, S("pp", 192 + c0, 192 + c1)), (rz, I256, zq)])
+            for h, rr in ((0, ra), (1, rz)):
+                ne = S(En, 192 * h + c0, 192 * h + c1)
+                tt(ne, rr, S(E, 192 * h + c0, 192 * h + c1), A.max)
+                ts(R("zi", h, slice(c0, c1)), ne, -(n0 + 128.0), A.add, -256.0, A.max)
+                if t == 0:
+                    cp(S("eu", 192 * h + c0, 192 * h + c1), ne)
+
+        phase1(0)
+        decide(0)
+        phase1(1)
+        decide(1)
+        phase1(2)
+        decide(2)
+        phase2(0)
+        post(0)
+        phase2(1)
+        post(1)
+        if t == 1:
+            for x in range(3):
+                dma(S("info", 3072, 3328, part=slice(x, 128, 16)), R("zi", x, slice(KB, NC)), eng="s", tag="n")
+            cp(S("info", 1 + B, 1 + B + P), IND(S("info", 3072, 3328), R("prm")))
+            for h in range(2):
+                cp(S("tr", 16 * h, 16 * h + 16), S("e2", 192 * h + KB, 192 * h + NC))
+            op("v", lambda e: e.transpose(T.trt[:], T.tr[:]), 100, [R("tr")], [R("trt")])
+            for a in range(4):
+                for gp in range(2):
+                    dma(T.ye[4 * a + 2 * gp:4 * a + 2 * gp + 2, B:B + P], S("trt", 16 * gp, 16 * gp + 16, part=slice(32 * a, 32 * a + 32)))
+        if t == 0:
+            for k, (a, b) in enumerate(((0, 512), (512, V))):
+                mm([(ps(k), ID, S("win", LO + a, LO + b)), (ps(k), ID, S("yn", a, b)), (ps(k), NI, S("d2", a, b))])
+                act(S("xb", a, b), ps(k), F.Relu, bias=-3.0)
+            mm([(ps(2, 0, P), ID, R("hd")), (ps(2, 0, P), ID, S("yn", 0, P)), (ps(2, 0, P), NI, S("d2", 0, P)), (ps(2, 0, P), ID, R("inv"))])
+            act(S("xb", V, V + P), ps(2, 0, P), F.Relu, bias=-3.0)
+            ts(R("xb"), R("xb"), 63.0, A.min)
+            cell_sums(1)
+            mm([(ps(5, 0, P), ONES, R("wd"))])
+            ts(R("pn"), ps(5, 0, P), 175.5, A.is_lt, -1024.0, A.mult)
+        phase2(2)
+        post(2)
+        if t == 0:
+            own_cells(1)
+            cell_preload(1)
+            old_live()
+
+        for x in range(3):
+            dma(S("info", 1, 1 + B, part=slice(x, 128, 16)), R("zi", x, slice(0, KB)), eng="sas"[x], tag="i%d" % t)
+        if t == 1:
+            dma(T.yy[:, 0:B], R("yo"))
+            ops[-1]["rd"].append(S("info", 16, 32)[1:4])
+            for h in range(2):
+                dma(T.ye[h::2, 0:B], S("e2", 192 * h, 192 * h + KB))
+                ops[-1]["rd"].append(S("info", 16, 32)[1:4])
+        iw = S("info", 0, 3040)
+        for k in range(4):
+            for u in (2 * k, 2 * k + 1):
+                (cp if u in (1, 3, 5) else act)(S("gs", 512 * u, 512 * u + 512), IND(iw, S("dvu", 32 * u, 32 * u + 32)))
+            pk = 6 + k % 2
+            oo = ps(pk, 0, 64)
+            i_ = S("ii", 64 * k, 64 * k + 64)
+            mm([(oo, NI, i_), (oo, N2048, i_)] + [(oo, W(WS, s), S("gs", 1024 * k + s, 1024 * k + 1024, 16)) for s in range(16)])
+            sl = lambda nm, b0=0: S(nm, b0 + 64 * k, b0 + 64 * k + 64)
+            ts(sl("s1"), oo, MAG * 2048, A.add, -MAG * 2048, A.add)
+            ts(sl("em", P), oo, 3.0 * 2 ** 20, A.is_gt)
+            tt(ps(pk, 128, 192), oo, sl("s1"), A.is_equal)
+            ts(sl("s2"), sl("s1"), 0.0, A.is_equal)
+            tt(ps(pk, 192, 256), ps(pk, 128, 192), sl("s2"), A.max)
+            tt(sl("em"), ps(pk, 192, 256), sl("em", P), A.is_gt)
+        mv, dead = S("em", 0, P), S("em", P, 2 * P)
+        if t == 0:
+            g2 = ps(6, 0, P)
+            mm([(g2, ID, R("pn")), (g2, ONES, dead), (g2, ON17, mv)])
+            act(R("s2"), g2, F.Abs, bias=-136.0)
+            op("a", lambda e: e.activation(T.tv[:], T.s2[:], F.Sign, bias=135.5, scale=-1.0, accum_out=col(16)[0]), 350, [R("s2")], [R("tv"), col(16)])
+
+        def slot_tail(t=t, n0=n0, mv=mv, dead=dead):
+            b0, b1, b2, b3 = (6, 7, 6, 7) if t == 0 else (0, 1, 2, 3)
+            gg = ps(b0, 0, P)
+            mm([(gg, ID, R("inv")), (gg, ONES, dead), (gg, ON17, mv)])
+            act(R("s1"), gg, F.Abs, bias=-136.0)
+            ts(R("made"), R("s1"), 135.5, A.is_lt)
+            sv, sn_ = ps(b1, 0, P), ps(b1, P, 2 * P)
+            mm([(sv, ID, S("ones", 0, P)), (sv, NI, mv), (sv, NI, dead)])
+            mm([(sn_, ID, mv)])
+            tt(S("tt", 0, P), sv, R("dvs"), A.mult)
+            tt(S("tt", P, 2 * P), sn_, R("dvs"), A.mult)
+            fv, fn = ps(b2, P, 2 * P), ps(b3, 0, P)
+            mm([(fv, R("idf"), R("nbc")), (fv, TF, mv), (fv, TF, dead)], stop=False)
+            mm([(fv, IBIG, R("made"))], start=False)
+            mm([(fn, R("idf"), R("nbc")), (fn, TF, S("ones", 0, P)), (fn, NTF, mv)], stop=False)
+            mm([(fn, IBIG, R("made"))], start=False)
+            tt(R("s2"), fv, S("tt", 0, P), A.max)
+            ynew = S("win", Y1 + B, Y1 + B + P) if t == 0 else S("yon", P, 2 * P)
+            if t == 0:
+                tt(ynew, R("made"), R("wd"), A.mult)
+                tt(S("bl", n0, n0 + P), fn, S("tt", P, 2 * P), A.max)
+                cp(IND(R("bl"), R("dlu")), R("s2"))
+                mm([(ps(7, 0, 16), W(P8, r), S("win", Y1 + B + r, Y1 + B + P, 16)) for r in range(16)])
+                ts(S("lv", KB, KB + 16), ps(7, 0, 16), 1407.5, A.is_gt)
+                mm([(ps(6, 0, 16), W(P8, r), S("made", r, P, 16)) for r in range(16)])
+                ts(R("mw"), ps(6, 0, 16), 1 / 128, A.mult)
+                for h, src in ((0, "dl"), (1, "nw")):
+                    tt(S("e1", 192 * h + KB, 192 * h + KB + 16), R("mw"), R(src), A.mult)
+                    cp(S("eu", 192 * h + KB, 192 * h + KB + 16), S("e1", 192 * h + KB, 192 * h + KB + 16))
+            else:
+                ts(IND(S("ylo", 0, C), R("dlu")), R("s2"), 1.0, A.mult, -1.0, A.add)
+                dma(T.yl[:, 0:n0], S("ylo", 0, n0), lat=3000.0)
+                tt(R("s1"), fn, S("tt", P, 2 * P), A.max)
+                act(R("tv"), R("s1"), bias=-1.0)
+                dma(T.yl[:, n0:C], R("tv"), eng="a")
+                tt(ynew, R("made"), R("wd"), A.mult)
+                dma(T.yy[:, B:B + 2 * P], R("yon"), eng="a")
+                tt(S("tt", 0, P), R("made"), S("dlw", 0, P), A.mult)
+                act(R("dvs"), R("xi"), bias=float(n0))
+                tt(S("tt", P, 2 * P), R("made"), R("dvs"), A.mult)
+                for h in range(2):
+                    dma(T.ye[h::2, B + P:B + 2 * P], S("tt", P * h, P * h + P, part=slice(0, 128, 16)), eng="a")
+        late.append(slot_tail)
+    late[1]()
+
+    emit(ops, queue, T)
+
+
+def emit(ops, queue, T):
+    n = len(ops)
+    hist = {}
+    deps = [set() for _ in range(n)]
+    for k, o in enumerate(ops):
+        for acc, wr in ((o["rd"], False), (o["wr"], True)):
+            for name, lo, hi in acc:
+                for j, l2, h2, w2 in hist.get(name, []):
+                    if j != k and (wr or w2) and l2 < hi and lo < h2 and not (o.get("tag") and o.get("tag") == ops[j].get("tag")):
+                        deps[k].add(j)
+        for name, lo, hi in o["wr"]:
+            hist[name] = [x for x in hist.get(name, []) if o.get("tag") or not (lo <= x[1] and x[2] <= hi)] + [(k, lo, hi, True)]
+        for name, lo, hi in o["rd"]:
+            hist.setdefault(name, []).append((k, lo, hi, False))
+
+    def meet(u, v):
+        return any(x[0] == y[0] and x[1] < y[2] and y[1] < x[2] for x in u for y in v)
+
+    def free_edge(j, k):
+        a, b = ops[j], ops[k]
+        if a["e"] != b["e"] or a["kind"] != "c" or b["kind"] != "c":
+            return False
+        return a["e"] == "p" or not (meet(a["tw"], b["tr"] + b["tw"]) or meet(a["tr"], b["tw"]))
+    succ = [[] for _ in range(n)]
+    for k in range(n):
+        for j in deps[k]:
+            succ[j].append(k)
+    tail = [0.0] * n
+    for k in range(n - 1, -1, -1):
+        tail[k] = ops[k]["cost"] + ops[k]["lat"] + max([HOP + tail[j] for j in succ[k]] + [0.0])
+    gap = [[ops[k]["lat"] + (0.0 if free_edge(k, j) else HOP) for j in succ[k]] for k in range(n)]
+
+    def plan(pri, look):
+        left = [len(d) for d in deps]
+        ready = {e: [] for e in queue}
+        at = [0.0] * n
+        for k in range(n):
+            if left[k] == 0:
+                ready[ops[k]["e"]].append(k)
+        free = {e: 0.0 for e in queue}
+        order, start, end = [], [0.0] * n, 0.0
+        while len(order) < n:
+            best = None
+            for e in queue:
+                if ready[e]:
+                    now = max(free[e], min(at[k] for k in ready[e]))
+                    k = max((k for k in ready[e] if at[k] <= now + 40), key=lambda k: pri[k])
+                    soon = [j for j in ready[e] if now + 40 < at[j] < now + look * ops[k]["cost"] and pri[j] > pri[k] + ops[k]["cost"]]
+                    if soon:
+                        j = max(soon, key=lambda j: pri[j])
+                        fit = [x for x in ready[e] if max(at[x], now) + ops[x]["cost"] <= at[j] + 60]
+                        k = max(fit, key=lambda x: pri[x]) if fit else j
+                    st = max(free[e], at[k])
+                    if best is None or st < best[0]:
+                        best = (st, k)
+            st, k = best
+            e = ops[k]["e"]
+            ready[e].remove(k)
+            order.append(k)
+            start[k] = st
+            free[e] = st + ops[k]["cost"]
+            end = max(end, free[e] + ops[k]["lat"])
+            for j, gp in zip(succ[k], gap[k]):
+                at[j] = max(at[j], free[e] + gp)
+                left[j] -= 1
+                if left[j] == 0:
+                    ready[ops[j]["e"]].append(j)
+        return end, order, start
+
+    rng = np.random.RandomState(7)
+    base = np.array([tail[k] + (1e6 if ops[k]["kind"] != "c" else 0.0) - 1e-3 * k for k in range(n)])
+    best = None
+    for trial in range(TRIES):
+        amp = (0.0, 100.0, 400.0, 1200.0)[(trial // 5) % 4]
+        cand = plan(list(base + amp * rng.rand(n)), (0.0, 0.3, 0.5, 0.7, 0.9)[trial % 5])
+        if best is None or cand[0] < best[0]:
+            best = cand
+    end, order, start = best
+    for k in range(n):
+        ops[k]["st"] = start[k]
+    pos = {k: i for i, k in enumerate(order)}
+    need = [False] * n
+    waits = [[] for _ in range(n)]
+    seen = {e: {} for e in queue}
+    for k in order:
+        e = ops[k]["e"]
+        last = {}
+        for j in deps[k]:
+            key = ops[j]["e"] if ops[j]["kind"] == "c" else j
+            if free_edge(j, k):
+                continue
+            if key not in last or pos[j] > pos[last[key]]:
+                last[key] = j
+        for key, j in last.items():
+            if seen[e].get(key, -1) < pos[j]:
+                seen[e][key] = pos[j]
+                need[j] = True
+                waits[k].append(j)
+    sig = {}
+    cnt = {e: 0 for e in queue}
+    nd = 0
+    ends = []
+    for k in order:
+        o = ops[k]
+        e = queue[o["e"]]
+        for j in waits[k]:
+            e.wait_ge(*sig[j])
+        r = o["fn"](e)
+        if o["kind"] == "d":
+            s = T.sem["d%d" % nd]
+            nd += 1
+            r.then_inc(s, 16)
+            sig[k] = (s, 16)
+            if not need[k]:
+                ends.append(sig[k])
+        elif o["kind"] == "c":
+            if need[k]:
+                cnt[o["e"]] += 1
+                s = T.sem["q" + o["e"]]
+                r.then_inc(s, 1)
+                sig[k] = (s, cnt[o["e"]])
+        else:
+            sig[k] = (T.sem["arr" + o["kind"][1]], 14)
+            ends.append((T.sem["out" + o["kind"][1]], 14))
+    for s in ends:
+        queue["s"].wait_ge(*s)
+    return end

@@ -14,30 +14,40 @@ SB = {
     "win": ([WEND], bf), "lw": ([2 * CW], bf), "hif": ([C], bf), "lof": ([1280], bf), "yn": ([B], bf), "xa": ([1280], bf), "xb": ([1280], bf),
     "yo": ([16, KB], bf), "yon": ([512], bf), "bli": ([V], i4), "bl": ([C], f4), "ylo": ([C], f4),
     "eni": ([2, 176], i4), "e0": ([384], f4), "e1": ([384], f4), "e2": ([384], f4), "eu": ([384], u2), "ofs": ([384], u2),
-    "sni": ([24], i4), "snf": ([96], f4), "snu": ([48], u2), "mk": ([GH], f4), "gm": ([GH], f4), "ow": ([42], u2),
-    "sb0": ([672], bf), "sb1": ([672], bf), "land0": ([7, 96], bf), "land1": ([7, 96], bf), "fh": ([GH], bf),
+    "sni": ([24], i4), "snf": ([96], f4), "snu": ([48], u2), "mk": ([GH], f4), "gm": ([GH], f4), "ow": ([72], u2),
+    "sb0": ([GH], bf), "sb1": ([GH], bf), "land0": ([GH], bf), "land1": ([GH], bf), "fhi": ([GH], bf), "flo": ([GH], bf),
+    "sx0": ([GH], bf), "sx1": ([GH], bf), "lx0": ([GH], bf), "lx1": ([GH], bf), "mk2": ([GH], bf),
     "tu": ([2048], bf), "t00": ([2048], bf), "t01": ([2048], bf), "wa": ([2048], bf),
     "a00": ([2048], bf), "a01": ([2048], bf), "a10": ([2048], bf), "a11": ([2048], bf),
     "ga": ([2048], bf), "dd": ([2048], bf), "hh": ([2048], bf), "ah": ([2048], bf),
     "kb": ([128], f4), "mm": ([128], f4), "pp": ([384], bf), "ut": ([64], bf), "oa": ([64], f4), "zq": ([64], bf), "pla": ([64], bf),
     "lv": ([192], bf), "kk": ([3, 192], bf), "zi": ([3, 192], bf), "info": ([3328], bf), "gs": ([4096], bf),
-    "jb": ([192], f4), "jb1": ([192], f4), "jc": ([80], f4), "ids": ([1280], f4), "dlw": ([C], f4), "dum": ([P], f4),
-    "cs": ([20], f4), "ci": ([8], i4), "cand": ([80], bf), "cum": ([80], bf), "inc": ([80], f4), "dv": ([80], bf), "dv1": ([80], bf), "dv2": ([80], bf),
-    "so": ([80], f4), "sou": ([80], u2), "one": ([80], bf), "dl": ([16], f4), "dlu": ([16], u2), "mw": ([16], f4), "nw": ([16], f4),
+    "jb": ([192], f4), "jb1": ([192], f4), "jc": ([32], f4), "dlw": ([P], f4),
+    "cs": ([24], f4), "ci": ([8], i4), "cand": ([80], bf), "cum": ([80], bf), "inc": ([80], f4), "dv": ([80], bf), "dv1": ([80], bf), "dv2": ([80], bf),
+    "sou": ([32], u2), "dl": ([16], f4), "dlu": ([16], u2), "mw": ([16], f4), "nw": ([16], f4),
     "hd": ([P], bf), "wd": ([P], bf), "bta": ([P], bf), "btz": ([P], bf), "inv": ([P], bf), "dvs": ([P], f4), "dvu": ([P], u2),
     "s1": ([P], f4), "s2": ([P], f4), "tt": ([512], f4), "tv": ([P], f4), "em": ([512], bf), "made": ([P], bf), "ii": ([P], bf), "nbc": ([P], f4),
     "prm": ([16], u2), "prf": ([16], f4), "tr": ([32], f4), "trt": ([32], f4), "d1": ([V], bf), "d2": ([V], bf), "c127": ([64], bf),
     "xi": ([256], f4), "gi": ([128], f4), "wt": ([16, 128], bf), "bm": ([5, 144], bf), "bmf": ([144], f4), "idf": ([128], f4),
-    "xs": ([80], f4), "pn": ([P], bf), "mt": ([19, 128], bf), "tb": ([16], f4), "pw": ([16], f4), "pw2": ([16], f4), "ones": ([2048], bf),
+    "xs": ([80], f4), "pn": ([P], bf), "mt": ([21, 128], bf),
+    "tin": ([5, 2, 16], bf), "tin2": ([32], bf), "tct": ([160], bf), "tbt": ([32], bf), "ca": ([P], bf), "cb": ([P], bf), "cc": ([P], bf),
+    "ib": ([P], bf), "obf": ([16], f4), "tb": ([16], f4), "pw": ([16], f4), "pw2": ([16], f4), "ones": ([2048], bf),
 }
 SCRATCH = {k: ("sbuf", [128] + s, d) for k, (s, d) in SB.items()}
 for _k in range(8):
     SCRATCH["ps%d" % _k] = ("psum", [128, 512], "float32")
 NDMA = 48
-SEMAPHORES = ["qv", "qa", "qp", "qg", "arr0", "arr1", "out0", "out1"] + ["d%d" % k for k in range(NDMA)]
-HOP = 120.0
-TRIES = 60
+SEMAPHORES = ["qv", "qa", "qp", "qg", "arr0", "arr1", "out0", "out1", "arr2", "arr3", "out2", "out3"] + ["d%d" % k for k in range(NDMA)]
+HOP = 200.0
+TRIES = 2200
+PLANS = {}
+CASES = ((-0.5, -2.0, 0.0, 1.0, 300.0, 1.4), (0.45, 2.0, -20.0, 1.0, 100.0, 0.8), (0.0, 0.0, 30.0, 1.2, 250.0, 1.3))
 PLAIN = ((1, 0, 0), (1, 0, 0))
+RELU = ((0, 0, 0), (0, 0, 0))
+SPLIT = ((0, 0, 0), (0, 0, 0))
+WEAVE = 2
+BOOST = 4000.0
+WHOLE = (0, 1, 1)
 
 
 def rank_program(g, core, T, topo):
@@ -74,6 +84,7 @@ def rank_program(g, core, T, topo):
         rd = [x for x in rd if isinstance(x, tuple)]
         rd = rd + [x[6] for x in rd + wr if len(x) > 6]
         ops.append({"e": eng, "fn": fn, "cost": cost, "lat": lat, "kind": kind,
+                    "ng": sum(x[4] for x in rd if len(x) > 6), "ns": sum(x[4] for x in wr if len(x) > 6),
                     "tr": [x[1:4] for x in rd], "tw": [x[1:4] for x in wr],
                     "rd": [x[1:4] for x in rd],
                     "wr": [x[1:4] for x in wr] + [("bank" + x[1], 0, 1) for x in rd + wr if x[1].startswith("ps")]})
@@ -131,7 +142,7 @@ def rank_program(g, core, T, topo):
     def M(k):
         return R("mt", k)
     ID, NI, I255, I8, NIH, IA, IZ, IN0, IN1, I256, N2048, IBIG, ONES, TRI, TF = [M(k) for k in range(15)]
-    NI8, NTF, ON17 = M(16), M(17), M(18)
+    NI8, NTF, ON17, ON16, NON = M(16), M(17), M(18), M(19), M(20)
 
     def W(kind, r):
         if kind == "f":
@@ -171,13 +182,18 @@ def rank_program(g, core, T, topo):
     tt(TRI, TRI, ONES, A.mult)
     ts(R("bmf"), x144, G15, A.is_equal)
     ts(R("tb"), S("xi", 0, 16), FC, A.is_equal)
-    ts(R("jc"), S("xi", 0, 80), 16.0, A.mult, FC, A.add)
-    ts(R("jb"), S("xi", 0, 192), 16.0, A.mult, FC, A.add)
-    ts(R("nw"), S("jc", 0, 16), float(V), A.add)
-    ts(R("jc"), R("jc"), 256.0, A.add)
-    ts(R("jb1"), R("jb"), float(Y1 - LO), A.add)
-    ts(R("jb"), R("jb"), float(Y0 - LO), A.add)
-    ms(R("one"), 1.0)
+    act(S("s2", 0, 192), S("xi", 0, 192), bias=FC, scale=16.0)
+    act(R("nw"), S("s2", 0, 16), bias=float(V))
+    act(S("jc", 0, 16), S("s2", 0, 16), bias=4096.0, scale=16.0)
+    act(S("jc", 16, 32), S("s2", 0, 16), scale=16.0)
+    ts(col(18), FC, 14.5, A.is_gt, 4096.0, A.mult)
+    ts(S("ci", 3, 4), S("ci", 0, 1), 16, A.bitwise_and)
+    cp(col(19), S("ci", 3, 4))
+    ms(R("tin2"), 512.0)
+    iota(R("ib"), [[1, 256]], 0, 0)
+    act(ON16, ONES, scale=16.0)
+    act(R("jb1"), S("s2", 0, 192), bias=float(Y1 - LO))
+    act(R("jb"), S("s2", 0, 192), bias=float(Y0 - LO))
     ms(R("c127"), -127.5)
     for m, c in ((NI, -1.0), (I255, 255 / 512), (I8, 0.125), (NI8, -0.125), (NIH, -0.5), (IA, 2.0 * CW), (IZ, 1.0 * CW), (IN0, 1024.0), (IN1, 1280.0),
                  (I256, 1 / 256), (N2048, -2048.0), (IBIG, 131072.0)):
@@ -189,6 +205,7 @@ def rank_program(g, core, T, topo):
     tt(TF, TF, M(15), A.add)
     act(NTF, TF, scale=-1.0)
     act(ON17, ONES, scale=17.0)
+    act(NON, ONES, scale=-1.0)
     ms(R("pw2"), 2.0)
     ms(R("prf"), 0.0)
     op("v", lambda e: e.tensor_tensor_scan(T.pw[:], T.pw2[:], T.prf[:], 0.5, A.mult, A.add), 100, [R("pw2"), R("prf")], [R("pw")])
@@ -206,24 +223,25 @@ def rank_program(g, core, T, topo):
     tt(R("pw"), R("pw"), R("tb"), A.mult)
     op("v", lambda e: e.tensor_reduce(RC[0], T.pw[:], AX.X, A.add), 100, [R("pw")], [RC])
     tt(RC, RC, col(12), A.mult)
-    ts(R("s1"), R("xi"), RC, A.mult, -0.5 + 2.0 ** -10, A.add)
-    ts(R("s2"), R("s1"), MAG, A.add, -MAG, A.add)
-    tt(R("s1"), R("s1"), R("s2"), A.subtract)
-    ts(R("bta"), R("s1"), 0.0, A.is_gt, MA, A.mult)
-    ts(R("btz"), R("s1"), 0.0, A.is_gt, MZ, A.mult)
+    act(R("s1"), R("xi"), bias=-0.5 + 2.0 ** -10, scale=RC)
+    ts(R("tv"), R("s1"), MAG, A.add, -MAG, A.add)
+    tt(R("made"), R("tv"), R("s1"), A.is_lt)
+    act(R("bta"), R("made"), scale=MA)
+    act(R("btz"), R("made"), scale=MZ)
     ts(col(13), S("tb", 1, 2), 2048.0, A.mult, S("tb", 0, 1), A.add)
-    ts(WSC, S("tb", 2, 3), 2.0 ** 22, A.mult, col(13), A.add)
+    ts(col(21), S("tb", 3, 4), 900.0, A.mult, col(13), A.add)
+    ts(WSC, S("tb", 2, 3), 2.0 ** 22, A.mult, col(21), A.add)
     ts(R("bm", WS), x144, G15, A.is_equal, WSC, A.mult)
     act(R("ii"), R("xi"), bias=-128.0)
-    act(R("dum"), R("xi"), bias=1280.0)
     ts(col(14), FC, 16.0, A.mult)
     ts(R("prm"), S("xi", 0, 16), col(14), A.add)
     z = lambda a, b: S("ones", 0, b - a)
     ms(S("win", 0, 16), 0.0)
-    for name, a, b in (("win", LO + V, LO + C), ("lw", V, CW), ("lw", CW + V, CW + C), ("hif", V, C), ("bl", V, C)):
+    for name, a, b in (("win", LO + V, LO + C), ("lw", V, C), ("lw", CW + V, CW + C), ("hif", V, C), ("bl", V, C)):
         act(S(name, a, b), z(a, b), scale=0.0)
-    ms(R("e0"), 0.0)
-    ms(R("e1"), 0.0)
+    for nm in ("e0", "e1"):
+        ms(S(nm, KB, 192), 0.0)
+        ms(S(nm, 192 + KB, 384), 0.0)
 
     for h in range(2):
         cp(S("e0", 192 * h, 192 * h + KB), R("eni", h, slice(0, KB)))
@@ -235,7 +253,7 @@ def rank_program(g, core, T, topo):
     ops[-1]["rd"].append(S("lv", 0, KB)[1:4])
     for r in range(16):
         o, i = S("win", Y0 + r, Y0 + B, 16), S("yn", KB * r, KB * r + KB)
-        (cp if r % 2 else act)(o, i)
+        (cp if r % WEAVE == 1 else act)(o, i)
         ops[-1]["tag"] = "weave"
     ts(S("bl", 0, V), R("bli"), 1.0, A.add)
     sn = lambda k: S("snf", 24 * k, 24 * k + 21)
@@ -249,7 +267,7 @@ def rank_program(g, core, T, topo):
         cp(S("snu", 0, nlow), S("snf", 48, 48 + nlow))
     if nlow < 21:
         ts(S("snu", nlow, 21), S("snf", 48 + nlow, 69), 192.0, A.add)
-    cp(R("mk"), IND(R("tb"), S("snu", 24, 45)))
+    act(R("mk"), IND(R("tb"), S("snu", 24, 45)))
     act(R("d1"), S("yn", 0, V), bias=-3.5)
     ts(R("d2"), R("d1"), MAG * 8, A.add, -MAG * 8, A.add)
 
@@ -260,9 +278,34 @@ def rank_program(g, core, T, topo):
         tt(R("gm"), IND(R("e%d" % t), S("snu", 0, 21)), R("mk"), A.mult)
         pb = 2 if t == 0 else 5
         mm([(ps(pb, 0, 21), W("f", r), S("gm", r, GH, 16)) for r in range(16)])
-        for k in range(3):
-            cp(S("ow", k, 42, 6), ps(pb, k, 21, 3))
-            ts(S("ow", 3 + k, 42, 6), ps(pb, k, 21, 3), float(CW), A.add)
+        K = 64 + 16 * t
+        own = ps(pb, 0, 21)
+        cp(S("ow", 0, 21), own)
+        ts(sn(0), own, 1.0 / K, A.mult, -0.5 + 0.5 / K, A.add)
+        ts(sn(1), sn(0), MAG, A.add, -MAG, A.add)
+        cp(S("ow", 24, 45), sn(1))
+        ts(sn(2), sn(1), -float(K), A.mult)
+        tt(sn(3), own, sn(2), A.add)
+        cp(S("ow", 48, 69), sn(3))
+        act(R("mk2"), IND(R("tb"), S("ow", 24, 45)))
+        act(R("sx%d" % t), IND(S("xa" if t == 0 else "xb", 0, V + P * t), S("ow", 0, 21)))
+        send("sx%d" % t, "lx%d" % t, 2 + t)
+        dl = float(DELTA[t])
+        ts(R("fhi"), R("lx%d" % t), dl, A.add, 63.0, A.min)
+        ts(R("flo"), R("lx%d" % t), -dl, A.add, 0.0, A.max)
+
+    def send(sb, land, k):
+        def fn(e):
+            trs = []
+            for d in range(1, N):
+                dst = T.cores[(q + d) % N]
+                rid, pid, _ = topo.addr(dst)
+                en = topo.engines(core, dst)
+                mask = (1 << en[2 * (d - 1)]) | (1 << en[2 * (d - 1) + 1])
+                trs.append(RemoteDMATransfer(dst_ids=[DstId(rid=rid, pnc=pid)], dma_engine_mask=mask, remote_sem=T.sem["arr%d" % k],
+                                             src=T[sb][:, 48 * (d - 1):48 * d], dst=T[land][:, 48 * (N - 1 - d):48 * (N - d)]))
+            e.remote_dma_fused(trs, local_sem=T.sem["out%d" % k])
+        op("g", fn, 300, [R(sb)], [R(land)], lat=2500.0, kind="r%d" % k)
 
     def banks_of(t):
         rb = 8 if t == 0 else 6
@@ -273,7 +316,7 @@ def rank_program(g, core, T, topo):
         ts(S("hif", 0, Ct), S(X, 0, Ct), dl, A.add, 63.0, A.min)
         ts(S("lof", 0, Ct), S(X, 0, Ct), -dl, A.add, 0.0, A.max)
         mm([(ps(6, 64, 64 + K), W(P8, r), S(X, K * r, K * r + K)) for r in range(16)])
-        act(S("xs", 0, K), ps(6, 64, 64 + K))
+        act(S("xs", 0, K), ps(6, 64, 64 + K), bias=0.5 - 124.0 - 8.0 * THETA[t])
 
     def cell_preload(t):
         X, K = "xa" if t == 0 else "xb", 64 + 16 * t
@@ -297,19 +340,21 @@ def rank_program(g, core, T, topo):
         E, En = "e%d" % t, "e%d" % (t + 1)
         YB = Y0 if t == 0 else Y1
         if t == 0:
-            cp(S("ci", 4, 5), col(15))
+            ts(TH, col(15), -8.0, A.mult, 124.0, A.add)
         else:
-            ts(S("ci", 4, 5), col(16), 0.5, A.mult, col(15), A.add)
-        ts(S("ci", 5, 6), S("ci", 4, 5), 31, A.bitwise_and)
-        ts(TH, S("ci", 5, 6), 8.0, A.mult, 8.0 * THETA[t] - 0.5, A.add)
-        ts(S("cand", 0, K), S("xs", 0, K), TH, A.is_gt)
-        op("v", lambda e, K=K: e.tensor_tensor_scan(T.cum[:, 0:K], T.one[:, 0:K], T.cand[:, 0:K], 0.0, A.mult, A.add), 100,
-           [R("one"), R("cand")], [R("cum")])
-        ts(S("dv2", 0, K), S("xs", 0, K), TH, A.is_gt, dl / 2, A.mult)
+            ts(col(15), col(15), -8.0, A.mult, 124.0, A.add)
+            ts(TH, col(16), -4.0, A.mult, col(15), A.add)
+        ts(col(20), TH, MAG * 256, A.add, -MAG * 256, A.add)
+        ts(S("cand", 0, K), S("xs", 0, K), TH, A.add, col(20), A.is_gt)
+        op("v", lambda e, K=K: e.tensor_tensor_scan(T.cum[:, 0:K], T.ones[:, 0:K], T.cand[:, 0:K], 0.0, A.mult, A.add), 100,
+           [R("ones"), R("cand")], [R("cum")])
+        ts(S("dv2", 0, K), S("cand", 0, K), dl / 2, A.mult)
         off = ps(7, 300, 301)
         mm([(off, TRI, S("cum", K - 1, K))])
         ts(S("dv1", 0, K), S("cum", 0, K), off, A.add, 256.5, A.is_lt)
         tt(S("dv", 0, K), S("dv1", 0, K), S("dv2", 0, K), A.mult)
+        tt(R("sb%d" % t), IND(S("dv", 0, K), S("ow", 48, 69)), R("mk2"), A.mult)
+        send("sb%d" % t, "land%d" % t, t)
         for k, (r0, r1) in enumerate(banks_of(t)):
             w = (r1 - r0) * K
             for kk_ in (k, 3 + k):
@@ -317,54 +362,62 @@ def rank_program(g, core, T, topo):
             ts(S("lw", K * r0, K * r1), ps(k, 0, w), -1.0, A.mult, 0.0, A.max)
             act(S("lw", CW + K * r0, CW + K * r1), ps(3 + k, 0, w), F.Relu, bias=-2.0 * dl, scale=4.0)
         sb, land = "sb%d" % t, "land%d" % t
-        cp(S(sb, 0, 320), IND(S("lw", 0, CW + C), S("ow", 0, 20)))
-        act(S(sb, 320, 672), IND(S("lw", 0, CW + C), S("ow", 20, 42)))
-
-        def send(e, t=t, sb=sb, land=land):
-            trs = []
-            for d in range(1, N):
-                dst = T.cores[(q + d) % N]
-                rid, pid, _ = topo.addr(dst)
-                en = topo.engines(core, dst)
-                mask = (1 << en[2 * (d - 1)]) | (1 << en[2 * (d - 1) + 1])
-                trs.append(RemoteDMATransfer(dst_ids=[DstId(rid=rid, pnc=pid)], dma_engine_mask=mask, remote_sem=T.sem["arr%d" % t],
-                                             src=T[sb][:, 96 * (d - 1):96 * d], dst=T[land][:, N - 1 - d, :]))
-            e.remote_dma_fused(trs, local_sem=T.sem["out%d" % t])
-        op("g", send, 300, [R(sb)], [R(land)], lat=3000.0, kind="r%d" % t)
         ts(S("inc", 0, K), S("cum", 0, K), off, A.add, -1.0, A.add)
         if t == 1:
             late[0]()
-        cp(S("lw", C, CW), R(land, slice(None), slice(0, 48)))
-        act(S("lw", CW + C, 2 * CW), R(land, slice(None), slice(48, 96)))
-        act(S("win", LO, LO + Ct), S("lw", 0, Ct), scale=2.0)
+        f0, f1 = ps(2, 0, GH), ps(5, 0, GH)
+        mm([(f0, NIH, R("lx%d" % t))], stop=False)
+        mm([(f1, I8, R("fhi")), (f1, NI8, R("flo"))], stop=False)
+        mm([(f0, ONES, R(land))], start=False)
+        mm([(f1, ONES, R(land))], start=False)
+        ts(S("lw", C, CW), f0, -1.0, A.mult, 0.0, A.max)
+        act(S("lw", CW + C, 2 * CW), f1, F.Relu, bias=-2.0 * dl, scale=4.0)
+        if t == 0:
+            act(S("win", LO, LO + Ct), S("lw", 0, Ct), scale=2.0)
+        else:
+            ts(S("win", LO, LO + Ct), S("lw", 0, Ct), 2.0, A.mult)
         ts(S("win", LO + C, LO + CW), S("lw", C, CW), 2.0, A.mult)
-        mm([(ps(5, 0, GH), ID, S("lw", C, CW)), (ps(5, 0, GH), ID, S("lw", CW + C, 2 * CW))])
-        act(S("win", HA + C, HA + CW), ps(5, 0, GH), scale=2.0)
-        ts(S("win", HZ + C, HZ + CW), S("win", HA + C, HA + CW), 1.0, A.mult)
-        iota(S("ids", 0, Ct), [[1, K], [K, 16]], 0, 0)
+        dma(S("win", HA + C, HA + CW), R("fhi"))
+        dma(S("win", HZ + C, HZ + CW), R("fhi"))
         if t == 0:
             for nm, a, b, v in (("win", HA, HA + C, 0), ("win", HZ, HZ + C, 0), ("info", 0, 3328, 1)):
                 iota(S(nm, a, b), [[0, b - a]], v, 0)
                 ops[-1]["rd"].append(R(land)[1:4])
-        ts(S("so", 0, K), S("dv", 0, K), 1.0, A.is_lt, 4096.0, A.mult)
-        tt(S("so", 0, K), S("so", 0, K), S("inc", 0, K), A.add)
-        tt(S("so", 0, K), S("so", 0, K), S("jc", 0, K), A.min)
-        cp(S("sou", 0, K), S("so", 0, K))
-        act(S("dlw", 0, P), R("dum"))
-        for a in range(0, K, 16):
-            cp(IND(R("dlw"), S("sou", a, a + 16)), S("ids", 16 * a, 16 * a + 256))
-            ops[-1]["rd"].append(R(sb)[1:4])
-        DL = S("dlw", 0, P)
+        nk = K // 16
+        for h in range(2):
+            ts(R("tin", slice(0, nk), h), S("inc", 0, K), 255.0, A.min)
+            ts(S("tin2", 16 * h, 16 * h + nk - 1), S("inc", 15, K - 1, 16), 255.0, A.min)
+        op("v", lambda e, nk=nk: e.transpose(T.tct[:, 0:32 * nk], T.tin[:, 0:nk]), 30 + 16 * nk, [R("tin")], [R("tct")])
+        op("v", lambda e: e.transpose(T.tbt[:], T.tin2[:]), 94, [R("tin2")], [R("tbt")])
+        ts(col(17), S("inc", K - 1, K), col(18), A.add)
+        ts(R("ca"), R("ib"), col(17), A.is_gt, float(K), A.mult)
+        pa_, pk_ = ps(7, 0, 16), ps(7, 16, 32)
+        mm([(pa_, W(P8, r), S("ca", r, P, 16)) for r in range(16)])
+        ts(R("obf"), pa_, 1.0 / (8 * K), A.mult, col(19), A.add)
+        cp(S("sou", 0, 16), R("obf"))
+        tt(R("cb"), IND(R("tbt"), S("sou", 0, 16)), R("ib"), A.is_lt)
+        mm([(pk_, W(P8, r), S("cb", r, P, 16)) for r in range(16)])
+        ts(R("dl"), pk_, 4.0, A.mult)
+        tt(R("dl"), R("dl"), R("obf"), A.add)
+        cp(S("sou", 16, 32), R("dl"))
+        tt(R("cc"), IND(S("tct", 0, 32 * nk), S("sou", 16, 32)), R("ib"), A.is_lt)
+        mm([(ps(7, P, 2 * P), ONES, R("ca")), (ps(7, P, 2 * P), ON16, R("cb")), (ps(7, P, 2 * P), ONES, R("cc"))])
+        DL = R("dlw")
+        act(DL, ps(7, P, 2 * P))
         mm([(ps(7, 0, 16), W("f", r), S("dlw", r, P, 16)) for r in range(16)])
-        ts(R("dl"), ps(7, 0, 16), 1 / 16, A.mult)
+        ts(R("obf"), ps(7, 0, 16), 16.0 * Ct - 8, A.is_gt)
+        tt(R("obf"), R("obf"), S("jc", 16 * t, 16 * t + 16), A.mult)
+        tt(R("dl"), ps(7, 0, 16), R("obf"), A.add)
+        ts(R("dl"), R("dl"), 1 / 16, A.mult)
         cp(R("dlu"), R("dl"))
         act(R("hd"), IND(R("hif"), R("dlu")))
         act(R("wd"), IND(S("lw", CW, CW + C), R("dlu")), scale=2.0)
         act(R("dvs"), IND(R("bl"), R("dlu")))
-        cp(R("dvu"), R("dvs"))
+        ts(R("dvu"), R("dvs"), 7.0, A.add)
         tt(IND(S("win", HA, HA + C), R("dlu")), R("hd"), R("bta"), A.add)
         tt(IND(S("win", HZ, HZ + C), R("dlu")), R("hd"), R("btz"), A.add)
-        ts(R("inv"), DL, 1279.5, A.is_gt, -1024.0, A.mult)
+        ops[-1]["lead"] = ops[-2]["lead"] = BOOST
+        ts(R("inv"), DL, Ct - 0.5, A.is_gt, -1024.0, A.mult)
         act(R("nbc"), R("xi"), bias=float(B + P * t + 1 - 4096 * 48))
         for k in range(3):
             ts(R("kk", k, slice(0, NC)), S("lv", 0, NC), k + 1 - 8192.0, A.mult, 8192.0, A.add)
@@ -384,13 +437,14 @@ def rank_program(g, core, T, topo):
             c0, c1 = chunks[k]
             n, o = c1 - c0, 1024 * (k % 2) - 16 * c0
             U = lambda nm, a, b: S(nm, o + 16 * a, o + 16 * b)
-            for a, b in units(c0, c1):
+            big = [(c0, c1)] if WHOLE[k] else units(c0, c1)
+            for a, b in big:
                 tt(U("tu", a, b), IND(loh, S("eu", a, b)), S("win", YB + 16 * a, YB + 16 * b), A.subtract)
                 act(U("wa", a, b), IND(wh, S("eu", a, b)))
-            for a, b in units(c0, c1):
+            for a, b in big:
                 tt(U("t00", a, b), IND(loh, S("eu", 192 + a, 192 + b)), U("tu", a, b), A.add)
             plain = PLAIN[t][k]
-            for a, b in units(c0, c1):
+            for a, b in big:
                 if plain:
                     act(U("t01", a, b), IND(wh, S("eu", 192 + a, 192 + b)))
                 else:
@@ -398,7 +452,10 @@ def rank_program(g, core, T, topo):
             for a, b in units(c0, c1):
                 w = 16 * (b - a)
                 p0, p1 = ps((2 * (a // 32)) % 3, 0, w), ps((2 * (a // 32) + 1) % 3, 0, w)
-                act(U("a00", a, b), U("t00", a, b), F.Abs)
+                if RELU[t][k]:
+                    ts(U("a00", a, b), U("t00", a, b), 0.0, A.max, 2.0, A.mult)
+                else:
+                    act(U("a00", a, b), U("t00", a, b), F.Abs)
                 mm([(p0, ID, U("t00", a, b)), (p0, ID, U("wa", a, b))])
                 act(U("a10", a, b), p0, F.Abs)
                 if plain:
@@ -415,7 +472,7 @@ def rank_program(g, core, T, topo):
             reg = lambda x: ps(5, 64 * x, 64 * x + n)
             lin = ((P8, "wa"), (P8, "t01")) if plain else ((P8, "wa"), (N8, "t00"), (P8, "t01"))
             mm([(reg(4), NI, kk(0))] + [(reg(4), W(w_, r), Z(nm, r)) for w_, nm in lin for r in range(16)])
-            mm([(reg(0), W(P8, r), Z("a00", r)) for r in range(16)])
+            mm([(reg(0), W(P8, r), Z("a00", r)) for r in range(16)] + [(reg(0), W(N8, r), Z("t00", r)) for r in range(16 * RELU[t][k])])
             mm([(reg(3), ID, kk(1))] + [(reg(3), W(P8, r), Z("a10", r)) for r in range(16)])
             mm([(reg(2), ID, kk(0))] + [(reg(2), W(P8, r), Z("a01", r)) for r in range(16)])
             mm([(reg(1), ID, kk(2))] + [(reg(1), W(P8, r), Z("a11", r)) for r in range(16)])
@@ -448,14 +505,21 @@ def rank_program(g, core, T, topo):
             U = lambda nm, a, b: S(nm, o + 16 * a, o + 16 * b)
             for a, b in units(c0, c1):
                 act(U("ga", a, b), IND(awin, S("ofs", a, b)))
-                tt(U("dd", a, b), IND(zwin, S("ofs", 192 + a, 192 + b)), U("ga", a, b), A.subtract)
+                if SPLIT[t][k]:
+                    act(U("dd", a, b), IND(zwin, S("ofs", 192 + a, 192 + b)))
+                else:
+                    tt(U("dd", a, b), IND(zwin, S("ofs", 192 + a, 192 + b)), U("ga", a, b), A.subtract)
             for a, b in units(c0, c1):
-                ts(U("hh", a, b), U("dd", a, b), MAG, A.add, -MAG, A.add)
+                d_ = U("dd", a, b)
+                if SPLIT[t][k]:
+                    d_ = ps((a // 32) % 2, 0, 16 * (b - a))
+                    mm([(d_, ID, U("dd", a, b)), (d_, NI, U("ga", a, b))])
+                ts(U("hh", a, b), d_, MAG, A.add, -MAG, A.add)
                 act(U("ah", a, b), U("hh", a, b), F.Abs)
             n = c1 - c0
             Z = lambda nm, r, cb=c1: S(nm, o + 16 * c0 + r, o + 16 * cb, 16)
             pl, ys = ps(7, 128, 128 + n), ps(6, 192, 192 + n)
-            mm([(pl, W(w_, r), Z(nm, r)) for w_, nm in ((WP, "dd"), (WN, "hh")) for r in range(16)] + [(pl, ID, S("c127", 0, n))])
+            mm([(pl, W(w_, r), Z(nm, r)) for w_, nm in ((WP, "dd"),) + ((WN, "ga"),) * SPLIT[t][k] + ((WN, "hh"),) for r in range(16)] + [(pl, ID, S("c127", 0, n))])
             if t == 0:
                 for a, b in units(c0, c1):
                     pb, w = 3 + (a // 32) % 2, 16 * (b - a)
@@ -509,9 +573,10 @@ def rank_program(g, core, T, topo):
         phase2(1)
         post(1)
         if t == 1:
-            for x in range(3):
-                dma(S("info", 3072, 3328, part=slice(x, 128, 16)), R("zi", x, slice(KB, NC)), eng="s", tag="n")
-            cp(S("info", 1 + B, 1 + B + P), IND(S("info", 3072, 3328), R("prm")))
+            for x in range(4):
+                dma(S("info", 3072, 3328, part=slice(x, 128, 16)), R("zi", min(x, 2), slice(KB, NC)), eng="s", tag="n")
+            act(S("info", 8 + B, 8 + B + P), IND(S("info", 3072, 3328), R("prm")))
+            ops[-1]["tag"] = "i1"
             for h in range(2):
                 cp(S("tr", 16 * h, 16 * h + 16), S("e2", 192 * h + KB, 192 * h + NC))
             op("v", lambda e: e.transpose(T.trt[:], T.tr[:]), 100, [R("tr")], [R("trt")])
@@ -535,8 +600,8 @@ def rank_program(g, core, T, topo):
             cell_preload(1)
             old_live()
 
-        for x in range(3):
-            dma(S("info", 1, 1 + B, part=slice(x, 128, 16)), R("zi", x, slice(0, KB)), eng="sas"[x], tag="i%d" % t)
+        for x in range(4):
+            dma(S("info", 8, 8 + B, part=slice(x, 128, 16)), R("zi", min(x, 2), slice(0, KB)), eng="sasa"[x], tag="i%d" % t)
         if t == 1:
             dma(T.yy[:, 0:B], R("yo"))
             ops[-1]["rd"].append(S("info", 16, 32)[1:4])
@@ -556,14 +621,13 @@ def rank_program(g, core, T, topo):
             ts(sl("em", P), oo, 3.0 * 2 ** 20, A.is_gt)
             tt(ps(pk, 128, 192), oo, sl("s1"), A.is_equal)
             ts(sl("s2"), sl("s1"), 0.0, A.is_equal)
-            tt(ps(pk, 192, 256), ps(pk, 128, 192), sl("s2"), A.max)
-            tt(sl("em"), ps(pk, 192, 256), sl("em", P), A.is_gt)
+            tt(sl("em"), ps(pk, 128, 192), sl("s2"), A.max)
         mv, dead = S("em", 0, P), S("em", P, 2 * P)
         if t == 0:
-            g2 = ps(6, 0, P)
-            mm([(g2, ID, R("pn")), (g2, ONES, dead), (g2, ON17, mv)])
-            act(R("s2"), g2, F.Abs, bias=-136.0)
-            op("a", lambda e: e.activation(T.tv[:], T.s2[:], F.Sign, bias=135.5, scale=-1.0, accum_out=col(16)[0]), 350, [R("s2")], [R("tv"), col(16)])
+            g2, g3 = ps(6, 0, P), ps(6, P, 2 * P)
+            mm([(g2, ID, R("pn")), (g2, ONES, dead), (g2, ONES, mv)])
+            mm([(g3, NI, R("pn")), (g3, ONES, S("ones", 0, P)), (g3, NON, mv)])
+            op("a", lambda e: e.activation(T.tt[:], T.ps6[:], F.Sign, bias=-0.5, accum_out=col(16)[0]), 700, [ps(6)], [R("tt"), col(16)])
 
         def slot_tail(t=t, n0=n0, mv=mv, dead=dead):
             b0, b1, b2, b3 = (6, 7, 6, 7) if t == 0 else (0, 1, 2, 3)
@@ -642,7 +706,7 @@ def emit(ops, queue, T):
             succ[j].append(k)
     tail = [0.0] * n
     for k in range(n - 1, -1, -1):
-        tail[k] = ops[k]["cost"] + ops[k]["lat"] + max([HOP + tail[j] for j in succ[k]] + [0.0])
+        tail[k] = ops[k]["cost"] + ops[k]["lat"] + ops[k].get("lead", 0.0) + max([HOP + tail[j] for j in succ[k]] + [0.0])
     gap = [[ops[k]["lat"] + (0.0 if free_edge(k, j) else HOP) for j in succ[k]] for k in range(n)]
 
     def plan(pri, look):
@@ -682,15 +746,51 @@ def emit(ops, queue, T):
                     ready[ops[j]["e"]].append(j)
         return end, order, start
 
+    plan0 = plan
+    back = [[(j, ops[j]["lat"], 0.0 if free_edge(j, k) else 1.0) for j in deps[k]] for k in range(n)]
+    cases = [([o["cost"] + dg * o["ng"] + ds * o["ns"] + fx + (pe - 1.0) * o["cost"] * (o["e"] == "p") for o in ops], hop, lat)
+             for dg, ds, fx, pe, hop, lat in CASES]
+
+    def plan(pri, look):
+        end, order, start = plan0(pri, look)
+        for cost, hop, lat in cases:
+            fin = [0.0] * n
+            free = {e: 0.0 for e in queue}
+            last = 0.0
+            for k in order:
+                s = free[ops[k]["e"]]
+                for j, l, h in back[k]:
+                    x = fin[j] + l * lat + h * hop
+                    if x > s:
+                        s = x
+                fin[k] = free[ops[k]["e"]] = s + cost[k]
+                if ops[k]["lat"]:
+                    last = max(last, fin[k] + ops[k]["lat"] * lat)
+            end += last
+        return end / (1 + len(cases)), order, start
+
     rng = np.random.RandomState(7)
     base = np.array([tail[k] + (1e6 if ops[k]["kind"] != "c" else 0.0) - 1e-3 * k for k in range(n)])
-    best = None
-    for trial in range(TRIES):
-        amp = (0.0, 100.0, 400.0, 1200.0)[(trial // 5) % 4]
-        cand = plan(list(base + amp * rng.rand(n)), (0.0, 0.3, 0.5, 0.7, 0.9)[trial % 5])
-        if best is None or cand[0] < best[0]:
-            best = cand
-    end, order, start = best
+    if n not in PLANS:
+        best = None
+        for trial in range(20):
+            pri, look = base + (0.0, 100.0, 400.0, 1200.0)[trial // 5] * rng.rand(n), (0.0, 0.3, 0.5, 0.7, 0.9)[trial % 5]
+            end = plan(list(pri), look)[0]
+            if best is None or end < best[0]:
+                best = (end, pri, look)
+        for trial in range(TRIES):
+            pri = best[1].copy()
+            a = rng.randint(n)
+            if trial % 2:
+                pri[a:a + rng.randint(1, 40)] += rng.randn() * 3000.0
+            else:
+                pri[a:a + 120] += rng.randn(len(pri[a:a + 120])) * 500.0
+            look = best[2] if trial % 7 else rng.rand()
+            end = plan(list(pri), look)[0]
+            if end <= best[0]:
+                best = (end, pri, look)
+        PLANS[n] = best
+    end, order, start = plan(list(PLANS[n][1]), PLANS[n][2])
     for k in range(n):
         ops[k]["st"] = start[k]
     pos = {k: i for i, k in enumerate(order)}

@@ -8,28 +8,32 @@ CW = C + GH
 LO, HZ, HA, Y0, Y1, WEND = 16, 16 + CW, 16 + 2 * CW, 16 + 3 * CW, 16 + 3 * CW + B, 16 + 3 * CW + B + B + P
 KB = 173
 MAG = 1.5 * 2 ** 23
+CUT = (0, 128)
+ZB = 16 * (KB - CUT[-1])
+EPS = 2.0 ** -13
+NB = 16 * (KB + 16)
 
 bf, f4, i4, u2 = "bfloat16", "float32", "int32", "uint16"
 SB = {
-    "win": ([WEND], bf), "lw": ([2 * CW], bf), "hif": ([C], bf), "lof": ([1280], bf), "yn": ([B], bf), "xa": ([1280], bf), "xb": ([1280], bf),
-    "yo": ([16, KB], bf), "yon": ([512], bf), "bli": ([V], i4), "bl": ([C], f4), "ylo": ([C], f4),
-    "eni": ([2, 176], i4), "e0": ([384], f4), "e1": ([384], f4), "e2": ([384], f4), "eu": ([384], u2), "ofs": ([384], u2),
-    "sni": ([24], i4), "snf": ([96], f4), "snu": ([48], u2), "mk": ([GH], f4), "gm": ([GH], f4), "ow": ([72], u2),
+    "win": ([WEND], bf), "lw": ([2 * CW], bf), "hif": ([C], bf), "lof": ([1280], bf), "yn": ([B], bf), "xa": ([V], bf), "xb": ([1280], bf),
+    "yo": ([16, KB], bf), "yon": ([ZB + 512], bf), "bli": ([V], i4), "bl": ([C], f4),
+    "eni": ([2 * KB], i4), "e0": ([384], f4), "e1": ([384], f4), "e2": ([384], f4), "eu": ([2, 192], u2), "ofs": ([384], u2),
+    "far": ([2, 192], bf), "ppl": ([2, 192], bf), "cod": ([192], bf),
+    "sni": ([24], i4), "snf": ([144], f4), "snu": ([72], u2), "mk": ([GH], f4), "gm": ([GH], f4), "ow": ([72], u2), "owt": ([136], f4),
     "sb0": ([GH], bf), "sb1": ([GH], bf), "land0": ([GH], bf), "land1": ([GH], bf), "fhi": ([GH], bf), "flo": ([GH], bf),
     "sx0": ([GH], bf), "sx1": ([GH], bf), "lx0": ([GH], bf), "lx1": ([GH], bf), "mk2": ([GH], bf),
-    "tu": ([2048], bf), "t00": ([2048], bf), "t01": ([2048], bf), "wa": ([2048], bf),
-    "a00": ([2048], bf), "a01": ([2048], bf), "a10": ([2048], bf), "a11": ([2048], bf),
-    "ga": ([2048], bf), "dd": ([2048], bf), "hh": ([2048], bf), "ah": ([2048], bf),
-    "kb": ([128], f4), "mm": ([128], f4), "pp": ([384], bf), "ut": ([64], bf), "oa": ([64], f4), "zq": ([64], bf), "pla": ([64], bf),
-    "lv": ([192], bf), "kk": ([3, 192], bf), "zi": ([3, 192], bf), "info": ([3328], bf), "gs": ([4096], bf),
-    "jb": ([192], f4), "jb1": ([192], f4), "jc": ([32], f4), "dlw": ([P], f4),
-    "cs": ([24], f4), "ci": ([8], i4), "cand": ([80], bf), "cum": ([80], bf), "inc": ([80], f4), "dv": ([80], bf), "dv1": ([80], bf), "dv2": ([80], bf),
+    "tu": ([NB], bf), "t00": ([NB], bf), "t01": ([NB], bf), "wa": ([NB], bf),
+    "r00": ([NB], bf), "r01": ([NB], bf), "r10": ([NB], bf), "r11": ([NB], bf),
+    "dkt": ([len(CUT) + 1, 128], bf), "rr": ([256], f4), "ppt": ([256], bf), "ut": ([128], bf), "nnt": ([256], bf), "oa": ([128], f4),
+    "info": ([3040], bf), "gs": ([4096], bf), "jb": ([192], f4), "jb1": ([192], f4), "jc": ([32], f4), "dlw": ([P], f4),
+    "cs": ([28], f4), "ci": ([8], i4), "cand": ([80], bf), "cum": ([80], bf), "inc": ([80], f4), "dv": ([80], bf), "dv1": ([80], f4), "dv2": ([80], f4),
     "sou": ([32], u2), "dl": ([16], f4), "dlu": ([16], u2), "mw": ([16], f4), "nw": ([16], f4),
-    "hd": ([P], bf), "wd": ([P], bf), "bta": ([P], bf), "btz": ([P], bf), "inv": ([P], bf), "dvs": ([P], f4), "dvu": ([P], u2),
-    "s1": ([P], f4), "s2": ([P], f4), "tt": ([512], f4), "tv": ([P], f4), "em": ([512], bf), "made": ([P], bf), "ii": ([P], bf), "nbc": ([P], f4),
-    "prm": ([16], u2), "prf": ([16], f4), "tr": ([32], f4), "trt": ([32], f4), "d1": ([V], bf), "d2": ([V], bf), "c127": ([64], bf),
-    "xi": ([256], f4), "gi": ([128], f4), "wt": ([16, 128], bf), "bm": ([5, 144], bf), "bmf": ([144], f4), "idf": ([128], f4),
-    "xs": ([80], f4), "pn": ([P], bf), "mt": ([21, 128], bf),
+    "hd": ([P], bf), "wd": ([P], bf), "bta": ([P], bf), "btz": ([P], bf), "inv": ([P], bf), "nd": ([2, P], f4), "dvu": ([P], u2),
+    "s1": ([P], f4), "s2": ([P], f4), "tt": ([512], f4), "tv": ([P], f4), "em": ([3, P], bf), "made": ([P], bf), "ii": ([P], bf),
+    "fv": ([2, P], f4), "fn": ([2, P], f4),
+    "prf": ([16], f4), "tr": ([32], f4), "trt": ([32], f4), "d2": ([V], bf),
+    "xi": ([256], f4), "gi": ([128], f4), "wt": ([16, 128], bf), "bm": ([2, 144], bf), "bmf": ([144], f4), "idf": ([128], f4),
+    "xs": ([80], f4), "pn": ([P], bf), "mt": ([28, 128], bf), "st": ([64], bf), "sw": ([32], bf),
     "tin": ([5, 2, 16], bf), "tin2": ([32], bf), "tct": ([160], bf), "tbt": ([32], bf), "ca": ([P], bf), "cb": ([P], bf), "cc": ([P], bf),
     "ib": ([P], bf), "obf": ([16], f4), "tb": ([16], f4), "pw": ([16], f4), "pw2": ([16], f4), "ones": ([2048], bf),
 }
@@ -42,12 +46,15 @@ HOP = 200.0
 TRIES = 2200
 PLANS = {}
 CASES = ((-0.5, -2.0, 0.0, 1.0, 300.0, 1.4), (0.45, 2.0, -20.0, 1.0, 100.0, 0.8), (0.0, 0.0, 30.0, 1.2, 250.0, 1.3))
-PLAIN = ((1, 0, 0), (1, 0, 0))
-RELU = ((0, 0, 0), (0, 0, 0))
-SPLIT = ((0, 0, 0), (0, 0, 0))
+PLAIN = ((0, 1), (0, 1))
+RV00 = ((0, 0), (0, 0))
+RV01 = ((0, 0), (0, 0))
+RVAH = ((0, 0), (0, 0))
+GU = (32, 64, 64, 32)
+GSV = (1, 3, 5)
 WEAVE = 2
 BOOST = 4000.0
-WHOLE = (0, 1, 1)
+HALVES = (1, 2)
 
 
 def rank_program(g, core, T, topo):
@@ -115,9 +122,12 @@ def rank_program(g, core, T, topo):
     def ms(o, c):
         op("v", lambda e: e.memset(o[0], c), vcost(o, o), [], [o])
 
-    def act(o, i, f=F.Identity, bias=0.0, scale=1.0):
-        op("a", lambda e: e.activation(o[0], i[0], f, bias=ap(bias), scale=ap(scale)),
-           70 + o[4] * (1.6 if len(i) > 6 else 1.0), [i, bias, scale], [o])
+    def act(o, i, f=F.Identity, bias=0.0, scale=1.0, acc=None):
+        if acc is None:
+            op("a", lambda e: e.activation(o[0], i[0], f, bias=ap(bias), scale=ap(scale)),
+               70 + o[4] * (1.6 if len(i) > 6 else 1.0), [i, bias, scale], [o])
+        else:
+            op("a", lambda e: e.activation(o[0], i[0], f, bias=ap(bias), scale=ap(scale), accum_out=acc[0]), 100 + o[4], [i, bias, scale], [o, acc])
 
     def mm(items, start=True, stop=True):
         def fn(e):
@@ -125,7 +135,7 @@ def rank_program(g, core, T, topo):
             for k, (o, l, x) in enumerate(items):
                 r = e.matmul(o[0], l[0], x[0], start and k == 0, stop and k == len(items) - 1)
             return r
-        cost = sum(max(64, x[4]) * (2.0 if x[5] == 4 else 0.5) for o, l, x in items)
+        cost = sum(max(min(64, l[4]), x[4]) * (2.0 if x[5] == 4 else 0.5) for o, l, x in items)
         op("p", fn, cost, [x for o, l, x in items] + [l for o, l, x in items], [o for o, l, x in items])
 
     def iota(o, pat, base, cm, small=True):
@@ -139,30 +149,37 @@ def rank_program(g, core, T, topo):
         op(eng, lambda e: e.dma_start(ap(o), ap(i)), 80, [i], w, lat=lat, kind="d")
         ops[-1]["tag"] = tag
 
-    def M(k):
-        return R("mt", k)
-    ID, NI, I255, I8, NIH, IA, IZ, IN0, IN1, I256, N2048, IBIG, ONES, TRI, TF = [M(k) for k in range(15)]
-    NI8, NTF, ON17, ON16, NON = M(16), M(17), M(18), M(19), M(20)
+    (ID, NI, I255, I8, NI8, NIH, IA, IZ, IN0, IN1, IK2, IK3, ONES, TRI, A1, NA1, O8192, A3, CV, N8192, P8192, K8, ON17, ON16, NON,
+     N255, KD) = range(27)
+
+    def M(k, n=128, m=None):
+        return R("mt", k, slice(0, n if m is None else m), part=slice(0, n))
 
     def W(kind, r):
         if kind == "f":
             return S("bmf", 15 - r, 143 - r)
         return R("bm", kind, slice(15 - r, 143 - r))
-    P8, N8, WP, WN, WS = 0, 1, 2, 3, 4
+    P8, WS = 0, 1
 
     def col(k):
         return S("cs", k, k + 1)
-    PC, FC, GC, G15, PWC, RC, MA, MZ, WSC, TH, NPW = [col(k) for k in range(11)]
+    PC, FC, GC, G15, PWC, RC, MA, MZ, WSC, TH, UO = [col(k) for k in range(11)]
 
-    def ps(k, a=0, b=512, st=1):
-        return S("ps%d" % k, a, b, st)
+    def ps(k, a=0, b=512, st=1, n=None):
+        return S("ps%d" % k, a, b, st, part=None if n is None else slice(0, n))
 
-    dma(S("yn", 0, B // 2), T.y0[:, 0:B // 2], lat=2600.0, tag="y")
-    dma(S("yn", B // 2, B), T.y0[:, B // 2:B], eng="a", lat=3200.0, tag="y")
-    dma(S("xa", 0, V), T.x0[:, :], lat=3600.0)
-    dma(S("sni", 0, 21), T.snd[:, :], lat=3000.0)
+    def chunks_of(t):
+        return list(zip(CUT, CUT[1:] + (KB + 16 * t,)))
+
+    def dk(k, n):
+        return R("dkt", k, part=slice(0, n))
+
     for h in range(2):
-        dma(R("eni", h, slice(0, KB)), T.en0[h::2, :], eng="sa"[h], lat=3400.0, tag="e")
+        dma(S("eni", KB * h, KB * h + KB), T.en0[h::2, :], eng="sa"[h], lat=2600.0, tag="e")
+    dma(S("sni", 0, 21), T.snd[:, :], lat=2400.0)
+    dma(S("yn", 0, B // 2), T.y0[:, 0:B // 2], lat=3000.0, tag="y")
+    dma(S("yn", B // 2, B), T.y0[:, B // 2:B], eng="a", lat=3400.0, tag="y")
+    dma(R("xa"), T.x0[:, :], lat=3600.0)
 
     iota(R("xi"), [[1, 256]], 0, 0)
     iota(S("ci", 0, 1), [[0, 1]], 0, 1, small=False)
@@ -174,14 +191,18 @@ def rank_program(g, core, T, topo):
     ts(S("ci", 2, 3), S("ci", 0, 1), 4, A.arith_shift_right)
     cp(S("cs", 1, 3), S("ci", 1, 3))
     ts(G15, GC, 16.0, A.mult, 15.0, A.add)
-    x144 = S("xi", 0, 144)
+    x144, x8 = S("xi", 0, 144), S("xi", 0, 8)
     ts(R("bm", P8), x144, G15, A.is_equal, 8.0, A.mult)
-    ts(ONES, R("gi"), GC, A.is_equal)
-    ts(ID, S("xi", 0, 128), PC, A.is_equal)
-    ts(TRI, S("xi", 0, 128), PC, A.is_gt)
-    tt(TRI, TRI, ONES, A.mult)
+    ts(M(ONES), R("gi"), GC, A.is_equal)
+    ts(M(ID), S("xi", 0, 128), PC, A.is_equal)
+    ts(M(TRI), S("xi", 0, 128), PC, A.is_gt)
+    tt(M(TRI), M(TRI), M(ONES), A.mult)
     ts(R("bmf"), x144, G15, A.is_equal)
     ts(R("tb"), S("xi", 0, 16), FC, A.is_equal)
+    ts(S("owt", 128, 136), x8, GC, A.is_equal)
+    ts(S("st", 0, 8), x8, GC, A.is_equal, 8.0, A.mult)
+    for k, c in ((1, 0.0), (2, 1.0), (3, 1.0), (4, 1.0), (5, -1.0), (6, -1.0), (7, -1.0)):
+        act(S("st", 8 * k, 8 * k + 8), S("st", 0, 8), scale=c)
     act(S("s2", 0, 192), S("xi", 0, 192), bias=FC, scale=16.0)
     act(R("nw"), S("s2", 0, 16), bias=float(V))
     act(S("jc", 0, 16), S("s2", 0, 16), bias=4096.0, scale=16.0)
@@ -190,22 +211,21 @@ def rank_program(g, core, T, topo):
     ts(S("ci", 3, 4), S("ci", 0, 1), 16, A.bitwise_and)
     cp(col(19), S("ci", 3, 4))
     ms(R("tin2"), 512.0)
-    iota(R("ib"), [[1, 256]], 0, 0)
-    act(ON16, ONES, scale=16.0)
+    act(R("ib"), R("xi"))
     act(R("jb1"), S("s2", 0, 192), bias=float(Y1 - LO))
     act(R("jb"), S("s2", 0, 192), bias=float(Y0 - LO))
-    ms(R("c127"), -127.5)
-    for m, c in ((NI, -1.0), (I255, 255 / 512), (I8, 0.125), (NI8, -0.125), (NIH, -0.5), (IA, 2.0 * CW), (IZ, 1.0 * CW), (IN0, 1024.0), (IN1, 1280.0),
-                 (I256, 1 / 256), (N2048, -2048.0), (IBIG, 131072.0)):
-        act(m, ID, scale=c)
-    act(R("idf"), ID)
-    act(R("bm", N8), R("bm", P8), scale=-1.0)
-    ts(TF, TRI, -4096.0, A.mult)
-    act(M(15), ID, scale=65536.0)
-    tt(TF, TF, M(15), A.add)
-    act(NTF, TF, scale=-1.0)
-    act(ON17, ONES, scale=17.0)
-    act(NON, ONES, scale=-1.0)
+    for m, c in ((NI, -1.0), (I255, 255 / 512), (N255, -255 / 512), (I8, 0.125), (NI8, -0.125), (NIH, -0.5), (IA, 2.0 * CW), (IZ, 1.0 * CW),
+                 (IN0, 2.0), (IN1, 2.5), (IK2, -16384.0), (IK3, -24576.0), (N8192, -8192.0), (P8192, 8192.0), (CV, -33.0 * 2 ** 19)):
+        if m != N255 or any(RVAH[0] + RVAH[1]):
+            act(M(m), M(ID), scale=c)
+    act(M(K8), M(ID), scale=-1.0, bias=64.0)
+    act(R("idf"), M(ID))
+    for m, c in ((O8192, 8192.0), (ON16, 16.0), (ON17, 17.0), (NON, -1.0)):
+        act(M(m), M(ONES), scale=c)
+    tt(M(A3), M(ID), M(TRI), A.subtract)
+    act(M(A3), M(A3), scale=262144.0)
+    tt(M(A1), M(A3), M(O8192), A.subtract)
+    act(M(NA1), M(A1), scale=-1.0)
     ms(R("pw2"), 2.0)
     ms(R("prf"), 0.0)
     op("v", lambda e: e.tensor_tensor_scan(T.pw[:], T.pw2[:], T.prf[:], 0.5, A.mult, A.add), 100, [R("pw2"), R("prf")], [R("pw")])
@@ -213,71 +233,66 @@ def rank_program(g, core, T, topo):
     op("v", lambda e: e.tensor_reduce(PWC[0], T.pw[:], AX.X, A.add), 100, [R("pw")], [PWC])
     ts(MA, FC, 7.5, A.is_lt, 0.25, A.mult)
     ts(MZ, FC, 7.5, A.is_gt, 0.25, A.mult)
-    ts(col(11), MZ, 32.0, A.mult, -4.0, A.add)
-    tt(NPW, PWC, col(11), A.mult)
-    ts(R("bm", WP), x144, G15, A.is_equal, NPW, A.mult)
-    act(R("bm", WN), R("bm", WP), scale=-1.0)
+    ts(col(11), PWC, MA, A.mult, -16.0, A.mult)
+    ts(col(13), PWC, MZ, A.mult, 1.0 / 16, A.mult)
+    ts(S("sw", 0, 8), x8, GC, A.is_equal, col(11), A.mult)
+    ts(S("sw", 8, 16), x8, GC, A.is_equal, col(13), A.mult)
+    act(S("sw", 16, 32), S("sw", 0, 16), scale=-1.0)
     ts(col(12), MZ, 1020.0, A.mult, 1.0, A.add)
-    ms(R("pw2"), 0.5)
-    op("v", lambda e: e.tensor_tensor_scan(T.pw[:], T.pw2[:], T.prf[:], 1.0, A.mult, A.add), 100, [R("pw2"), R("prf")], [R("pw")])
-    tt(R("pw"), R("pw"), R("tb"), A.mult)
-    op("v", lambda e: e.tensor_reduce(RC[0], T.pw[:], AX.X, A.add), 100, [R("pw")], [RC])
-    tt(RC, RC, col(12), A.mult)
+    op("v", lambda e: e.reciprocal(RC[0], PWC[0]), 200, [PWC], [RC])
+    ts(RC, RC, col(12), A.mult, 0.5, A.mult)
     act(R("s1"), R("xi"), bias=-0.5 + 2.0 ** -10, scale=RC)
     ts(R("tv"), R("s1"), MAG, A.add, -MAG, A.add)
     tt(R("made"), R("tv"), R("s1"), A.is_lt)
     act(R("bta"), R("made"), scale=MA)
     act(R("btz"), R("made"), scale=MZ)
-    ts(col(13), S("tb", 1, 2), 2048.0, A.mult, S("tb", 0, 1), A.add)
-    ts(col(21), S("tb", 3, 4), 900.0, A.mult, col(13), A.add)
-    ts(WSC, S("tb", 2, 3), 2.0 ** 22, A.mult, col(21), A.add)
-    ts(R("bm", WS), x144, G15, A.is_equal, WSC, A.mult)
+    ts(R("bm", WS), x144, G15, A.is_equal, S("tb", 0, 1), A.mult)
     act(R("ii"), R("xi"), bias=-128.0)
-    ts(col(14), FC, 16.0, A.mult)
-    ts(R("prm"), S("xi", 0, 16), col(14), A.add)
-    z = lambda a, b: S("ones", 0, b - a)
     ms(S("win", 0, 16), 0.0)
-    for name, a, b in (("win", LO + V, LO + C), ("lw", V, C), ("lw", CW + V, CW + C), ("hif", V, C), ("bl", V, C)):
-        act(S(name, a, b), z(a, b), scale=0.0)
-    for nm in ("e0", "e1"):
-        ms(S(nm, KB, 192), 0.0)
-        ms(S(nm, 192 + KB, 384), 0.0)
+    for a, b in ((V, C), (CW + V, CW + C)):
+        ms(S("lw", a, b), 0.0)
+    ms(R("far"), 0.0)
+    ms(S("e1", KB, 192), 0.0)
+    ms(S("e1", 192 + KB, 384), 0.0)
 
+    sn = lambda k: S("snf", 24 * k, 24 * k + 21)
+    nlow = 3 * (N - 1 - q)
+    ts(sn(4), S("xi", 0, 21), nlow - 0.5, A.is_gt, float(KB), A.mult)
+    ts(sn(5), S("xi", 0, 21), nlow - 0.5, A.is_gt, 192.0 - KB, A.mult)
+    ts(sn(0), S("sni", 0, 21), 1.0 / KB, A.mult, -0.5 + 0.5 / KB, A.add)
+    ts(sn(1), sn(0), MAG, A.add, -MAG, A.add)
+    cp(S("snu", 24, 45), sn(1))
+    tt(sn(4), sn(4), S("sni", 0, 21), A.add)
+    ts(sn(2), sn(1), -float(KB), A.mult)
+    tt(sn(2), sn(2), sn(4), A.add)
+    cp(S("snu", 0, 21), sn(2))
+    tt(sn(5), sn(5), sn(2), A.add)
+    cp(S("snu", 48, 69), sn(5))
+    act(R("mk"), IND(R("tb"), S("snu", 24, 45)))
+    for k, (c0, c1) in enumerate(chunks_of(0)):
+        n = c1 - c0
+        pb = (7, 5)[k % 2]
+        mm([(ps(pb, r, 128, 16, n=n), S("yn", KB * r + c0, KB * r + c1), S("st", 0, 8)) for r in range(16)])
+        ts(dk(k, n), ps(pb, 0, 128, n=n), 1407.5, A.is_lt, EPS, A.add)
     for h in range(2):
-        cp(S("e0", 192 * h, 192 * h + KB), R("eni", h, slice(0, KB)))
-        cp(S("eu", 192 * h, 192 * h + KB), R("eni", h, slice(0, KB)))
-    mm([(ps(7, 0, KB), W(P8, r), S("yn", KB * r, KB * r + KB)) for r in range(7)], stop=False)
-    mm([(ps(7, 0, KB), W(P8, r), S("yn", KB * r, KB * r + KB)) for r in range(7, 16)], start=False)
-    ts(S("lv", 0, KB), ps(7, 0, KB), 1407.5, A.is_gt)
+        cp(S("e0", 192 * h, 192 * h + KB), S("eni", KB * h, KB * h + KB))
+    cp(R("eu", slice(None), slice(0, KB)), R("eni"))
+    ts(R("far", slice(None), slice(0, KB)), R("eni"), C - 0.5, A.is_gt)
     dma(R("bli"), T.bl0[:, :], lat=3000.0)
-    ops[-1]["rd"].append(S("lv", 0, KB)[1:4])
+    ops[-1]["rd"].append(dk(0, 1)[1:4])
     for r in range(16):
         o, i = S("win", Y0 + r, Y0 + B, 16), S("yn", KB * r, KB * r + KB)
         (cp if r % WEAVE == 1 else act)(o, i)
         ops[-1]["tag"] = "weave"
-    ts(S("bl", 0, V), R("bli"), 1.0, A.add)
-    sn = lambda k: S("snf", 24 * k, 24 * k + 21)
-    ts(sn(0), S("sni", 0, 21), 1.0 / KB, A.mult, -0.5 + 0.5 / KB, A.add)
-    ts(sn(1), sn(0), MAG, A.add, -MAG, A.add)
-    cp(S("snu", 24, 45), sn(1))
-    ts(sn(2), sn(1), -float(KB), A.mult)
-    tt(sn(2), sn(2), S("sni", 0, 21), A.add)
-    nlow = 3 * (N - 1 - q)
-    if nlow > 0:
-        cp(S("snu", 0, nlow), S("snf", 48, 48 + nlow))
-    if nlow < 21:
-        ts(S("snu", nlow, 21), S("snf", 48 + nlow, 69), 192.0, A.add)
-    act(R("mk"), IND(R("tb"), S("snu", 24, 45)))
-    act(R("d1"), S("yn", 0, V), bias=-3.5)
-    ts(R("d2"), R("d1"), MAG * 8, A.add, -MAG * 8, A.add)
-
-    def reduce(o, i):
-        op("v", lambda e: e.tensor_reduce(o[0], i[0], AX.X, A.add), 30 + max(64, i[4]), [i], [o])
+    cp(S("bl", 0, V), R("bli"))
+    ts(R("d2"), S("yn", 0, V), 1028.5, A.add)
 
     def own_cells(t):
-        tt(R("gm"), IND(R("e%d" % t), S("snu", 0, 21)), R("mk"), A.mult)
+        tt(R("gm"), IND(R("eni") if t == 0 else R("e1"), S("snu", 48 * t, 48 * t + 21)), R("mk"), A.mult)
         pb = 2 if t == 0 else 5
-        mm([(ps(pb, 0, 21), W("f", r), S("gm", r, GH, 16)) for r in range(16)])
+        mm([(ps(pb, r, 128, 16, n=21), S("gm", r, GH, 16), S("owt", 128, 136)) for r in range(16)])
+        act(S("owt", 0, 128, part=slice(0, 21)), ps(pb, 0, 128, n=21))
+        mm([(ps(pb, 0, 21), S("owt", 0, 128, part=slice(0, 21)), S("idf", 0, 21, part=slice(0, 21)))])
         K = 64 + 16 * t
         own = ps(pb, 0, 21)
         cp(S("ow", 0, 21), own)
@@ -315,44 +330,43 @@ def rank_program(g, core, T, topo):
         X, K, Ct, dl = "xa" if t == 0 else "xb", 64 + 16 * t, V + P * t, float(DELTA[t])
         ts(S("hif", 0, Ct), S(X, 0, Ct), dl, A.add, 63.0, A.min)
         ts(S("lof", 0, Ct), S(X, 0, Ct), -dl, A.add, 0.0, A.max)
-        mm([(ps(6, 64, 64 + K), W(P8, r), S(X, K * r, K * r + K)) for r in range(16)])
-        act(S("xs", 0, K), ps(6, 64, 64 + K), bias=0.5 - 124.0 - 8.0 * THETA[t])
+        pb = 6 + t
+        mm([(ps(pb, 0, K), W(P8, r), S(X, K * r, K * r + K)) for r in range(16)])
+        act(S("xs", 0, K), ps(pb, 0, K), bias=0.5 - 124.0 - 8.0 * THETA[t])
 
     def cell_preload(t):
         X, K = "xa" if t == 0 else "xb", 64 + 16 * t
         for k, (r0, r1) in enumerate(banks_of(t)):
             w = (r1 - r0) * K
-            mm([(ps(k, 0, w), NIH, S(X, K * r0, K * r1))], stop=False)
-            mm([(ps(3 + k, 0, w), I8, S("hif", K * r0, K * r1)), (ps(3 + k, 0, w), NI8, S("lof", K * r0, K * r1))], stop=False)
+            mm([(ps(k, 0, w), M(NIH), S(X, K * r0, K * r1))], stop=False)
+            mm([(ps(3 + k, 0, w), M(I8), S("hif", K * r0, K * r1)), (ps(3 + k, 0, w), M(NI8), S("lof", K * r0, K * r1))], stop=False)
 
-    def old_live():
-        mm([(ps(7, 0, KB), ONES, S("lv", 0, KB))])
-        reduce(col(15), ps(7, 0, KB))
+    def old_live(u):
+        o = ps(7, 384, 512)
+        mm([(o, M(ID), M(O8192))], stop=False)
+        mm([(o, S("ones", 0, 128, part=slice(0, c1 - c0)), dk(k, c1 - c0)) for k, (c0, c1) in enumerate(chunks_of(0))], start=False)
+        act(S("tt", 0, 128), o, F.Relu, bias=-8192.0, acc=col(15))
+        ts(u, col(15), 8.0 / (1 - EPS), A.mult, 124.0 - 8.0 * B / (1 - EPS), A.add)
 
     own_cells(0)
     cell_sums(0)
     cell_preload(0)
-    old_live()
+    old_live(TH)
     late = []
     for t in range(2):
         Ct, K, NC = V + P * t, 64 + 16 * t, KB + 16 * t
         n0, dl = V + P * t, float(DELTA[t])
         E, En = "e%d" % t, "e%d" % (t + 1)
         YB = Y0 if t == 0 else Y1
-        if t == 0:
-            ts(TH, col(15), -8.0, A.mult, 124.0, A.add)
-        else:
-            ts(col(15), col(15), -8.0, A.mult, 124.0, A.add)
-            ts(TH, col(16), -4.0, A.mult, col(15), A.add)
         ts(col(20), TH, MAG * 256, A.add, -MAG * 256, A.add)
         ts(S("cand", 0, K), S("xs", 0, K), TH, A.add, col(20), A.is_gt)
-        op("v", lambda e, K=K: e.tensor_tensor_scan(T.cum[:, 0:K], T.ones[:, 0:K], T.cand[:, 0:K], 0.0, A.mult, A.add), 100,
-           [R("ones"), R("cand")], [R("cum")])
-        ts(S("dv2", 0, K), S("cand", 0, K), dl / 2, A.mult)
+        op("v", lambda e, K=K: e.tensor_tensor_scan(T.cum[:, 0:K], T.ones[:, 0:K], T.cand[:, 0:K], 0.0, A.mult, A.subtract), 100,
+           [S("ones", 0, K), R("cand")], [R("cum")])
+        ts(S("dv2", 0, K), S("cand", 0, K), -1024.0, A.mult, 767.5, A.add)
         off = ps(7, 300, 301)
-        mm([(off, TRI, S("cum", K - 1, K))])
-        ts(S("dv1", 0, K), S("cum", 0, K), off, A.add, 256.5, A.is_lt)
-        tt(S("dv", 0, K), S("dv1", 0, K), S("dv2", 0, K), A.mult)
+        mm([(off, M(TRI), S("cum", K - 1, K))])
+        tt(S("dv1", 0, K), S("dv2", 0, K), S("cum", 0, K), A.subtract)
+        ts(S("dv", 0, K), S("dv1", 0, K), off, A.is_lt, dl / 2, A.mult)
         tt(R("sb%d" % t), IND(S("dv", 0, K), S("ow", 48, 69)), R("mk2"), A.mult)
         send("sb%d" % t, "land%d" % t, t)
         for k, (r0, r1) in enumerate(banks_of(t)):
@@ -362,46 +376,44 @@ def rank_program(g, core, T, topo):
             ts(S("lw", K * r0, K * r1), ps(k, 0, w), -1.0, A.mult, 0.0, A.max)
             act(S("lw", CW + K * r0, CW + K * r1), ps(3 + k, 0, w), F.Relu, bias=-2.0 * dl, scale=4.0)
         sb, land = "sb%d" % t, "land%d" % t
-        ts(S("inc", 0, K), S("cum", 0, K), off, A.add, -1.0, A.add)
+        ts(S("inc", 0, K), S("cum", 0, K), off, A.add, -1.0, A.mult)
         if t == 1:
             late[0]()
         f0, f1 = ps(2, 0, GH), ps(5, 0, GH)
-        mm([(f0, NIH, R("lx%d" % t))], stop=False)
-        mm([(f1, I8, R("fhi")), (f1, NI8, R("flo"))], stop=False)
-        mm([(f0, ONES, R(land))], start=False)
-        mm([(f1, ONES, R(land))], start=False)
+        mm([(f0, M(NIH), R("lx%d" % t))], stop=False)
+        mm([(f1, M(I8), R("fhi")), (f1, M(NI8), R("flo"))], stop=False)
+        mm([(f0, M(ONES), R(land))], start=False)
+        mm([(f1, M(ONES), R(land))], start=False)
         ts(S("lw", C, CW), f0, -1.0, A.mult, 0.0, A.max)
         act(S("lw", CW + C, 2 * CW), f1, F.Relu, bias=-2.0 * dl, scale=4.0)
         if t == 0:
-            act(S("win", LO, LO + Ct), S("lw", 0, Ct), scale=2.0)
-        else:
-            ts(S("win", LO, LO + Ct), S("lw", 0, Ct), 2.0, A.mult)
+            for nm, a, b, v in (("hif", V, C, 0), ("win", HA, HA + C, 0), ("win", HZ, HZ + C, 0), ("win", LO + V, LO + C, 0), ("bl", V, C, -1),
+                                ("info", 0, 3040, -8192), ("yon", 0, ZB, 0)):
+                iota(S(nm, a, b), [[0, b - a]], v, 0)
+                ops[-1]["rd"].append(R(land)[1:4])
+        ts(S("win", LO, LO + Ct), S("lw", 0, Ct), 2.0, A.mult)
         ts(S("win", LO + C, LO + CW), S("lw", C, CW), 2.0, A.mult)
         dma(S("win", HA + C, HA + CW), R("fhi"))
         dma(S("win", HZ + C, HZ + CW), R("fhi"))
-        if t == 0:
-            for nm, a, b, v in (("win", HA, HA + C, 0), ("win", HZ, HZ + C, 0), ("info", 0, 3328, 1)):
-                iota(S(nm, a, b), [[0, b - a]], v, 0)
-                ops[-1]["rd"].append(R(land)[1:4])
         nk = K // 16
         for h in range(2):
-            ts(R("tin", slice(0, nk), h), S("inc", 0, K), 255.0, A.min)
-            ts(S("tin2", 16 * h, 16 * h + nk - 1), S("inc", 15, K - 1, 16), 255.0, A.min)
+            ts(R("tin", slice(0, nk), h), S("inc", 0, K), 256.0, A.min)
+            ts(S("tin2", 16 * h, 16 * h + nk - 1), S("inc", 15, K - 1, 16), 256.0, A.min)
         op("v", lambda e, nk=nk: e.transpose(T.tct[:, 0:32 * nk], T.tin[:, 0:nk]), 30 + 16 * nk, [R("tin")], [R("tct")])
         op("v", lambda e: e.transpose(T.tbt[:], T.tin2[:]), 94, [R("tin2")], [R("tbt")])
         ts(col(17), S("inc", K - 1, K), col(18), A.add)
-        ts(R("ca"), R("ib"), col(17), A.is_gt, float(K), A.mult)
+        ts(R("ca"), R("ib"), col(17), A.is_ge, float(K), A.mult)
         pa_, pk_ = ps(7, 0, 16), ps(7, 16, 32)
         mm([(pa_, W(P8, r), S("ca", r, P, 16)) for r in range(16)])
         ts(R("obf"), pa_, 1.0 / (8 * K), A.mult, col(19), A.add)
         cp(S("sou", 0, 16), R("obf"))
-        tt(R("cb"), IND(R("tbt"), S("sou", 0, 16)), R("ib"), A.is_lt)
+        tt(R("cb"), IND(R("tbt"), S("sou", 0, 16)), R("ib"), A.is_le)
         mm([(pk_, W(P8, r), S("cb", r, P, 16)) for r in range(16)])
         ts(R("dl"), pk_, 4.0, A.mult)
         tt(R("dl"), R("dl"), R("obf"), A.add)
         cp(S("sou", 16, 32), R("dl"))
-        tt(R("cc"), IND(S("tct", 0, 32 * nk), S("sou", 16, 32)), R("ib"), A.is_lt)
-        mm([(ps(7, P, 2 * P), ONES, R("ca")), (ps(7, P, 2 * P), ON16, R("cb")), (ps(7, P, 2 * P), ONES, R("cc"))])
+        tt(R("cc"), IND(S("tct", 0, 32 * nk), S("sou", 16, 32)), R("ib"), A.is_le)
+        mm([(ps(7, P, 2 * P), M(ONES), R("ca")), (ps(7, P, 2 * P), M(ON16), R("cb")), (ps(7, P, 2 * P), M(ONES), R("cc"))])
         DL = R("dlw")
         act(DL, ps(7, P, 2 * P))
         mm([(ps(7, 0, 16), W("f", r), S("dlw", r, P, 16)) for r in range(16)])
@@ -412,265 +424,275 @@ def rank_program(g, core, T, topo):
         cp(R("dlu"), R("dl"))
         act(R("hd"), IND(R("hif"), R("dlu")))
         act(R("wd"), IND(S("lw", CW, CW + C), R("dlu")), scale=2.0)
-        act(R("dvs"), IND(R("bl"), R("dlu")))
-        ts(R("dvu"), R("dvs"), 7.0, A.add)
+        act(R("nd", 1), IND(R("bl"), R("dlu")))
+        ts(R("dvu"), R("nd", 1), 8.0, A.add)
         tt(IND(S("win", HA, HA + C), R("dlu")), R("hd"), R("bta"), A.add)
         tt(IND(S("win", HZ, HZ + C), R("dlu")), R("hd"), R("btz"), A.add)
         ops[-1]["lead"] = ops[-2]["lead"] = BOOST
-        ts(R("inv"), DL, Ct - 0.5, A.is_gt, -1024.0, A.mult)
-        act(R("nbc"), R("xi"), bias=float(B + P * t + 1 - 4096 * 48))
-        for k in range(3):
-            ts(R("kk", k, slice(0, NC)), S("lv", 0, NC), k + 1 - 8192.0, A.mult, 8192.0, A.add)
+        ts(R("inv"), DL, Ct - 0.5, A.is_gt, 2.0 ** -7, A.add)
+        act(R("nd", 0), R("xi"), bias=float(B + P * t))
         if t == 1:
             dma(T.yx[:, 0:Ct], S("win", LO, LO + Ct))
             dma(T.yx[:, Ct:C], R("hd"))
-            act(S("ylo", 0, Ct), S("bl", 0, Ct), bias=-1.0)
+        if t == 0:
+            for a, b in ((0, 512), (512, V)):
+                mm([(ps(7), M(ID), S("win", LO + a, LO + b)), (ps(7), M(ID), S("yn", a, b)), (ps(7), M(NI), S("d2", a, b))])
+                act(S("xb", a, b), ps(7), F.Relu, bias=1029.0)
+            o = ps(7, 0, P)
+            mm([(o, M(ID), R("hd")), (o, M(ID), S("yn", 0, P)), (o, M(NI), S("d2", 0, P)), (o, M(N8192), R("inv"))])
+            act(S("xb", V, V + P), o, F.Relu, bias=1093.0)
+            ts(R("xb"), R("xb"), 63.0, A.min)
+            cell_sums(1)
+            mm([(ps(7, P, 2 * P), M(ONES), R("wd"))])
+            ts(R("pn"), ps(7, P, 2 * P), 175.5, A.is_lt, -1024.0, A.mult)
 
-        chunks = [(0, 64), (64, 128), (128, NC)] if t == 0 else [(0, 64), (128, NC), (64, 128)]
+        chunks = chunks_of(t)
         loh, wh = S("lw", 0, CW), S("lw", CW, 2 * CW)
         awin, zwin = S("win", LO, Y1 if t == 0 else WEND), S("win", 0, HA)
+        U = lambda nm, a, b: S(nm, 16 * a, 16 * b)
+        EU = lambda h, a, b: R("eu", h, slice(a, b))
+        rot = [0]
 
-        def units(c0, c1):
-            return [(a, min(c1, a + 32)) for a in range(c0, c1, 32)]
+        def units(c0, c1, w=32):
+            return [(a, min(c1, a + w)) for a in range(c0, c1, w)]
+
+        def bank(w):
+            rot[0] += 1
+            return ps(rot[0] % 3, 0, w)
+
+        def relu2(o, i, on_v):
+            if on_v:
+                ts(o, i, 0.0, A.max, 2.0, A.mult)
+            else:
+                act(o, i, F.Relu, scale=2.0)
 
         def phase1(k):
             c0, c1 = chunks[k]
-            n, o = c1 - c0, 1024 * (k % 2) - 16 * c0
-            U = lambda nm, a, b: S(nm, o + 16 * a, o + 16 * b)
-            big = [(c0, c1)] if WHOLE[k] else units(c0, c1)
-            for a, b in big:
-                tt(U("tu", a, b), IND(loh, S("eu", a, b)), S("win", YB + 16 * a, YB + 16 * b), A.subtract)
-                act(U("wa", a, b), IND(wh, S("eu", a, b)))
-            for a, b in big:
-                tt(U("t00", a, b), IND(loh, S("eu", 192 + a, 192 + b)), U("tu", a, b), A.add)
+            n, sc = c1 - c0, 5 - k % 2
             plain = PLAIN[t][k]
+            d_ = dk(len(CUT) if t == 1 and k == len(CUT) - 1 else k, n)
+            mm([(ps(sc, 128 * j, 128 * j + 128, n=n), M(m, n), d_) for j, m in enumerate((IK2, N8192, IK3, IK2))], stop=False)
+
+            def sums(nm, k0, k1, w0, stop=False):
+                mm([(ps(sc, 128 * k0 + r, 128 * k1, 16, n=n), S(nm, 16 * c0 + r, 16 * c1, 16), S("st", 8 * w0, 8 * (w0 + k1 - k0)))
+                    for r in range(16)], start=False, stop=stop)
+            big = units(c0, c1, GU[1])
+            if k == 0:
+                big = units(c0, c0 + GU[1], GU[0]) + big[1:]
             for a, b in big:
+                tt(U("tu", a, b), IND(loh, EU(0, a, b)), S("win", YB + 16 * a, YB + 16 * b), A.subtract)
+                act(U("wa", a, b), IND(wh, EU(0, a, b)))
+                tt(U("t00", a, b), IND(loh, EU(1, a, b)), U("tu", a, b), A.add)
                 if plain:
-                    act(U("t01", a, b), IND(wh, S("eu", 192 + a, 192 + b)))
+                    act(U("t01", a, b), IND(wh, EU(1, a, b)))
                 else:
-                    tt(U("t01", a, b), IND(wh, S("eu", 192 + a, 192 + b)), U("t00", a, b), A.add)
+                    tt(U("t01", a, b), IND(wh, EU(1, a, b)), U("t00", a, b), A.add)
             for a, b in units(c0, c1):
-                w = 16 * (b - a)
-                p0, p1 = ps((2 * (a // 32)) % 3, 0, w), ps((2 * (a // 32) + 1) % 3, 0, w)
-                if RELU[t][k]:
-                    ts(U("a00", a, b), U("t00", a, b), 0.0, A.max, 2.0, A.mult)
-                else:
-                    act(U("a00", a, b), U("t00", a, b), F.Abs)
-                mm([(p0, ID, U("t00", a, b)), (p0, ID, U("wa", a, b))])
-                act(U("a10", a, b), p0, F.Abs)
+                w, u = 16 * (b - a), (a // 32) % 4
+                relu2(U("r00", a, b), U("t00", a, b), u < RV00[t][k])
+                p0 = bank(w)
+                mm([(p0, M(ID), U("t00", a, b)), (p0, M(ID), U("wa", a, b))])
+                relu2(U("r10", a, b), p0, False)
                 if plain:
-                    mm([(p1, ID, U("t00", a, b)), (p1, ID, U("t01", a, b))])
-                    act(U("a01", a, b), p1, F.Abs)
-                    mm([(p0, ID, U("t00", a, b)), (p0, ID, U("wa", a, b)), (p0, ID, U("t01", a, b))])
-                    p1 = p0
+                    p1 = bank(w)
+                    mm([(p1, M(ID), U("t00", a, b)), (p1, M(ID), U("t01", a, b))])
+                    relu2(U("r01", a, b), p1, False)
+                    p1 = bank(w)
+                    mm([(p1, M(ID), U("t00", a, b)), (p1, M(ID), U("wa", a, b)), (p1, M(ID), U("t01", a, b))])
                 else:
-                    act(U("a01", a, b), U("t01", a, b), F.Abs)
-                    mm([(p1, ID, U("t01", a, b)), (p1, ID, U("wa", a, b))])
-                act(U("a11", a, b), p1, F.Abs)
-            Z = lambda nm, r: S(nm, o + 16 * c0 + r, o + 16 * c1, 16)
-            kk = lambda x: R("kk", x, slice(c0, c1))
-            reg = lambda x: ps(5, 64 * x, 64 * x + n)
-            lin = ((P8, "wa"), (P8, "t01")) if plain else ((P8, "wa"), (N8, "t00"), (P8, "t01"))
-            mm([(reg(4), NI, kk(0))] + [(reg(4), W(w_, r), Z(nm, r)) for w_, nm in lin for r in range(16)])
-            mm([(reg(0), W(P8, r), Z("a00", r)) for r in range(16)] + [(reg(0), W(N8, r), Z("t00", r)) for r in range(16 * RELU[t][k])])
-            mm([(reg(3), ID, kk(1))] + [(reg(3), W(P8, r), Z("a10", r)) for r in range(16)])
-            mm([(reg(2), ID, kk(0))] + [(reg(2), W(P8, r), Z("a01", r)) for r in range(16)])
-            mm([(reg(1), ID, kk(2))] + [(reg(1), W(P8, r), Z("a11", r)) for r in range(16)])
+                    relu2(U("r01", a, b), U("t01", a, b), u < RV01[t][k])
+                    p1 = bank(w)
+                    mm([(p1, M(ID), U("t01", a, b)), (p1, M(ID), U("wa", a, b))])
+                relu2(U("r11", a, b), p1, False)
+            sums("wa", 0, 4, 0)
+            if not plain:
+                sums("t00", 1, 4, 5)
+            sums("t01", 1, 4, 2)
+            sums("r00", 0, 3, 2)
+            sums("r10", 0, 1, 5)
+            sums("r01", 1, 2, 5)
+            sums("r11", 2, 3, 5, stop=True)
 
         def decide(k):
             c0, c1 = chunks[k]
-            n = c1 - c0
-            reg = lambda x: ps(5, 64 * x, 64 * x + n)
-            k01, k10 = S("kb", 0, n), S("kb", 64, 64 + n)
-            act(k01, reg(2))
-            act(k10, reg(3))
-            ts(S("ut", 0, n), reg(4), 0.5, A.is_lt, 16384.0, A.mult)
-            tt(S("mm", 0, n), reg(1), k10, A.min)
-            tt(S("mm", 64, 64 + n), reg(1), k01, A.min)
-            tt(reg(5), reg(0), k01, A.min)
-            tt(reg(6), reg(0), k10, A.min)
-            pa, pz = S("pp", c0, c1), S("pp", 192 + c0, 192 + c1)
-            tt(pa, reg(5), S("mm", 0, n), A.is_gt)
-            tt(pz, reg(6), S("mm", 64, 64 + n), A.is_gt)
-            oa, oz = ps(6, 0, n), ps(6, 64, 64 + n)
-            mm([(oa, R("idf"), S(E, c0, c1)), (oa, ID, S("ut", 0, n)), (oa, IA, pa)])
-            mm([(oz, R("idf"), S(E, 192 + c0, 192 + c1)), (oz, NI, S("ut", 0, n)), (oz, IZ, pz)])
+            n, sc = c1 - c0, 5 - k % 2
+            pn_ = slice(0, n)
+            oa, oz, pp = ps(3, 0, n), ps(3, 128, 128 + n), lambda h: ps(3, 256 + n * h, 256 + n * h + n)
+            mm([(oa, R("idf"), S(E, c0, c1)), (oz, R("idf"), S(E, 192 + c0, 192 + c1))]
+               + [(pp(h), M(NI), R("far", h, slice(c0, c1))) for h in range(2)], stop=False)
+            act(S("rr", 0, 256, part=pn_), ps(sc, 0, 256, n=n), F.Relu)
+            tt(ps(6, 0, 128, n=n), ps(sc, 256, 384, n=n), S("rr", 128, 256, part=pn_), A.max)
+            tt(ps(6, 128, 256, n=n), ps(sc, 256, 384, n=n), S("rr", 0, 128, part=pn_), A.max)
+            act(S("ut", 0, 128, part=pn_), ps(sc, 384, 512, n=n), F.Relu, scale=-1.0)
+            tt(S("ppt", 0, 256, part=pn_), ps(6, 0, 256, n=n), S("rr", 0, 256, part=pn_), A.is_gt)
+            pz, pa, ut = S("ppt", 0, 128, part=pn_), S("ppt", 128, 256, part=pn_), S("ut", 0, 128, part=pn_)
+            mm([(oa, ut, M(P8192, n)), (oz, ut, M(N8192, n))], start=False, stop=False)
+            mm([(oa, pa, M(IA, n)), (oz, pz, M(IZ, n)), (pp(0), pa, M(ID, n)), (pp(1), pz, M(ID, n))], start=False)
             tt(S("oa", 0, n), oa, S("jb" if t == 0 else "jb1", c0, c1), A.min)
-            ts(S("ofs", 192 + c0, 192 + c1), oz, 16.0, A.add)
             cp(S("ofs", c0, c1), S("oa", 0, n))
+            ts(S("ofs", 192 + c0, 192 + c1), oz, 16.0, A.add)
+            act(R("ppl", slice(None), slice(c0, c1)), ps(3, 256, 256 + 2 * n), F.Relu, scale=512.0)
 
         def phase2(k):
             c0, c1 = chunks[k]
-            o = 1024 * (k % 2) - 16 * c0
-            U = lambda nm, a, b: S(nm, o + 16 * a, o + 16 * b)
+            n, sc = c1 - c0, 5 - k % 2
+            GA, DD, HH, AH = "r00", "r01", "r10", "r11"
+            gu = GU[3] if k == len(chunks) - 1 else GU[2]
+            big = units(c0, c1, gu)
+            if k == 0:
+                big = units(c0, c0 + gu, 32) + big[1:]
+            for a, b in big:
+                act(U(GA, a, b), IND(awin, S("ofs", a, b)))
+                tt(U(DD, a, b), IND(zwin, S("ofs", 192 + a, 192 + b)), U(GA, a, b), A.subtract)
+                ts(U(HH, a, b), U(DD, a, b), MAG, A.add, -MAG, A.add)
+            onv = lambda a: (a // 32) % 4 < RVAH[t][k]
             for a, b in units(c0, c1):
-                act(U("ga", a, b), IND(awin, S("ofs", a, b)))
-                if SPLIT[t][k]:
-                    act(U("dd", a, b), IND(zwin, S("ofs", 192 + a, 192 + b)))
+                if onv(a):
+                    relu2(U(AH, a, b), U(HH, a, b), True)
                 else:
-                    tt(U("dd", a, b), IND(zwin, S("ofs", 192 + a, 192 + b)), U("ga", a, b), A.subtract)
-            for a, b in units(c0, c1):
-                d_ = U("dd", a, b)
-                if SPLIT[t][k]:
-                    d_ = ps((a // 32) % 2, 0, 16 * (b - a))
-                    mm([(d_, ID, U("dd", a, b)), (d_, NI, U("ga", a, b))])
-                ts(U("hh", a, b), d_, MAG, A.add, -MAG, A.add)
-                act(U("ah", a, b), U("hh", a, b), F.Abs)
-            n = c1 - c0
-            Z = lambda nm, r, cb=c1: S(nm, o + 16 * c0 + r, o + 16 * cb, 16)
-            pl, ys = ps(7, 128, 128 + n), ps(6, 192, 192 + n)
-            mm([(pl, W(w_, r), Z(nm, r)) for w_, nm in ((WP, "dd"),) + ((WN, "ga"),) * SPLIT[t][k] + ((WN, "hh"),) for r in range(16)] + [(pl, ID, S("c127", 0, n))])
+                    act(U(AH, a, b), U(HH, a, b), F.Abs)
+            mm([(ps(sc, 128 + r, 384, 16, n=n), S(nm, 16 * c0 + r, 16 * c1, 16), S("sw", w0, w0 + 16)) for nm, w0 in ((DD, 0), (HH, 16)) for r in range(16)])
+            act(S("nnt", 0, 256, part=slice(0, n)), ps(sc, 128, 384, n=n))
+            ys = lambda r, m=n: ps(sc, r, 128, 16, n=m)
+
+            def woven(a, b, o):
+                p = bank(16 * (b - a))
+                mm([(p, M(I255), S("win", YB + 16 * a, YB + 16 * b)), (p, M(I255), U(AH, a, b))] + [(p, M(N255), U(HH, a, b))] * onv(a))
+                ts(o, p, MAG, A.add, -MAG, A.add)
             if t == 0:
                 for a, b in units(c0, c1):
-                    pb, w = 3 + (a // 32) % 2, 16 * (b - a)
-                    mm([(ps(pb, 0, w), I255, S("win", Y0 + 16 * a, Y0 + 16 * b)), (ps(pb, 0, w), I255, U("ah", a, b))])
-                    ts(S("win", Y1 + 16 * a, Y1 + 16 * b), ps(pb, 0, w), MAG, A.add, -MAG, A.add)
-                mm([(ys, W(P8, r), S("win", Y1 + 16 * c0 + r, Y1 + 16 * c1, 16)) for r in range(16)])
+                    woven(a, b, S("win", Y1 + 16 * a, Y1 + 16 * b))
+                mm([(ys(r), S("win", Y1 + 16 * c0 + r, Y1 + 16 * c1, 16), S("st", 0, 8)) for r in range(16)])
             else:
                 cb = min(c1, KB)
                 m = cb - c0
-                for hf in range(2):
-                    for r in range(8 * hf, 8 * hf + 8):
-                        oo = ps(3 + hf, m * (r % 8), m * (r % 8 + 1))
-                        mm([(oo, I255, S("win", Y1 + 16 * c0 + r, Y1 + 16 * cb, 16)), (oo, I255, Z("ah", r, cb))])
-                    ts(R("yo", slice(8 * hf, 8 * hf + 8), slice(c0, cb)), ps(3 + hf, 0, 8 * m), MAG, A.add, -MAG, A.add)
+                rb = 16 if m <= 32 else 8 if m <= 64 else 4
                 if cb < c1:
-                    mm([(ps(2, 0, P), I255, S("win", Y1 + B, Y1 + B + P)), (ps(2, 0, P), I255, U("ah", cb, c1))])
-                    ts(S("yon", 0, P), ps(2, 0, P), MAG, A.add, -MAG, A.add)
-                mm([(ps(6, 192, 192 + m), W(P8, r), R("yo", r, slice(c0, cb))) for r in range(16)])
-                if cb < c1:
-                    mm([(ps(6, 192 + m, 192 + n), W(P8, r), S("yon", r, P, 16)) for r in range(16)])
+                    woven(cb, c1, S("yon", ZB, ZB + P))
+                    mm([(ys(r), S("yon", r, 16 * n, 16), S("st", 0, 8)) for r in range(16)], stop=False)
+                for r0 in range(0, 16, rb):
+                    p = bank(rb * m)
+                    its = []
+                    for r in range(r0, r0 + rb):
+                        oo = S(p[1], m * (r - r0), m * (r - r0 + 1))
+                        its += [(oo, M(I255), S("win", Y1 + 16 * c0 + r, Y1 + 16 * cb, 16)), (oo, M(I255), S(AH, 16 * c0 + r, 16 * cb, 16))]
+                        if RVAH[t][k]:
+                            its += [(oo, M(N255), S(HH, 16 * c0 + r, 16 * cb, 16))]
+                    mm(its)
+                    ts(R("yo", slice(r0, r0 + rb), slice(c0, cb)), p, MAG, A.add, -MAG, A.add)
+                    mm([(ys(r, m), R("yo", r, slice(c0, cb)), S("st", 0, 8)) for r in range(r0, r0 + rb)], start=r0 == 0 and cb == c1, stop=r0 + rb == 16)
 
         def post(k):
             c0, c1 = chunks[k]
-            n = c1 - c0
-            pl, ys = ps(7, 128, 128 + n), ps(6, 192, 192 + n)
-            zq, pla = S("zq", 0, n), S("pla", 0, n)
-            ts(zq, pl, MAG * 256, A.add, -MAG * 256, A.add)
-            tt(pla, pl, zq, A.subtract)
-            ts(R("zi", 2, slice(c0, c1)), ys, 1407.5, A.is_lt)
-            if t == 0:
-                ts(S("lv", c0, c1), ys, 1407.5, A.is_gt)
-            ra, rz = ps(7, 256, 256 + n), ps(7, 320, 320 + n)
+            n, sc = c1 - c0, 5 - k % 2
+            pn_ = slice(0, n)
+            na, nz = S("nnt", 0, 128, part=pn_), S("nnt", 128, 256, part=pn_)
+            PL = lambda h: R("ppl", h, slice(c0, c1))
+            cd = ps(6, 256, 256 + n)
+            mm([(cd, na, M(ID, n)), (cd, nz, M(ID, n)), (cd, M(ID), PL(0)), (cd, M(ID), PL(1))], stop=False)
             IN = IN0 if t == 0 else IN1
-            mm([(ra, NI, S("c127", 0, n)), (ra, IN, S("pp", c0, c1)), (ra, ID, pla)])
-            mm([(rz, IN, S("pp", 192 + c0, 192 + c1)), (rz, I256, zq)])
-            for h, rr in ((0, ra), (1, rz)):
-                ne = S(En, 192 * h + c0, 192 * h + c1)
-                tt(ne, rr, S(E, 192 * h + c0, 192 * h + c1), A.max)
-                ts(R("zi", h, slice(c0, c1)), ne, -(n0 + 128.0), A.add, -256.0, A.max)
-                if t == 0:
-                    cp(S("eu", 192 * h + c0, 192 * h + c1), ne)
-
-        phase1(0)
-        decide(0)
-        phase1(1)
-        decide(1)
-        phase1(2)
-        decide(2)
-        phase2(0)
-        post(0)
-        phase2(1)
-        post(1)
-        if t == 1:
-            for x in range(4):
-                dma(S("info", 3072, 3328, part=slice(x, 128, 16)), R("zi", min(x, 2), slice(KB, NC)), eng="s", tag="n")
-            act(S("info", 8 + B, 8 + B + P), IND(S("info", 3072, 3328), R("prm")))
-            ops[-1]["tag"] = "i1"
+            rr = lambda h: ps(3, 128 * h, 128 * h + n)
+            mm([(rr(0), na, M(ID, n)), (rr(0), M(IN), PL(0)), (rr(1), nz, M(ID, n)), (rr(1), M(IN), PL(1))])
+            ts(dk(k, n), ps(sc, 0, 128, n=n), 1407.5, A.is_lt, EPS, A.add)
+            mm([(cd, dk(k, n), M(N8192, n))], start=False)
+            act(S("cod", c0, c1), cd, bias=-639.0)
             for h in range(2):
+                ne = S(En, 192 * h + c0, 192 * h + c1)
+                tt(ne, rr(h), S(E, 192 * h + c0, 192 * h + c1), A.max)
+                if t == 0:
+                    cp(EU(h, c0, c1), ne)
+
+        for k in range(len(chunks)):
+            phase1(k)
+            decide(k)
+        for k in range(len(chunks)):
+            phase2(k)
+            post(k)
+
+        dma(S("info", 8, 8 + B, part=slice(0, 128, 16)), S("cod", 0, KB), tag="i%d" % t)
+        if t == 0:
+            own_cells(1)
+            cell_preload(1)
+            old_live(UO)
+        else:
+            mm([(ps(0, r, P, 16), R("wt", r), S("cod", KB, NC)) for r in range(16)])
+            act(S("info", 8 + B, 8 + B + P), ps(0, 0, P))
+            ops[-1]["tag"] = "i1"
+            dma(T.yy[:, 0:B], R("yo"))
+            ops[-1]["rd"].append(S("info", 16, 32)[1:4])
+            for h in range(2):
+                dma(T.ye[h::2, 0:B], S("e2", 192 * h, 192 * h + KB), eng="sa"[h])
                 cp(S("tr", 16 * h, 16 * h + 16), S("e2", 192 * h + KB, 192 * h + NC))
             op("v", lambda e: e.transpose(T.trt[:], T.tr[:]), 100, [R("tr")], [R("trt")])
             for a in range(4):
                 for gp in range(2):
                     dma(T.ye[4 * a + 2 * gp:4 * a + 2 * gp + 2, B:B + P], S("trt", 16 * gp, 16 * gp + 16, part=slice(32 * a, 32 * a + 32)))
-        if t == 0:
-            for k, (a, b) in enumerate(((0, 512), (512, V))):
-                mm([(ps(k), ID, S("win", LO + a, LO + b)), (ps(k), ID, S("yn", a, b)), (ps(k), NI, S("d2", a, b))])
-                act(S("xb", a, b), ps(k), F.Relu, bias=-3.0)
-            mm([(ps(2, 0, P), ID, R("hd")), (ps(2, 0, P), ID, S("yn", 0, P)), (ps(2, 0, P), NI, S("d2", 0, P)), (ps(2, 0, P), ID, R("inv"))])
-            act(S("xb", V, V + P), ps(2, 0, P), F.Relu, bias=-3.0)
-            ts(R("xb"), R("xb"), 63.0, A.min)
-            cell_sums(1)
-            mm([(ps(5, 0, P), ONES, R("wd"))])
-            ts(R("pn"), ps(5, 0, P), 175.5, A.is_lt, -1024.0, A.mult)
-        phase2(2)
-        post(2)
-        if t == 0:
-            own_cells(1)
-            cell_preload(1)
-            old_live()
-
-        for x in range(4):
-            dma(S("info", 8, 8 + B, part=slice(x, 128, 16)), R("zi", min(x, 2), slice(0, KB)), eng="sasa"[x], tag="i%d" % t)
-        if t == 1:
-            dma(T.yy[:, 0:B], R("yo"))
-            ops[-1]["rd"].append(S("info", 16, 32)[1:4])
-            for h in range(2):
-                dma(T.ye[h::2, 0:B], S("e2", 192 * h, 192 * h + KB))
-                ops[-1]["rd"].append(S("info", 16, 32)[1:4])
-        iw = S("info", 0, 3040)
-        for k in range(4):
-            for u in (2 * k, 2 * k + 1):
-                (cp if u in (1, 3, 5) else act)(S("gs", 512 * u, 512 * u + 512), IND(iw, S("dvu", 32 * u, 32 * u + 32)))
-            pk = 6 + k % 2
-            oo = ps(pk, 0, 64)
-            i_ = S("ii", 64 * k, 64 * k + 64)
-            mm([(oo, NI, i_), (oo, N2048, i_)] + [(oo, W(WS, s), S("gs", 1024 * k + s, 1024 * k + 1024, 16)) for s in range(16)])
-            sl = lambda nm, b0=0: S(nm, b0 + 64 * k, b0 + 64 * k + 64)
-            ts(sl("s1"), oo, MAG * 2048, A.add, -MAG * 2048, A.add)
-            ts(sl("em", P), oo, 3.0 * 2 ** 20, A.is_gt)
-            tt(ps(pk, 128, 192), oo, sl("s1"), A.is_equal)
-            ts(sl("s2"), sl("s1"), 0.0, A.is_equal)
-            tt(sl("em"), ps(pk, 128, 192), sl("s2"), A.max)
-        mv, dead = S("em", 0, P), S("em", P, 2 * P)
-        if t == 0:
-            g2, g3 = ps(6, 0, P), ps(6, P, 2 * P)
-            mm([(g2, ID, R("pn")), (g2, ONES, dead), (g2, ONES, mv)])
-            mm([(g3, NI, R("pn")), (g3, ONES, S("ones", 0, P)), (g3, NON, mv)])
-            op("a", lambda e: e.activation(T.tt[:], T.ps6[:], F.Sign, bias=-0.5, accum_out=col(16)[0]), 700, [ps(6)], [R("tt"), col(16)])
-
-        def slot_tail(t=t, n0=n0, mv=mv, dead=dead):
-            b0, b1, b2, b3 = (6, 7, 6, 7) if t == 0 else (0, 1, 2, 3)
-            gg = ps(b0, 0, P)
-            mm([(gg, ID, R("inv")), (gg, ONES, dead), (gg, ON17, mv)])
-            act(R("s1"), gg, F.Abs, bias=-136.0)
-            ts(R("made"), R("s1"), 135.5, A.is_lt)
-            sv, sn_ = ps(b1, 0, P), ps(b1, P, 2 * P)
-            mm([(sv, ID, S("ones", 0, P)), (sv, NI, mv), (sv, NI, dead)])
-            mm([(sn_, ID, mv)])
-            tt(S("tt", 0, P), sv, R("dvs"), A.mult)
-            tt(S("tt", P, 2 * P), sn_, R("dvs"), A.mult)
-            fv, fn = ps(b2, P, 2 * P), ps(b3, 0, P)
-            mm([(fv, R("idf"), R("nbc")), (fv, TF, mv), (fv, TF, dead)], stop=False)
-            mm([(fv, IBIG, R("made"))], start=False)
-            mm([(fn, R("idf"), R("nbc")), (fn, TF, S("ones", 0, P)), (fn, NTF, mv)], stop=False)
-            mm([(fn, IBIG, R("made"))], start=False)
-            tt(R("s2"), fv, S("tt", 0, P), A.max)
-            ynew = S("win", Y1 + B, Y1 + B + P) if t == 0 else S("yon", P, 2 * P)
+        iw = R("info")
+        EM = lambda x, a, b: R("em", x, slice(a, b))
+        for h in range(2):
+            a, b = 128 * h, 128 * h + 128
+            oo = ps(6 + h, 0, 128)
+            mm([(oo, M(NI), S("ii", a, b))], stop=False)
+            for k in (2 * h, 2 * h + 1):
+                for u in (2 * k, 2 * k + 1):
+                    (cp if u in GSV else act)(S("gs", 512 * u, 512 * u + 512), IND(iw, S("dvu", 32 * u, 32 * u + 32)))
+                mm([(ps(6 + h, 64 * (k % 2), 64 * (k % 2) + 64), W(WS, s), S("gs", 1024 * k + s, 1024 * k + 1024, 16)) for s in range(16)],
+                   start=False, stop=k % 2 == 1)
+            ts(EM(0, a, b), oo, 0.0, A.is_equal)
+            ts(EM(1, a, b), oo, 256.5, A.is_gt)
+            ts(EM(2, a, b), oo, -2000.0, A.is_lt)
             if t == 0:
-                tt(ynew, R("made"), R("wd"), A.mult)
-                tt(S("bl", n0, n0 + P), fn, S("tt", P, 2 * P), A.max)
-                cp(IND(R("bl"), R("dlu")), R("s2"))
-                mm([(ps(7, 0, 16), W(P8, r), S("win", Y1 + B + r, Y1 + B + P, 16)) for r in range(16)])
-                ts(S("lv", KB, KB + 16), ps(7, 0, 16), 1407.5, A.is_gt)
+                g2, g3 = ps(6 + h, 128, 256), ps(6 + h, 256, 384)
+                mm([(g2, M(ID), S("pn", a, b)), (g3, M(NI), S("pn", a, b)), (g3, M(ONES), S("ones", 0, 128))], stop=False)
+                mm([(g2, M(ONES), EM(0, a, b)), (g3, M(NON), EM(0, a, b)), (g2, M(ONES), EM(1, a, b)), (g3, M(NON), EM(1, a, b)),
+                    (g2, M(ONES), EM(2, a, b))], start=False)
+                act(S("tt", 0, 256), ps(6 + h, 128, 384), F.Sign, bias=-0.5, acc=col(22 + h))
+                ts(TH if h else UO, col(22 + h), -4.0, A.mult, UO, A.add)
+
+        def slot_tail(t=t, n0=n0):
+            w = P // HALVES[t]
+            for a in range(0, P, w):
+                b = a + w
+                bv, bn, bg = (3, 4, 6) if t == 0 else (a // w, 2 + a // w, 4 + a // w)
+                e0, e1, e2, on = EM(0, a, b), EM(1, a, b), EM(2, a, b), S("ones", 0, w)
+                f, fk = ps(bv, 0, w), ps(bv, w, 2 * w)
+                mm([(f, M(CV), S("inv", a, b)), (fk, M(K8), on)], stop=False)
+                mm([(f, M(A1), e0), (fk, M(N8192), e0), (f, M(A1), e1), (fk, M(N8192), e1), (f, M(A3), e2), (fk, M(N8192), e2)], start=False)
+                tt(R("fv", slice(None), slice(a, b)), ps(bv, 0, 2 * w), R("nd", slice(None), slice(a, b)), A.min)
+                tt(IND(R("bl"), S("dlu", a // 16, b // 16)), R("fv", 0, slice(a, b)), R("fv", 1, slice(a, b)), A.max)
+                f, fk = ps(bn, 0, w), ps(bn, w, 2 * w)
+                mm([(f, M(CV), S("inv", a, b)), (f, M(A1), on), (fk, M(NI), on)], stop=False)
+                mm([(f, M(NA1), e0), (fk, M(P8192), e0), (f, M(NA1), e1), (fk, M(P8192), e1), (f, M(O8192), e2)], start=False)
+                tt(R("fn", slice(None), slice(a, b)), ps(bn, 0, 2 * w), R("nd", slice(None), slice(a, b)), A.min)
+                tt(S("bl", n0 + a, n0 + b) if t == 0 else S("tv", a, b), R("fn", 0, slice(a, b)), R("fn", 1, slice(a, b)), A.max)
+                gg = ps(bg, 0, w)
+                mm([(gg, M(N8192), S("inv", a, b)), (gg, M(ON17), e0), (gg, M(ON17), e1), (gg, M(ONES), e2)])
+                act(S("s1", a, b), gg, F.Abs, bias=-72.0)
+                if t == 0:
+                    ts(S("made", a, b), S("s1", a, b), 135.5, A.is_lt)
+                    tt(S("win", Y1 + B + a, Y1 + B + b), S("made", a, b), S("wd", a, b), A.mult)
+                else:
+                    ts(gg, S("s1", a, b), 135.5, A.is_lt)
+                    tt(S("yon", ZB + P + a, ZB + P + b), gg, S("wd", a, b), A.mult)
+                    tt(S("tt", a, b), gg, S("dlw", a, b), A.mult)
+                    tt(S("tt", P + a, P + b), gg, S("s2", a, b), A.mult)
+            if t == 0:
+                c0, n = CUT[-1], KB + 16 - CUT[-1]
+                mm([(ps(7, r, 128, 16, n=n), S("win", Y1 + 16 * c0 + r, WEND, 16), S("st", 0, 8)) for r in range(16)])
+                ts(dk(len(CUT), n), ps(7, 0, 128, n=n), 1407.5, A.is_lt, EPS, A.add)
                 mm([(ps(6, 0, 16), W(P8, r), S("made", r, P, 16)) for r in range(16)])
                 ts(R("mw"), ps(6, 0, 16), 1 / 128, A.mult)
                 for h, src in ((0, "dl"), (1, "nw")):
                     tt(S("e1", 192 * h + KB, 192 * h + KB + 16), R("mw"), R(src), A.mult)
-                    cp(S("eu", 192 * h + KB, 192 * h + KB + 16), S("e1", 192 * h + KB, 192 * h + KB + 16))
+                    cp(R("eu", h, slice(KB, KB + 16)), S("e1", 192 * h + KB, 192 * h + KB + 16))
             else:
-                ts(IND(S("ylo", 0, C), R("dlu")), R("s2"), 1.0, A.mult, -1.0, A.add)
-                dma(T.yl[:, 0:n0], S("ylo", 0, n0), lat=3000.0)
-                tt(R("s1"), fn, S("tt", P, 2 * P), A.max)
-                act(R("tv"), R("s1"), bias=-1.0)
+                dma(T.yl[:, 0:n0], S("bl", 0, n0), lat=3000.0)
                 dma(T.yl[:, n0:C], R("tv"), eng="a")
-                tt(ynew, R("made"), R("wd"), A.mult)
-                dma(T.yy[:, B:B + 2 * P], R("yon"), eng="a")
-                tt(S("tt", 0, P), R("made"), S("dlw", 0, P), A.mult)
-                act(R("dvs"), R("xi"), bias=float(n0))
-                tt(S("tt", P, 2 * P), R("made"), R("dvs"), A.mult)
+                dma(T.yy[:, B:B + 2 * P], S("yon", ZB, ZB + 2 * P), eng="a")
                 for h in range(2):
                     dma(T.ye[h::2, B + P:B + 2 * P], S("tt", P * h, P * h + P, part=slice(0, 128, 16)), eng="a")
+        if t == 1:
+            act(R("s2"), R("xi"), bias=float(n0))
         late.append(slot_tail)
     late[1]()
 

@@ -5,7 +5,9 @@ from concourse.mybir import AluOpType as A, AxisListType as AX, ActivationFuncti
 V, B, P, C, GH = 1024, 2768, 256, 1536, 336
 THETA, DELTA = (465, 580), (7, 9)
 CW = C + GH
-LO, HZ, HA, Y0, Y1, WEND = 16, 16 + CW, 16 + 2 * CW, 16 + 3 * CW, 16 + 3 * CW + B, 16 + 3 * CW + B + B + P
+LO, HZ, HA = 16, 16 + CW, 16 + 4992
+XA, YN, Y0 = HZ, HA + C - B, HA + CW
+Y1, WEND = Y0 + B, Y0 + B + B + P
 KB = 173
 MAG = 1.5 * 2 ** 23
 CUT = (0, 128)
@@ -15,46 +17,66 @@ NB = 16 * (KB + 16)
 
 bf, f4, i4, u2 = "bfloat16", "float32", "int32", "uint16"
 SB = {
-    "win": ([WEND], bf), "lw": ([2 * CW], bf), "hif": ([C], bf), "lof": ([1280], bf), "yn": ([B], bf), "xa": ([V], bf), "xb": ([1280], bf),
+    "win": ([WEND], bf), "lw": ([2 * CW], bf), "ax": ([1280], bf), "xb": ([1280], bf), "wb": ([2], bf),
     "yo": ([16, KB], bf), "yon": ([ZB + 512], bf), "bli": ([V], i4), "bl": ([C], f4),
     "eni": ([2 * KB], i4), "e0": ([384], f4), "e1": ([384], f4), "e2": ([384], f4), "eu": ([2, 192], u2), "ofs": ([384], u2),
-    "far": ([2, 192], bf), "ppl": ([2, 192], bf), "cod": ([192], bf),
+    "cod": ([192], bf),
     "sni": ([24], i4), "snf": ([144], f4), "snu": ([72], u2), "mk": ([GH], f4), "gm": ([GH], f4), "ow": ([72], u2), "owt": ([136], f4),
-    "sb0": ([GH], bf), "sb1": ([GH], bf), "land0": ([GH], bf), "land1": ([GH], bf), "fhi": ([GH], bf), "flo": ([GH], bf),
+    "sb0": ([GH], bf), "sb1": ([GH], bf), "land0": ([GH], bf), "land1": ([GH], bf), "flo": ([GH], bf),
     "sx0": ([GH], bf), "sx1": ([GH], bf), "lx0": ([GH], bf), "lx1": ([GH], bf), "mk2": ([GH], bf),
-    "tu": ([NB], bf), "t00": ([NB], bf), "t01": ([NB], bf), "wa": ([NB], bf),
+    "tu": ([NB + 16], bf), "t00": ([NB], bf), "t01": ([NB], bf), "wa": ([NB], bf),
     "r00": ([NB], bf), "r01": ([NB], bf), "r10": ([NB], bf), "r11": ([NB], bf),
-    "dkt": ([len(CUT) + 1, 128], bf), "rr": ([256], f4), "ppt": ([256], bf), "ut": ([128], bf), "nnt": ([256], bf), "oa": ([128], f4),
-    "info": ([3040], bf), "gs": ([4096], bf), "jb": ([192], f4), "jb1": ([192], f4), "jc": ([32], f4), "dlw": ([P], f4),
-    "cs": ([28], f4), "ci": ([8], i4), "cand": ([80], bf), "cum": ([80], bf), "inc": ([80], f4), "dv": ([80], bf), "dv1": ([80], f4), "dv2": ([80], f4),
+    "dkt": ([len(CUT) + 1, 128], bf), "rr": ([256], f4), "ppt": ([len(CUT), 256], bf), "ut": ([128], bf), "nnt": ([256], bf), "oa": ([128], f4),
+    "gs": ([4096], bf), "jb": ([192], f4), "jb1": ([192], f4), "dlw": ([P], f4),
+    "cs": ([32], f4), "ci": ([8], i4), "cand": ([80], bf), "cum": ([80], bf), "dvb": ([80], bf), "dv": ([80], bf), "dv1": ([80], f4), "dv2": ([80], f4),
     "sou": ([32], u2), "dl": ([16], f4), "dlu": ([16], u2), "mw": ([16], f4), "nw": ([16], f4),
-    "hd": ([P], bf), "wd": ([P], bf), "bta": ([P], bf), "btz": ([P], bf), "inv": ([P], bf), "nd": ([2, P], f4), "dvu": ([P], u2),
+    "hd": ([P], bf), "wd": ([P], bf), "bta": ([P], bf), "btz": ([P], bf), "inv": ([2, P], bf), "nd": ([2, P], f4), "dvu": ([P], u2),
     "s1": ([P], f4), "s2": ([P], f4), "tt": ([512], f4), "tv": ([P], f4), "em": ([3, P], bf), "made": ([P], bf), "ii": ([P], bf),
     "fv": ([2, P], f4), "fn": ([2, P], f4),
     "prf": ([16], f4), "tr": ([32], f4), "trt": ([32], f4), "d2": ([V], bf),
-    "xi": ([256], f4), "gi": ([128], f4), "wt": ([16, 128], bf), "bm": ([2, 144], bf), "bmf": ([144], f4), "idf": ([128], f4),
-    "xs": ([80], f4), "pn": ([P], bf), "mt": ([28, 128], bf), "st": ([64], bf), "sw": ([32], bf),
+    "xi": ([256], f4), "gi": ([128], f4), "wt": ([16, 128], bf), "bm": ([3, 144], bf), "idf": ([128], f4),
+    "xs": ([80], f4), "pn": ([P], bf), "mt": ([29, 128], bf), "um": ([P], bf), "c768": ([P], bf), "st": ([104], bf), "sw": ([32], bf), "sk": ([4, 8], bf), "g8": ([104], f4), "ex": ([P], bf),
     "tin": ([5, 2, 16], bf), "tin2": ([32], bf), "tct": ([160], bf), "tbt": ([32], bf), "ca": ([P], bf), "cb": ([P], bf), "cc": ([P], bf),
-    "ib": ([P], bf), "obf": ([16], f4), "tb": ([16], f4), "pw": ([16], f4), "pw2": ([16], f4), "ones": ([2048], bf),
+    "ib": ([P], bf), "tb": ([16], f4), "pw": ([16], f4), "pw2": ([16], f4), "ones": ([1024], bf),
 }
 SCRATCH = {k: ("sbuf", [128] + s, d) for k, (s, d) in SB.items()}
-for _k in range(8):
+for _k in range(4, 8):
     SCRATCH["ps%d" % _k] = ("psum", [128, 512], "float32")
+for _k in (0, 2):
+    SCRATCH["ps%d" % _k] = ("psum", [128, 1024], "float32")
 NDMA = 48
 SEMAPHORES = ["qv", "qa", "qp", "qg", "arr0", "arr1", "out0", "out1", "arr2", "arr3", "out2", "out3"] + ["d%d" % k for k in range(NDMA)]
 HOP = 200.0
-TRIES = 2200
+TRIES = 100
 PLANS = {}
-CASES = ((-0.5, -2.0, 0.0, 1.0, 300.0, 1.4), (0.45, 2.0, -20.0, 1.0, 100.0, 0.8), (0.0, 0.0, 30.0, 1.2, 250.0, 1.3))
-PLAIN = ((0, 1), (0, 1))
+DBG = {}
+MOVES = 100000
+STARTS = 1
+FAR = 8
+TTG = 1.6
+CASES = ((1.0, 1.0, 1.3, 3.0, 30.0, 70.0, 0.45, 170.0, 1.0, 1.0, 0.0), (1.0, 1.0, 1.1, 1.8, 30.0, 70.0, 0.5, 300.0, 1.4, 1.4, 1500.0),
+         (1.0, 1.0, 2.05, 5.8, 10.0, 50.0, 0.5, 100.0, 0.8, 0.8, -1500.0), (1.0, 1.0, 1.4, 3.8, 60.0, 100.0, 0.75, 250.0, 1.2, 1.2, 0.0))
+PLAIN = ((4, 5), (4, 5))
 RV00 = ((0, 0), (0, 0))
 RV01 = ((0, 0), (0, 0))
 RVAH = ((0, 0), (0, 0))
 GU = (32, 64, 64, 32)
-GSV = (1, 3, 5)
-WEAVE = 2
+GSV = ((1, 3, 5), (1, 3, 5))
+PIECES = ((0, 128), (128, 192), (192, 256))
+AW = 64
+PW = 32
+PSX = 0.0
+TEMP = 300.0
+LOV = (0, 0)
+LWV = ((0, 1), (0, 1))
+FIRST = 1500.0
+WEAVE = 3
 BOOST = 4000.0
-HALVES = (1, 2)
+TAILS = (((0, 256),), ((0, 128), (128, 256)))
+WG = ()
+ORD1 = ((0, 1), (0, 1))
+ORD2 = ((0, 1), (0, 1))
+HHA = ((), ())
 
 
 def rank_program(g, core, T, topo):
@@ -94,7 +116,7 @@ def rank_program(g, core, T, topo):
                     "ng": sum(x[4] for x in rd if len(x) > 6), "ns": sum(x[4] for x in wr if len(x) > 6),
                     "tr": [x[1:4] for x in rd], "tw": [x[1:4] for x in wr],
                     "rd": [x[1:4] for x in rd],
-                    "wr": [x[1:4] for x in wr] + [("bank" + x[1], 0, 1) for x in rd + wr if x[1].startswith("ps")]})
+                    "wr": [x[1:4] for x in wr] + [("bank" + x[1], x[2] // 512, (x[3] - 1) // 512 + 1) for x in rd + wr if x[1].startswith("ps")]})
 
     def ap(x):
         return x[0] if isinstance(x, tuple) else x
@@ -103,7 +125,7 @@ def rank_program(g, core, T, topo):
         if len(o) > 6:
             return 60 + 3.8 * o[4]
         if len(i) > 6:
-            return 60 + 1.6 * o[4]
+            return 60 + (TTG if two else 1.6) * o[4]
         return 30 + max(64, o[4] * (2 if two else 0.5 if o[5] == 2 and i[5] == 2 else 1))
 
     def ts(o, i, s1, o0, s2=None, o1=None):
@@ -145,27 +167,29 @@ def rank_program(g, core, T, topo):
             op("g", lambda e: e.iota(o[0], pat, base, cm), 150 + 2 * o[4], [], [o])
 
     def dma(o, i, eng="s", lat=2200.0, tag=None):
-        w = [(o[0], o[1], o[2] - 8, o[3] + 8)] if isinstance(o, tuple) else []
+        w = [(o[0], o[1], o[2] * o[5] // 16 * 16 // o[5], -(-o[3] * o[5] // 16) * 16 // o[5])] if isinstance(o, tuple) else []
         op(eng, lambda e: e.dma_start(ap(o), ap(i)), 80, [i], w, lat=lat, kind="d")
         ops[-1]["tag"] = tag
 
-    (ID, NI, I255, I8, NI8, NIH, IA, IZ, IN0, IN1, IK2, IK3, ONES, TRI, A1, NA1, O8192, A3, CV, N8192, P8192, K8, ON17, ON16, NON,
-     N255, KD) = range(27)
+    (ID, NI, I255, IBIG, ON128, NIH, IA, IZ, IN0, IN1, IK2, IK3, ONES, TRI, A1, NA1, O8192, A3, CV, N8192, P8192, K8, ON17, ON16, NON,
+     N255, KD, ON80, IH) = range(29)
 
     def M(k, n=128, m=None):
         return R("mt", k, slice(0, n if m is None else m), part=slice(0, n))
 
     def W(kind, r):
-        if kind == "f":
-            return S("bmf", 15 - r, 143 - r)
         return R("bm", kind, slice(15 - r, 143 - r))
-    P8, WS = 0, 1
+    P8, WS, W256 = 0, 1, 2
+    G8 = S("st", 0, 8)
 
     def col(k):
         return S("cs", k, k + 1)
     PC, FC, GC, G15, PWC, RC, MA, MZ, WSC, TH, UO = [col(k) for k in range(11)]
+    WB = S("wb", 0, 1)
 
     def ps(k, a=0, b=512, st=1, n=None):
+        if k in (1, 3):
+            k, a, b = k - 1, a + 512, b + 512
         return S("ps%d" % k, a, b, st, part=None if n is None else slice(0, n))
 
     def chunks_of(t):
@@ -175,17 +199,27 @@ def rank_program(g, core, T, topo):
         return R("dkt", k, part=slice(0, n))
 
     for h in range(2):
-        dma(S("eni", KB * h, KB * h + KB), T.en0[h::2, :], eng="sa"[h], lat=2600.0, tag="e")
+        dma(S("eni", KB * h, KB * h + KB), T.en0[h::2, :], eng="sa"[h], lat=2500.0, tag="e")
+        ops[-1]["lead"] = 9000.0
     dma(S("sni", 0, 21), T.snd[:, :], lat=2400.0)
-    dma(S("yn", 0, B // 2), T.y0[:, 0:B // 2], lat=3000.0, tag="y")
-    dma(S("yn", B // 2, B), T.y0[:, B // 2:B], eng="a", lat=3400.0, tag="y")
-    dma(R("xa"), T.x0[:, :], lat=3600.0)
+    ops[-1]["lead"] = 9000.0
+    yn = lambda a, b: S("win", YN + a, YN + b)
+    XS = lambda t, a, b: S("win", XA + a, XA + b) if t == 0 else S("xb", a, b)
+    dma(yn(0, B // 2), T.y0[:, 0:B // 2], lat=3000.0, tag="y")
+    dma(yn(B // 2, B), T.y0[:, B // 2:B], eng="a", lat=3400.0, tag="y")
+    dma(XS(0, 0, V), T.x0[:, :], lat=3600.0)
+    for k, j in ((2, 0), (3, 2), (4, 1), (5, 3)):
+        ops[k]["after"] = [j]
 
     iota(R("xi"), [[1, 256]], 0, 0)
     iota(S("ci", 0, 1), [[0, 1]], 0, 1, small=False)
     iota(R("gi"), [[1, 8], [0, 16]], 0, 0)
+    iota(R("g8"), [[0, 13], [1, 8]], 0, 0)
     ms(R("ones"), 1.0)
-    op("g", lambda e: e.affine_select(T.wt[:], T.ones[:], [[-1, 16], [-16, 8], [0, 16]], A.is_equal, 0.0, 0, 1), 4300, [R("ones")], [R("wt")])
+    for h in (0, 8):
+        op("g", lambda e, h=h: e.affine_select(T.wt[:, h:h + 8], T.ones[:], [[-1, 8], [-16, 8], [0, 16]], A.is_equal, 0.0, -h, 1), 2250,
+           [R("ones")], [R("wt", slice(h, h + 8))])
+    iota(R("ib"), [[1, P]], 0, 0)
     cp(PC, S("ci", 0, 1))
     ts(S("ci", 1, 2), S("ci", 0, 1), 15, A.bitwise_and)
     ts(S("ci", 2, 3), S("ci", 0, 1), 4, A.arith_shift_right)
@@ -195,32 +229,28 @@ def rank_program(g, core, T, topo):
     ts(R("bm", P8), x144, G15, A.is_equal, 8.0, A.mult)
     ts(M(ONES), R("gi"), GC, A.is_equal)
     ts(M(ID), S("xi", 0, 128), PC, A.is_equal)
-    ts(M(TRI), S("xi", 0, 128), PC, A.is_gt)
-    tt(M(TRI), M(TRI), M(ONES), A.mult)
-    ts(R("bmf"), x144, G15, A.is_equal)
+    op("g", lambda e: e.affine_select(M(TRI)[0], M(ONES)[0], [[1, 128]], A.is_gt, 0.0, 0, -1), 430, [M(ONES)], [M(TRI)])
+    act(R("bm", W256), R("bm", P8), scale=32.0)
     ts(R("tb"), S("xi", 0, 16), FC, A.is_equal)
     ts(S("owt", 128, 136), x8, GC, A.is_equal)
-    ts(S("st", 0, 8), x8, GC, A.is_equal, 8.0, A.mult)
-    for k, c in ((1, 0.0), (2, 1.0), (3, 1.0), (4, 1.0), (5, -1.0), (6, -1.0), (7, -1.0)):
-        act(S("st", 8 * k, 8 * k + 8), S("st", 0, 8), scale=c)
+    ts(R("st"), R("g8"), GC, A.is_equal, 8.0, A.mult)
+    for a, b, c in ((1, 2, 0.0), (2, 3, -1.0), (4, 5, -1.0), (8, 11, -1.0), (11, 12, 0.0))[:5 if any(RV00[0] + RV00[1] + RV01[0] + RV01[1]) else 3]:
+        act(S("st", 8 * a, 8 * b), S("st", 8 * a, 8 * b), scale=c)
+    for k, c in enumerate((64.0, 80.0, 16.0, 1.0 / 16)):
+        act(R("sk", k), G8, scale=c)
     act(S("s2", 0, 192), S("xi", 0, 192), bias=FC, scale=16.0)
     act(R("nw"), S("s2", 0, 16), bias=float(V))
-    act(S("jc", 0, 16), S("s2", 0, 16), bias=4096.0, scale=16.0)
-    act(S("jc", 16, 32), S("s2", 0, 16), scale=16.0)
-    ts(col(18), FC, 14.5, A.is_gt, 4096.0, A.mult)
+    ts(col(18), FC, 14.5, A.is_lt)
     ts(S("ci", 3, 4), S("ci", 0, 1), 16, A.bitwise_and)
     cp(col(19), S("ci", 3, 4))
     ms(R("tin2"), 512.0)
-    act(R("ib"), R("xi"))
     act(R("jb1"), S("s2", 0, 192), bias=float(Y1 - LO))
     act(R("jb"), S("s2", 0, 192), bias=float(Y0 - LO))
-    for m, c in ((NI, -1.0), (I255, 255 / 512), (N255, -255 / 512), (I8, 0.125), (NI8, -0.125), (NIH, -0.5), (IA, 2.0 * CW), (IZ, 1.0 * CW),
-                 (IN0, 2.0), (IN1, 2.5), (IK2, -16384.0), (IK3, -24576.0), (N8192, -8192.0), (P8192, 8192.0), (CV, -33.0 * 2 ** 19)):
-        if m != N255 or any(RVAH[0] + RVAH[1]):
-            act(M(m), M(ID), scale=c)
+    act(M(NIH), M(ID), scale=-0.5)
+    act(M(IH), M(ID), scale=0.5)
     act(M(K8), M(ID), scale=-1.0, bias=64.0)
     act(R("idf"), M(ID))
-    for m, c in ((O8192, 8192.0), (ON16, 16.0), (ON17, 17.0), (NON, -1.0)):
+    for m, c in ((O8192, 8192.0), (ON16, 16.0), (ON17, 17.0), (NON, -1.0), (ON128, -128.0), (ON80, 80.0)):
         act(M(m), M(ONES), scale=c)
     tt(M(A3), M(ID), M(TRI), A.subtract)
     act(M(A3), M(A3), scale=262144.0)
@@ -247,11 +277,10 @@ def rank_program(g, core, T, topo):
     act(R("bta"), R("made"), scale=MA)
     act(R("btz"), R("made"), scale=MZ)
     ts(R("bm", WS), x144, G15, A.is_equal, S("tb", 0, 1), A.mult)
-    act(R("ii"), R("xi"), bias=-128.0)
     ms(S("win", 0, 16), 0.0)
-    for a, b in ((V, C), (CW + V, CW + C)):
-        ms(S("lw", a, b), 0.0)
-    ms(R("far"), 0.0)
+    ms(S("lw", V, V + 128), 0.0)
+    for k in range(4):
+        act(col(24 + k), (MA, MZ)[k % 2], scale=-1.0, bias=float(DELTA[k // 2]))
     ms(S("e1", KB, 192), 0.0)
     ms(S("e1", 192 + KB, 384), 0.0)
 
@@ -259,11 +288,9 @@ def rank_program(g, core, T, topo):
     nlow = 3 * (N - 1 - q)
     ts(sn(4), S("xi", 0, 21), nlow - 0.5, A.is_gt, float(KB), A.mult)
     ts(sn(5), S("xi", 0, 21), nlow - 0.5, A.is_gt, 192.0 - KB, A.mult)
-    ts(sn(0), S("sni", 0, 21), 1.0 / KB, A.mult, -0.5 + 0.5 / KB, A.add)
-    ts(sn(1), sn(0), MAG, A.add, -MAG, A.add)
-    cp(S("snu", 24, 45), sn(1))
+    ts(S("snu", 24, 45), S("sni", 0, 21), 1.0 / KB, A.mult, -0.5 + 0.5 / KB, A.add)
     tt(sn(4), sn(4), S("sni", 0, 21), A.add)
-    ts(sn(2), sn(1), -float(KB), A.mult)
+    ts(sn(2), S("snu", 24, 45), -float(KB), A.mult)
     tt(sn(2), sn(2), sn(4), A.add)
     cp(S("snu", 0, 21), sn(2))
     tt(sn(5), sn(5), sn(2), A.add)
@@ -272,20 +299,22 @@ def rank_program(g, core, T, topo):
     for k, (c0, c1) in enumerate(chunks_of(0)):
         n = c1 - c0
         pb = (7, 5)[k % 2]
-        mm([(ps(pb, r, 128, 16, n=n), S("yn", KB * r + c0, KB * r + c1), S("st", 0, 8)) for r in range(16)])
+        mm([(ps(pb, r, 128, 16, n=n), yn(KB * r + c0, KB * r + c1), G8) for r in range(16)])
         ts(dk(k, n), ps(pb, 0, 128, n=n), 1407.5, A.is_lt, EPS, A.add)
     for h in range(2):
         cp(S("e0", 192 * h, 192 * h + KB), S("eni", KB * h, KB * h + KB))
     cp(R("eu", slice(None), slice(0, KB)), R("eni"))
-    ts(R("far", slice(None), slice(0, KB)), R("eni"), C - 0.5, A.is_gt)
     dma(R("bli"), T.bl0[:, :], lat=3000.0)
     ops[-1]["rd"].append(dk(0, 1)[1:4])
     for r in range(16):
-        o, i = S("win", Y0 + r, Y0 + B, 16), S("yn", KB * r, KB * r + KB)
-        (cp if r % WEAVE == 1 else act)(o, i)
+        o, i = S("win", Y0 + r, Y0 + B, 16), yn(KB * r, KB * r + KB)
+        if r in WG:
+            op("g", lambda e, o=o, i=i: e.affine_select(o[0], i[0], [[0, KB]], A.is_ge, 0.0, 0, 0), 520, [i], [o])
+        else:
+            (cp if r % WEAVE == 1 else act)(o, i)
         ops[-1]["tag"] = "weave"
     cp(S("bl", 0, V), R("bli"))
-    ts(R("d2"), S("yn", 0, V), 1028.5, A.add)
+    ts(R("d2"), yn(0, V), 1028.5, A.add)
 
     def own_cells(t):
         tt(R("gm"), IND(R("eni") if t == 0 else R("e1"), S("snu", 48 * t, 48 * t + 21)), R("mk"), A.mult)
@@ -296,18 +325,17 @@ def rank_program(g, core, T, topo):
         K = 64 + 16 * t
         own = ps(pb, 0, 21)
         cp(S("ow", 0, 21), own)
-        ts(sn(0), own, 1.0 / K, A.mult, -0.5 + 0.5 / K, A.add)
-        ts(sn(1), sn(0), MAG, A.add, -MAG, A.add)
-        cp(S("ow", 24, 45), sn(1))
-        ts(sn(2), sn(1), -float(K), A.mult)
+        ts(S("ow", 24, 45), own, 1.0 / K, A.mult, -0.5 + 0.5 / K, A.add)
+        ts(sn(2), S("ow", 24, 45), -float(K), A.mult)
         tt(sn(3), own, sn(2), A.add)
         cp(S("ow", 48, 69), sn(3))
         act(R("mk2"), IND(R("tb"), S("ow", 24, 45)))
-        act(R("sx%d" % t), IND(S("xa" if t == 0 else "xb", 0, V + P * t), S("ow", 0, 21)))
+        act(R("sx%d" % t), IND(XS(t, 0, V + P * t), S("ow", 0, 21)))
         send("sx%d" % t, "lx%d" % t, 2 + t)
         dl = float(DELTA[t])
-        ts(R("fhi"), R("lx%d" % t), dl, A.add, 63.0, A.min)
-        ts(R("flo"), R("lx%d" % t), -dl, A.add, 0.0, A.max)
+        for h, H in enumerate((HA, HZ)):
+            ts(S("win", H + C, H + CW), R("lx%d" % t), 63.0 - dl, A.min, col(24 + 2 * t + h), A.add)
+        act(R("flo"), R("lx%d" % t), F.Abs, bias=-31.5)
 
     def send(sb, land, k):
         def fn(e):
@@ -320,126 +348,152 @@ def rank_program(g, core, T, topo):
                 trs.append(RemoteDMATransfer(dst_ids=[DstId(rid=rid, pnc=pid)], dma_engine_mask=mask, remote_sem=T.sem["arr%d" % k],
                                              src=T[sb][:, 48 * (d - 1):48 * d], dst=T[land][:, 48 * (N - 1 - d):48 * (N - d)]))
             e.remote_dma_fused(trs, local_sem=T.sem["out%d" % k])
-        op("g", fn, 300, [R(sb)], [R(land)], lat=2500.0, kind="r%d" % k)
+        op("g", fn, 300 + FIRST * (k == 2), [R(sb)], [R(land)], lat=2500.0, kind="r%d" % k)
 
     def banks_of(t):
         rb = 8 if t == 0 else 6
         return [(r0, min(16, r0 + rb)) for r0 in range(0, 16, rb)]
 
     def cell_sums(t):
-        X, K, Ct, dl = "xa" if t == 0 else "xb", 64 + 16 * t, V + P * t, float(DELTA[t])
-        ts(S("hif", 0, Ct), S(X, 0, Ct), dl, A.add, 63.0, A.min)
-        ts(S("lof", 0, Ct), S(X, 0, Ct), -dl, A.add, 0.0, A.max)
+        K, Ct = 64 + 16 * t, V + P * t
+        act(S("ax", 0, Ct), XS(t, 0, Ct), F.Abs, bias=-31.5)
         pb = 6 + t
-        mm([(ps(pb, 0, K), W(P8, r), S(X, K * r, K * r + K)) for r in range(16)])
-        act(S("xs", 0, K), ps(pb, 0, K), bias=0.5 - 124.0 - 8.0 * THETA[t])
+        mm([(ps(pb, 0, K), W(P8, r), XS(t, K * r, K * r + K)) for r in range(16)])
+        if t == 0:
+            act(S("xs", 0, K), ps(pb, 0, K), scale=(1 - EPS) / 8, bias=(0.5 - 8.0 * THETA[0] - 4 * 8320.0) * (1 - EPS) / 8 - B)
+        else:
+            act(S("xs", 0, K), ps(pb, 0, K), bias=0.5 - 124.0 - 8.0 * THETA[1] - 4 * 8320.0)
 
-    def cell_preload(t):
-        X, K = "xa" if t == 0 else "xb", 64 + 16 * t
-        for k, (r0, r1) in enumerate(banks_of(t)):
+    def cell_preload(t, ks=(0, 1)):
+        K = 64 + 16 * t
+        for k in ks:
+            r0, r1 = banks_of(t)[k]
             w = (r1 - r0) * K
-            mm([(ps(k, 0, w), M(NIH), S(X, K * r0, K * r1))], stop=False)
-            mm([(ps(3 + k, 0, w), M(I8), S("hif", K * r0, K * r1)), (ps(3 + k, 0, w), M(NI8), S("lof", K * r0, K * r1))], stop=False)
+            mm([(ps(k, 0, w), M(NIH), XS(t, K * r0, K * r1))], stop=False)
+            mm([(ps(3 + k, 0, w), M(IH), S("ax", K * r0, K * r1))], stop=False)
 
     def old_live(u):
         o = ps(7, 384, 512)
         mm([(o, M(ID), M(O8192))], stop=False)
         mm([(o, S("ones", 0, 128, part=slice(0, c1 - c0)), dk(k, c1 - c0)) for k, (c0, c1) in enumerate(chunks_of(0))], start=False)
         act(S("tt", 0, 128), o, F.Relu, bias=-8192.0, acc=col(15))
-        ts(u, col(15), 8.0 / (1 - EPS), A.mult, 124.0 - 8.0 * B / (1 - EPS), A.add)
+        if u is TH:
+            ts(WB, col(15), -2.0 / (1 - EPS), A.mult, 8320.0 - 31.0 + 2.0 * B / (1 - EPS), A.add)
+            ts(S("xs", 0, 64), S("xs", 0, 64), col(15), A.add, -2.0 / (1 - EPS), A.mult)
+        else:
+            ts(u, col(15), 8.0 / (1 - EPS), A.mult, 124.0 - 8.0 * B / (1 - EPS), A.add)
 
     own_cells(0)
     cell_sums(0)
     cell_preload(0)
     old_live(TH)
+    for m, c in ((NI, -1.0), (IBIG, 131072.0), (IK2, -16384.0), (N8192, -8192.0), (IK3, -24576.0), (IA, float(HA - LO)), (IZ, float(HZ - LO)), (I255, 255 / 512),
+                 (N255, -255 / 512), (IN0, float(V)), (IN1, float(V + P)), (KD, 255.0), (P8192, 8192.0), (CV, -33.0 * 2 ** 19)):
+        if m != N255 or any(RVAH[0] + RVAH[1]):
+            op("g", lambda e, m=m, c=c: e.affine_select(M(m)[0], T.lw[:, V:V + 128], [[-1, 128]], A.not_equal, c, 0, 1), 430,
+               [S("lw", V, V + 128), R("sx0")], [M(m)])
     late = []
     for t in range(2):
         Ct, K, NC = V + P * t, 64 + 16 * t, KB + 16 * t
         n0, dl = V + P * t, float(DELTA[t])
         E, En = "e%d" % t, "e%d" % (t + 1)
         YB = Y0 if t == 0 else Y1
-        ts(col(20), TH, MAG * 256, A.add, -MAG * 256, A.add)
-        ts(S("cand", 0, K), S("xs", 0, K), TH, A.add, col(20), A.is_gt)
+        ts(S("cand", 0, K), S("xs", 0, K), WB, A.is_lt)
         op("v", lambda e, K=K: e.tensor_tensor_scan(T.cum[:, 0:K], T.ones[:, 0:K], T.cand[:, 0:K], 0.0, A.mult, A.subtract), 100,
            [S("ones", 0, K), R("cand")], [R("cum")])
         ts(S("dv2", 0, K), S("cand", 0, K), -1024.0, A.mult, 767.5, A.add)
-        off = ps(7, 300, 301)
-        mm([(off, M(TRI), S("cum", K - 1, K))])
+        off, cnt = ps(7, 300, 301), ps(7, 301, 302)
+        mm([(off, M(TRI), S("cum", K - 1, K)), (cnt, M(NON), S("cum", K - 1, K))])
         tt(S("dv1", 0, K), S("dv2", 0, K), S("cum", 0, K), A.subtract)
         ts(S("dv", 0, K), S("dv1", 0, K), off, A.is_lt, dl / 2, A.mult)
         tt(R("sb%d" % t), IND(S("dv", 0, K), S("ow", 48, 69)), R("mk2"), A.mult)
         send("sb%d" % t, "land%d" % t, t)
+        ts(S("dvb", 0, K), S("dv1", 0, K), off, A.is_lt, -64 * dl, A.mult)
+        ts(S("cs", 28, 30), ps(7, 300, 302), -1.0, A.mult)
+
+        def low(o, p, on_v):
+            if on_v:
+                ts(o, p, -1.0, A.mult, 0.0, A.max)
+            else:
+                act(o, p, F.Relu, scale=-1.0)
+
+        def width(o, p, on_v):
+            if on_v:
+                ts(o, p, 64.5 * dl - 15.75, A.add, 0.0, A.max)
+            else:
+                act(o, p, F.Relu, bias=64.5 * dl - 15.75)
         for k, (r0, r1) in enumerate(banks_of(t)):
             w = (r1 - r0) * K
-            for kk_ in (k, 3 + k):
-                mm([(ps(kk_, K * (r - r0), K * (r - r0 + 1)), R("wt", r), S("dv", 0, K)) for r in range(r0, r1)], start=False)
-            ts(S("lw", K * r0, K * r1), ps(k, 0, w), -1.0, A.mult, 0.0, A.max)
-            act(S("lw", CW + K * r0, CW + K * r1), ps(3 + k, 0, w), F.Relu, bias=-2.0 * dl, scale=4.0)
+            for kk_, nm in ((k, "dv"), (3 + k, "dvb")):
+                mm([(ps(kk_, K * (r - r0), K * (r - r0 + 1)), R("wt", r), S(nm, 0, K)) for r in range(r0, r1)], start=False)
+            low(S("lw", K * r0, K * r1), ps(k, 0, w), False)
+            width(S("lw", CW + K * r0, CW + K * r1), ps(3 + k, 0, w), k in LWV[t])
         sb, land = "sb%d" % t, "land%d" % t
-        ts(S("inc", 0, K), S("cum", 0, K), off, A.add, -1.0, A.mult)
+        nk = K // 16
+        place = lambda o, i: act(o, i, scale=-1.0, bias=col(28))
+        for h in range(2):
+            place(R("tin", slice(0, nk), h), S("cum", 0, K))
+            place(S("tin2", 16 * h, 16 * h + nk - 1), S("cum", 15, K - 1, 16))
+        place(col(17), S("cum", K - 1, K))
+        act(R("ex"), R("ib"), F.Relu, bias=col(29))
+        ts(R("inv", t), R("ib"), cnt, A.is_ge, 2.0 ** -7, A.add)
         if t == 1:
             late[0]()
+            iota(S("lw", CW + Ct, CW + C), [[0, C - Ct]], DELTA[1], 0)
         f0, f1 = ps(2, 0, GH), ps(5, 0, GH)
         mm([(f0, M(NIH), R("lx%d" % t))], stop=False)
-        mm([(f1, M(I8), R("fhi")), (f1, M(NI8), R("flo"))], stop=False)
+        mm([(f1, M(IH), R("flo"))], stop=False)
         mm([(f0, M(ONES), R(land))], start=False)
-        mm([(f1, M(ONES), R(land))], start=False)
-        ts(S("lw", C, CW), f0, -1.0, A.mult, 0.0, A.max)
-        act(S("lw", CW + C, 2 * CW), f1, F.Relu, bias=-2.0 * dl, scale=4.0)
+        mm([(f1, M(ON128), R(land))], start=False)
+        low(S("lw", C, CW), f0, True)
+        width(S("lw", CW + C, 2 * CW), f1, False)
         if t == 0:
-            for nm, a, b, v in (("hif", V, C, 0), ("win", HA, HA + C, 0), ("win", HZ, HZ + C, 0), ("win", LO + V, LO + C, 0), ("bl", V, C, -1),
-                                ("info", 0, 3040, -8192), ("yon", 0, ZB, 0)):
-                iota(S(nm, a, b), [[0, b - a]], v, 0)
-                ops[-1]["rd"].append(R(land)[1:4])
-        ts(S("win", LO, LO + Ct), S("lw", 0, Ct), 2.0, A.mult)
-        ts(S("win", LO + C, LO + CW), S("lw", C, CW), 2.0, A.mult)
-        dma(S("win", HA + C, HA + CW), R("fhi"))
-        dma(S("win", HZ + C, HZ + CW), R("fhi"))
-        nk = K // 16
-        for h in range(2):
-            ts(R("tin", slice(0, nk), h), S("inc", 0, K), 256.0, A.min)
-            ts(S("tin2", 16 * h, 16 * h + nk - 1), S("inc", 15, K - 1, 16), 256.0, A.min)
+            for nm, a, b, st, v in (("lw", V + 128, C, 0, 0), ("lw", CW + V, CW + C, 0, DELTA[0]), ("win", LO + V, LO + C, 0, 0), ("win", HZ + V, HZ + C, 0, 0), ("bl", V, C, 0, -1), ("yon", 0, ZB, 0, 0),
+                                    ("tu", B, NB + 16, 0, 0), ("win", HZ + CW, YN, 0, 0), ("ii", 0, P, 1, -128),
+                                    ("c768", 0, 128, 0, -768), ("c768", 128, 256, 0, 768)):
+                iota(S(nm, a, b), [[st, b - a]], v, 0)
+                ops[-1]["rd"].append(R(sb)[1:4])
+        for a, b in ((0, Ct // 2), (Ct // 2, Ct), (C, CW)):
+            if LOV[t]:
+                ts(S("win", LO + a, LO + b), S("lw", a, b), 2.0, A.mult)
+            else:
+                act(S("win", LO + a, LO + b), S("lw", a, b), scale=2.0)
         op("v", lambda e, nk=nk: e.transpose(T.tct[:, 0:32 * nk], T.tin[:, 0:nk]), 30 + 16 * nk, [R("tin")], [R("tct")])
         op("v", lambda e: e.transpose(T.tbt[:], T.tin2[:]), 94, [R("tin2")], [R("tbt")])
-        ts(col(17), S("inc", K - 1, K), col(18), A.add)
-        ts(R("ca"), R("ib"), col(17), A.is_ge, float(K), A.mult)
-        pa_, pk_ = ps(7, 0, 16), ps(7, 16, 32)
+        ts(R("ca"), R("ib"), col(17), A.is_ge, col(18), A.mult)
+        pa_ = ps(7, 0, 16)
         mm([(pa_, W(P8, r), S("ca", r, P, 16)) for r in range(16)])
-        ts(R("obf"), pa_, 1.0 / (8 * K), A.mult, col(19), A.add)
-        cp(S("sou", 0, 16), R("obf"))
+        ts(S("sou", 0, 16), pa_, 0.125, A.mult, col(19), A.add)
+        mm([(pa_, W(P8, r), S("ca", r, P, 16)) for r in range(16)], stop=False)
         tt(R("cb"), IND(R("tbt"), S("sou", 0, 16)), R("ib"), A.is_le)
-        mm([(pk_, W(P8, r), S("cb", r, P, 16)) for r in range(16)])
-        ts(R("dl"), pk_, 4.0, A.mult)
-        tt(R("dl"), R("dl"), R("obf"), A.add)
-        cp(S("sou", 16, 32), R("dl"))
+        mm([(pa_, W(W256, r), S("cb", r, P, 16)) for r in range(16)], start=False)
+        ts(S("sou", 16, 32), pa_, 0.125, A.mult, col(19), A.add)
         tt(R("cc"), IND(S("tct", 0, 32 * nk), S("sou", 16, 32)), R("ib"), A.is_le)
-        mm([(ps(7, P, 2 * P), M(ONES), R("ca")), (ps(7, P, 2 * P), M(ON16), R("cb")), (ps(7, P, 2 * P), M(ONES), R("cc"))])
-        DL = R("dlw")
-        act(DL, ps(7, P, 2 * P))
-        mm([(ps(7, 0, 16), W("f", r), S("dlw", r, P, 16)) for r in range(16)])
-        ts(R("obf"), ps(7, 0, 16), 16.0 * Ct - 8, A.is_gt)
-        tt(R("obf"), R("obf"), S("jc", 16 * t, 16 * t + 16), A.mult)
-        tt(R("dl"), ps(7, 0, 16), R("obf"), A.add)
-        ts(R("dl"), R("dl"), 1 / 16, A.mult)
-        cp(R("dlu"), R("dl"))
-        act(R("hd"), IND(R("hif"), R("dlu")))
-        act(R("wd"), IND(S("lw", CW, CW + C), R("dlu")), scale=2.0)
+        mm([(ps(7, 128 + r, 256, 16, n=16), S(nm, r, P, 16), w_) for nm, w_ in (("ca", R("sk", t)), ("cb", R("sk", 2)), ("ex", R("sk", 3)), ("cc", G8))
+            for r in range(16)])
+        act(S("owt", 0, 128, part=slice(0, 16)), ps(7, 128, 256, n=16), scale=0.125)
+        mm([(pa_, S("owt", 0, 128, part=slice(0, 16)), S("idf", 0, 16, part=slice(0, 16)))])
+        cp(R("dlu"), pa_)
+        if t == 0:
+            act(R("dl"), pa_)
+        act(R("wd"), IND(S("lw", CW, CW + C), R("dlu")), scale=-2.0, bias=2 * dl)
+        tt(R("hd"), IND(S("win", LO, LO + C), R("dlu")), R("wd"), A.add)
         act(R("nd", 1), IND(R("bl"), R("dlu")))
         ts(R("dvu"), R("nd", 1), 8.0, A.add)
         tt(IND(S("win", HA, HA + C), R("dlu")), R("hd"), R("bta"), A.add)
         tt(IND(S("win", HZ, HZ + C), R("dlu")), R("hd"), R("btz"), A.add)
         ops[-1]["lead"] = ops[-2]["lead"] = BOOST
-        ts(R("inv"), DL, Ct - 0.5, A.is_gt, 2.0 ** -7, A.add)
-        act(R("nd", 0), R("xi"), bias=float(B + P * t))
+        iota(R("nd", 0), [[1, P]], B + P * t, 0)
+        ops[-1]["rd"].append(R(sb)[1:4])
         if t == 1:
             dma(T.yx[:, 0:Ct], S("win", LO, LO + Ct))
             dma(T.yx[:, Ct:C], R("hd"))
         if t == 0:
             for a, b in ((0, 512), (512, V)):
-                mm([(ps(7), M(ID), S("win", LO + a, LO + b)), (ps(7), M(ID), S("yn", a, b)), (ps(7), M(NI), S("d2", a, b))])
+                mm([(ps(7), M(ID), S("win", LO + a, LO + b)), (ps(7), M(ID), yn(a, b)), (ps(7), M(NI), S("d2", a, b))])
                 act(S("xb", a, b), ps(7), F.Relu, bias=1029.0)
             o = ps(7, 0, P)
-            mm([(o, M(ID), R("hd")), (o, M(ID), S("yn", 0, P)), (o, M(NI), S("d2", 0, P)), (o, M(N8192), R("inv"))])
+            mm([(o, M(ID), R("hd")), (o, M(ID), yn(0, P)), (o, M(NI), S("d2", 0, P)), (o, M(N8192), R("inv", 0))])
             act(S("xb", V, V + P), o, F.Relu, bias=1093.0)
             ts(R("xb"), R("xb"), 63.0, A.min)
             cell_sums(1)
@@ -448,7 +502,7 @@ def rank_program(g, core, T, topo):
 
         chunks = chunks_of(t)
         loh, wh = S("lw", 0, CW), S("lw", CW, 2 * CW)
-        awin, zwin = S("win", LO, Y1 if t == 0 else WEND), S("win", 0, HA)
+        awin, zwin = S("win", LO, Y1 if t == 0 else WEND), S("win", 0, HZ + CW)
         U = lambda nm, a, b: S(nm, 16 * a, 16 * b)
         EU = lambda h, a, b: R("eu", h, slice(a, b))
         rot = [0]
@@ -457,8 +511,17 @@ def rank_program(g, core, T, topo):
             return [(a, min(c1, a + w)) for a in range(c0, c1, w)]
 
         def bank(w):
+            if w > 512:
+                rot[0] += rot[0] % 2 + 2
+                return ps(rot[0] % 4, 0, w)
             rot[0] += 1
-            return ps(rot[0] % 3, 0, w)
+            return ps((rot[0] + 1) % 4, 0, w)
+
+        def adds(a, b, terms):
+            p = bank(16 * (b - a))
+            for x, y in units(a, b):
+                mm([(S(p[1], p[2] + 16 * (x - a), p[2] + 16 * (y - a)), M(m), S(nm, o + 16 * x, o + 16 * y)) for m, nm, o in terms])
+            return p
 
         def relu2(o, i, on_v):
             if on_v:
@@ -469,104 +532,97 @@ def rank_program(g, core, T, topo):
         def phase1(k):
             c0, c1 = chunks[k]
             n, sc = c1 - c0, 5 - k % 2
-            plain = PLAIN[t][k]
+            plain = lambda a: a // 32 in PLAIN[t]
             d_ = dk(len(CUT) if t == 1 and k == len(CUT) - 1 else k, n)
-            mm([(ps(sc, 128 * j, 128 * j + 128, n=n), M(m, n), d_) for j, m in enumerate((IK2, N8192, IK3, IK2))], stop=False)
+            mm([(ps(sc, 128 * j, 128 * j + 128, n=n), M(m, n), d_) for j, m in enumerate((IBIG, IK2, N8192, IK3))], stop=False)
 
             def sums(nm, k0, k1, w0, stop=False):
                 mm([(ps(sc, 128 * k0 + r, 128 * k1, 16, n=n), S(nm, 16 * c0 + r, 16 * c1, 16), S("st", 8 * w0, 8 * (w0 + k1 - k0)))
                     for r in range(16)], start=False, stop=stop)
             big = units(c0, c1, GU[1])
-            if k == 0:
-                big = units(c0, c0 + GU[1], GU[0]) + big[1:]
+            if k == ORD1[t][0]:
+                big = units(c0, min(c1, c0 + GU[1]), GU[0]) + big[1:]
             for a, b in big:
                 tt(U("tu", a, b), IND(loh, EU(0, a, b)), S("win", YB + 16 * a, YB + 16 * b), A.subtract)
                 act(U("wa", a, b), IND(wh, EU(0, a, b)))
                 tt(U("t00", a, b), IND(loh, EU(1, a, b)), U("tu", a, b), A.add)
-                if plain:
-                    act(U("t01", a, b), IND(wh, EU(1, a, b)))
+                for a, b in [(a, b)] if plain(a) == plain(b - 1) else units(a, b):
+                    if plain(a):
+                        act(U("t01", a, b), IND(wh, EU(1, a, b)))
+                    else:
+                        tt(U("t01", a, b), IND(wh, EU(1, a, b)), U("t00", a, b), A.subtract)
+            for a, b in units(c0, c1, AW):
+                if RV00[t][k]:
+                    relu2(U("r00", a, b), U("t00", a, b), a - c0 < 32 * RV00[t][k])
                 else:
-                    tt(U("t01", a, b), IND(wh, EU(1, a, b)), U("t00", a, b), A.add)
-            for a, b in units(c0, c1):
-                w, u = 16 * (b - a), (a // 32) % 4
-                relu2(U("r00", a, b), U("t00", a, b), u < RV00[t][k])
-                p0 = bank(w)
-                mm([(p0, M(ID), U("t00", a, b)), (p0, M(ID), U("wa", a, b))])
-                relu2(U("r10", a, b), p0, False)
-                if plain:
-                    p1 = bank(w)
-                    mm([(p1, M(ID), U("t00", a, b)), (p1, M(ID), U("t01", a, b))])
-                    relu2(U("r01", a, b), p1, False)
-                    p1 = bank(w)
-                    mm([(p1, M(ID), U("t00", a, b)), (p1, M(ID), U("wa", a, b)), (p1, M(ID), U("t01", a, b))])
-                else:
-                    relu2(U("r01", a, b), U("t01", a, b), u < RV01[t][k])
-                    p1 = bank(w)
-                    mm([(p1, M(ID), U("t01", a, b)), (p1, M(ID), U("wa", a, b))])
-                relu2(U("r11", a, b), p1, False)
-            sums("wa", 0, 4, 0)
-            if not plain:
-                sums("t00", 1, 4, 5)
-            sums("t01", 1, 4, 2)
-            sums("r00", 0, 3, 2)
-            sums("r10", 0, 1, 5)
-            sums("r01", 1, 2, 5)
-            sums("r11", 2, 3, 5, stop=True)
+                    act(U("r00", a, b), U("t00", a, b), F.Abs)
+                for a, b in [(a, b)] if plain(a) == plain(b - 1) else units(a, b):
+                    if not plain(a):
+                        act(U("r01", a, b), U("t01", a, b), F.Abs, bias=-dl)
+            for a, b in units(c0, c1, PW):
+                act(U("r10", a, b), adds(a, b, ((ID, "t00", 0), (NI, "wa", 0))), F.Abs, bias=dl)
+                for a, b in [(a, b)] if plain(a) == plain(b - 1) else units(a, b):
+                    if plain(a):
+                        act(U("r01", a, b), adds(a, b, ((ID, "t00", 0), (NI, "t01", 0))), F.Abs, bias=dl)
+                    act(U("r11", a, b), adds(a, b, ((NI, "t00", 0),) * plain(a) + ((ID, "t01", 0), (ID, "wa", 0))), F.Abs, bias=-2 * dl)
+            if RV00[t][k]:
+                sums("t00", 1, 4, 8)
+            sums("r00", 1, 4, 5)
+            sums("r01", 0, 3, 0)
+            sums("r10", 0, 2, 3)
+            sums("r11", 3, 4, 2, stop=True)
 
         def decide(k):
             c0, c1 = chunks[k]
             n, sc = c1 - c0, 5 - k % 2
             pn_ = slice(0, n)
-            oa, oz, pp = ps(3, 0, n), ps(3, 128, 128 + n), lambda h: ps(3, 256 + n * h, 256 + n * h + n)
-            mm([(oa, R("idf"), S(E, c0, c1)), (oz, R("idf"), S(E, 192 + c0, 192 + c1))]
-               + [(pp(h), M(NI), R("far", h, slice(c0, c1))) for h in range(2)], stop=False)
-            act(S("rr", 0, 256, part=pn_), ps(sc, 0, 256, n=n), F.Relu)
-            tt(ps(6, 0, 128, n=n), ps(sc, 256, 384, n=n), S("rr", 128, 256, part=pn_), A.max)
-            tt(ps(6, 128, 256, n=n), ps(sc, 256, 384, n=n), S("rr", 0, 128, part=pn_), A.max)
-            act(S("ut", 0, 128, part=pn_), ps(sc, 384, 512, n=n), F.Relu, scale=-1.0)
-            tt(S("ppt", 0, 256, part=pn_), ps(6, 0, 256, n=n), S("rr", 0, 256, part=pn_), A.is_gt)
-            pz, pa, ut = S("ppt", 0, 128, part=pn_), S("ppt", 128, 256, part=pn_), S("ut", 0, 128, part=pn_)
-            mm([(oa, ut, M(P8192, n)), (oz, ut, M(N8192, n))], start=False, stop=False)
-            mm([(oa, pa, M(IA, n)), (oz, pz, M(IZ, n)), (pp(0), pa, M(ID, n)), (pp(1), pz, M(ID, n))], start=False)
+            oa, oz = ps(6, 256, 256 + n), ps(6, 384, 384 + n)
+            mm([(oa, R("idf"), S(E, c0, c1)), (oz, R("idf"), S(E, 192 + c0, 192 + c1))], stop=False)
+            act(S("rr", 0, 256, part=pn_), ps(sc, 128, 384, n=n), F.Relu)
+            tt(ps(6, 0, 128, n=n), ps(sc, 384, 512, n=n), S("rr", 128, 256, part=pn_), A.max)
+            tt(ps(6, 128, 256, n=n), ps(sc, 384, 512, n=n), S("rr", 0, 128, part=pn_), A.max)
+            act(S("ut", 0, 128, part=pn_), ps(sc, 0, 128, n=n), F.Relu, bias=-8.0 * (9600, 12000)[t])
+            tt(R("ppt", k, part=pn_), ps(6, 0, 256, n=n), S("rr", 0, 256, part=pn_), A.is_gt)
+            pz, pa, ut = R("ppt", k, slice(0, 128), part=pn_), R("ppt", k, slice(128, 256), part=pn_), S("ut", 0, 128, part=pn_)
+            mm([(oa, ut, M(ID, n)), (oz, ut, M(NI, n))], start=False, stop=False)
+            mm([(oa, pa, M(IA, n)), (oz, pz, M(IZ, n))], start=False)
             tt(S("oa", 0, n), oa, S("jb" if t == 0 else "jb1", c0, c1), A.min)
             cp(S("ofs", c0, c1), S("oa", 0, n))
             ts(S("ofs", 192 + c0, 192 + c1), oz, 16.0, A.add)
-            act(R("ppl", slice(None), slice(c0, c1)), ps(3, 256, 256 + 2 * n), F.Relu, scale=512.0)
 
         def phase2(k):
             c0, c1 = chunks[k]
             n, sc = c1 - c0, 5 - k % 2
             GA, DD, HH, AH = "r00", "r01", "r10", "r11"
-            gu = GU[3] if k == len(chunks) - 1 else GU[2]
-            big = units(c0, c1, gu)
-            if k == 0:
-                big = units(c0, c0 + gu, 32) + big[1:]
+            big = units(c0, c1, GU[2])
+            if k == ORD2[t][0]:
+                big = units(c0, min(c1, c0 + GU[2]), 32) + big[1:]
+            else:
+                big = big[:-1] + units(big[-1][0], c1, GU[3])
             for a, b in big:
                 act(U(GA, a, b), IND(awin, S("ofs", a, b)))
                 tt(U(DD, a, b), IND(zwin, S("ofs", 192 + a, 192 + b)), U(GA, a, b), A.subtract)
-                ts(U(HH, a, b), U(DD, a, b), MAG, A.add, -MAG, A.add)
-            onv = lambda a: (a // 32) % 4 < RVAH[t][k]
-            for a, b in units(c0, c1):
-                if onv(a):
-                    relu2(U(AH, a, b), U(HH, a, b), True)
+                if a // 32 in HHA[t]:
+                    act(U(HH, a, b), U(DD, a, b), bias=192.0)
                 else:
-                    act(U(AH, a, b), U(HH, a, b), F.Abs)
-            mm([(ps(sc, 128 + r, 384, 16, n=n), S(nm, 16 * c0 + r, 16 * c1, 16), S("sw", w0, w0 + 16)) for nm, w0 in ((DD, 0), (HH, 16)) for r in range(16)])
+                    ts(U(HH, a, b), U(DD, a, b), 192.0, A.add)
+            onv = lambda a: False
+            for a, b in big if k == ORD2[t][-1] else units(c0, c1, AW):
+                act(U(AH, a, b), U(HH, a, b), F.Abs, bias=-192.0)
+            mm([(ps(sc, 128, 384, n=n), M(KD, n), S("c768", 0, 256, part=slice(0, n)))] + [(ps(sc, 128 + r, 384, 16, n=n), S(nm, 16 * c0 + r, 16 * c1, 16), S("sw", w0, w0 + 16)) for nm, w0 in ((DD, 0), (HH, 16)) for r in range(16)])
             act(S("nnt", 0, 256, part=slice(0, n)), ps(sc, 128, 384, n=n))
-            ys = lambda r, m=n: ps(sc, r, 128, 16, n=m)
+            ys = lambda r, m=n: ps(9 - sc if k == ORD2[t][-1] else sc, r, 128, 16, n=m)
 
             def woven(a, b, o):
-                p = bank(16 * (b - a))
-                mm([(p, M(I255), S("win", YB + 16 * a, YB + 16 * b)), (p, M(I255), U(AH, a, b))] + [(p, M(N255), U(HH, a, b))] * onv(a))
-                ts(o, p, MAG, A.add, -MAG, A.add)
+                ts(o, adds(a, b, ((I255, "win", YB), (I255, AH, 0))), MAG, A.add, -MAG, A.add)
             if t == 0:
-                for a, b in units(c0, c1):
+                for a, b in big if k == ORD2[t][-1] else units(c0, c1, PW):
                     woven(a, b, S("win", Y1 + 16 * a, Y1 + 16 * b))
                 mm([(ys(r), S("win", Y1 + 16 * c0 + r, Y1 + 16 * c1, 16), S("st", 0, 8)) for r in range(16)])
             else:
                 cb = min(c1, KB)
                 m = cb - c0
-                rb = 16 if m <= 32 else 8 if m <= 64 else 4
+                rb = 8 if m <= 64 or PW > 32 and m == 128 else 4
                 if cb < c1:
                     woven(cb, c1, S("yon", ZB, ZB + P))
                     mm([(ys(r), S("yon", r, 16 * n, 16), S("st", 0, 8)) for r in range(16)], stop=False)
@@ -574,11 +630,10 @@ def rank_program(g, core, T, topo):
                     p = bank(rb * m)
                     its = []
                     for r in range(r0, r0 + rb):
-                        oo = S(p[1], m * (r - r0), m * (r - r0 + 1))
+                        oo = S(p[1], p[2] + m * (r - r0), p[2] + m * (r - r0 + 1))
                         its += [(oo, M(I255), S("win", Y1 + 16 * c0 + r, Y1 + 16 * cb, 16)), (oo, M(I255), S(AH, 16 * c0 + r, 16 * cb, 16))]
-                        if RVAH[t][k]:
-                            its += [(oo, M(N255), S(HH, 16 * c0 + r, 16 * cb, 16))]
-                    mm(its)
+                    for x in range(0, 2 * rb, 2 * min(rb, 512 // m)):
+                        mm(its[x:x + 2 * min(rb, 512 // m)])
                     ts(R("yo", slice(r0, r0 + rb), slice(c0, cb)), p, MAG, A.add, -MAG, A.add)
                     mm([(ys(r, m), R("yo", r, slice(c0, cb)), S("st", 0, 8)) for r in range(r0, r0 + rb)], start=r0 == 0 and cb == c1, stop=r0 + rb == 16)
 
@@ -587,112 +642,128 @@ def rank_program(g, core, T, topo):
             n, sc = c1 - c0, 5 - k % 2
             pn_ = slice(0, n)
             na, nz = S("nnt", 0, 128, part=pn_), S("nnt", 128, 256, part=pn_)
-            PL = lambda h: R("ppl", h, slice(c0, c1))
-            cd = ps(6, 256, 256 + n)
-            mm([(cd, na, M(ID, n)), (cd, nz, M(ID, n)), (cd, M(ID), PL(0)), (cd, M(ID), PL(1))], stop=False)
+            pz, pa = R("ppt", k, slice(0, 128), part=pn_), R("ppt", k, slice(128, 256), part=pn_)
             IN = IN0 if t == 0 else IN1
-            rr = lambda h: ps(3, 128 * h, 128 * h + n)
-            mm([(rr(0), na, M(ID, n)), (rr(0), M(IN), PL(0)), (rr(1), nz, M(ID, n)), (rr(1), M(IN), PL(1))])
-            ts(dk(k, n), ps(sc, 0, 128, n=n), 1407.5, A.is_lt, EPS, A.add)
-            mm([(cd, dk(k, n), M(N8192, n))], start=False)
-            act(S("cod", c0, c1), cd, bias=-639.0)
+            rr = lambda h: ps(6, 256 + 128 * h, 256 + 128 * h + n)
+            mm([(rr(0), pa, M(IN, n)), (rr(1), pz, M(IN, n)), (rr(0), na, M(ID, n)), (rr(1), nz, M(ID, n))])
             for h in range(2):
                 ne = S(En, 192 * h + c0, 192 * h + c1)
                 tt(ne, rr(h), S(E, 192 * h + c0, 192 * h + c1), A.max)
                 if t == 0:
                     cp(EU(h, c0, c1), ne)
+            cd = ps(sc if k == ORD2[t][-1] else 6, 0, n)
+            mm([(cd, pa, M(KD, n)), (cd, pz, M(KD, n)), (cd, na, M(ID, n)), (cd, nz, M(ID, n))], stop=False)
+            ts(dk(k, n), ps(9 - sc if k == ORD2[t][-1] else sc, 0, 128, n=n), 1407.5, A.is_lt, EPS, A.add)
+            mm([(cd, dk(k, n), M(N8192, n))], start=False)
+            act(S("cod", c0, c1), cd, bias=-382.0)
 
-        for k in range(len(chunks)):
+        for k in ORD1[t]:
             phase1(k)
             decide(k)
-        for k in range(len(chunks)):
+        for k in ORD2[t]:
             phase2(k)
             post(k)
+        iota(S("tu", 0, 8), [[0, 8]], -8192, 0)
+        dma(S("tu", 8, 8 + B, part=slice(0, 128, 16)), S("cod", 0, KB))
 
-        dma(S("info", 8, 8 + B, part=slice(0, 128, 16)), S("cod", 0, KB), tag="i%d" % t)
         if t == 0:
             own_cells(1)
-            cell_preload(1)
+            cell_preload(1, (0, 1))
             old_live(UO)
         else:
             mm([(ps(0, r, P, 16), R("wt", r), S("cod", KB, NC)) for r in range(16)])
-            act(S("info", 8 + B, 8 + B + P), ps(0, 0, P))
-            ops[-1]["tag"] = "i1"
+            act(S("tu", 8 + B, 8 + B + P), ps(0, 0, P))
             dma(T.yy[:, 0:B], R("yo"))
-            ops[-1]["rd"].append(S("info", 16, 32)[1:4])
+            ops[-1]["rd"].append(S("tu", 16, 32)[1:4])
             for h in range(2):
-                dma(T.ye[h::2, 0:B], S("e2", 192 * h, 192 * h + KB), eng="sa"[h])
+                dma(T.ye[h::2, 0:B], S("e2", 192 * h, 192 * h + KB))
+                ops[-1]["rd"].append(S("tu", 16, 32)[1:4])
                 cp(S("tr", 16 * h, 16 * h + 16), S("e2", 192 * h + KB, 192 * h + NC))
             op("v", lambda e: e.transpose(T.trt[:], T.tr[:]), 100, [R("tr")], [R("trt")])
             for a in range(4):
                 for gp in range(2):
                     dma(T.ye[4 * a + 2 * gp:4 * a + 2 * gp + 2, B:B + P], S("trt", 16 * gp, 16 * gp + 16, part=slice(32 * a, 32 * a + 32)))
-        iw = R("info")
+                    ops[-1]["rd"].append(S("tu", 16, 32)[1:4])
+        iw = R("tu")
         EM = lambda x, a, b: R("em", x, slice(a, b))
-        for h in range(2):
-            a, b = 128 * h, 128 * h + 128
-            oo = ps(6 + h, 0, 128)
-            mm([(oo, M(NI), S("ii", a, b))], stop=False)
-            for k in (2 * h, 2 * h + 1):
+        for pb, (a, b) in zip((6, 7, 2 + 4 * t), PIECES):
+            oo = ps(pb, 0, b - a)
+            for k in range(a // 64, b // 64):
                 for u in (2 * k, 2 * k + 1):
-                    (cp if u in GSV else act)(S("gs", 512 * u, 512 * u + 512), IND(iw, S("dvu", 32 * u, 32 * u + 32)))
-                mm([(ps(6 + h, 64 * (k % 2), 64 * (k % 2) + 64), W(WS, s), S("gs", 1024 * k + s, 1024 * k + 1024, 16)) for s in range(16)],
-                   start=False, stop=k % 2 == 1)
-            ts(EM(0, a, b), oo, 0.0, A.is_equal)
-            ts(EM(1, a, b), oo, 256.5, A.is_gt)
+                    (cp if u in GSV[t] else act)(S("gs", 512 * u, 512 * u + 512), IND(iw, S("dvu", 32 * u, 32 * u + 32)))
+                mm([(ps(pb, 64 * k - a, 64 * k - a + 64), W(WS, s), S("gs", 1024 * k + s, 1024 * k + 1024, 16)) for s in range(16)],
+                   start=k == a // 64, stop=k == b // 64 - 1)
+            tt(EM(0, a, b), oo, S("ii", a, b), A.is_equal)
+            ts(EM(1, a, b), oo, 127.5, A.is_gt)
             ts(EM(2, a, b), oo, -2000.0, A.is_lt)
             if t == 0:
-                g2, g3 = ps(6 + h, 128, 256), ps(6 + h, 256, 384)
-                mm([(g2, M(ID), S("pn", a, b)), (g3, M(NI), S("pn", a, b)), (g3, M(ONES), S("ones", 0, 128))], stop=False)
-                mm([(g2, M(ONES), EM(0, a, b)), (g3, M(NON), EM(0, a, b)), (g2, M(ONES), EM(1, a, b)), (g3, M(NON), EM(1, a, b)),
-                    (g2, M(ONES), EM(2, a, b))], start=False)
-                act(S("tt", 0, 256), ps(6 + h, 128, 384), F.Sign, bias=-0.5, acc=col(22 + h))
-                ts(TH if h else UO, col(22 + h), -4.0, A.mult, UO, A.add)
+                h = a // 128
+                g2, g3 = lambda a, b: ps(5, a % 128, a % 128 + b - a), lambda a, b: ps(5, 128 + a % 128, 128 + a % 128 + b - a)
+                if a % 128 == 0:
+                    mm([(g2(a, a + 128), M(ID), S("pn", a, a + 128)), (g3(a, a + 128), M(NI), S("pn", a, a + 128)),
+                        (g3(a, a + 128), M(ONES), S("ones", 0, 128))], stop=False)
+                for x in range(2):
+                    mm([(g2(a, b), M(ONES), EM(x, a, b)), (g3(a, b), M(NON), EM(x, a, b))], start=False, stop=False)
+                mm([(g2(a, b), M(ONES), EM(2, a, b))], start=False, stop=b % 128 == 0)
+                if b % 128 == 0:
+                    act(S("tt", 0, 256), ps(5, 0, 256), F.Sign, bias=-0.5, acc=col(22 + h))
+                    if h:
+                        ts(WB, col(23), col(20), A.add)
+                        ts(R("xs"), R("xs"), col(23), A.add)
+                    else:
+                        ts(UO, col(22), -4.0, A.mult, UO, A.add)
+                        ts(col(20), UO, -0.25, A.mult, 8320.0, A.add)
+                        ts(R("xs"), R("xs"), UO, A.add, -0.25, A.mult)
+        if t == 0:
+            cell_preload(1, (2,))
 
         def slot_tail(t=t, n0=n0):
-            w = P // HALVES[t]
-            for a in range(0, P, w):
-                b = a + w
-                bv, bn, bg = (3, 4, 6) if t == 0 else (a // w, 2 + a // w, 4 + a // w)
+            for x, (a, b) in enumerate(TAILS[t]):
+                w = b - a
+                bv, bn, bg = (4, 4, 6) if t == 0 else (x % 2, 2 + x % 2, 4 + x % 2)
                 e0, e1, e2, on = EM(0, a, b), EM(1, a, b), EM(2, a, b), S("ones", 0, w)
                 f, fk = ps(bv, 0, w), ps(bv, w, 2 * w)
-                mm([(f, M(CV), S("inv", a, b)), (fk, M(K8), on)], stop=False)
+                inv = R("inv", t, slice(a, b))
+                mm([(f, M(CV), inv), (fk, M(K8), on)], stop=False)
                 mm([(f, M(A1), e0), (fk, M(N8192), e0), (f, M(A1), e1), (fk, M(N8192), e1), (f, M(A3), e2), (fk, M(N8192), e2)], start=False)
                 tt(R("fv", slice(None), slice(a, b)), ps(bv, 0, 2 * w), R("nd", slice(None), slice(a, b)), A.min)
                 tt(IND(R("bl"), S("dlu", a // 16, b // 16)), R("fv", 0, slice(a, b)), R("fv", 1, slice(a, b)), A.max)
                 f, fk = ps(bn, 0, w), ps(bn, w, 2 * w)
-                mm([(f, M(CV), S("inv", a, b)), (f, M(A1), on), (fk, M(NI), on)], stop=False)
+                mm([(f, M(CV), inv), (f, M(A1), on), (fk, M(NI), on)], stop=False)
                 mm([(f, M(NA1), e0), (fk, M(P8192), e0), (f, M(NA1), e1), (fk, M(P8192), e1), (f, M(O8192), e2)], start=False)
                 tt(R("fn", slice(None), slice(a, b)), ps(bn, 0, 2 * w), R("nd", slice(None), slice(a, b)), A.min)
                 tt(S("bl", n0 + a, n0 + b) if t == 0 else S("tv", a, b), R("fn", 0, slice(a, b)), R("fn", 1, slice(a, b)), A.max)
                 gg = ps(bg, 0, w)
-                mm([(gg, M(N8192), S("inv", a, b)), (gg, M(ON17), e0), (gg, M(ON17), e1), (gg, M(ONES), e2)])
+                mm([(gg, M(N8192), inv), (gg, M(ON17), e0), (gg, M(ON17), e1), (gg, M(ONES), e2)])
                 act(S("s1", a, b), gg, F.Abs, bias=-72.0)
+                um = S("um", a, b)
+                act(um, S("s1", a, b), F.Relu, bias=-135.0)
+                yy, ev, en = gg, ps(bg, 256, 256 + w // 2 * (t + 1)), ps(bg, 384, 384 + w // 2 * (t + 1))
                 if t == 0:
-                    ts(S("made", a, b), S("s1", a, b), 135.5, A.is_lt)
-                    tt(S("win", Y1 + B + a, Y1 + B + b), S("made", a, b), S("wd", a, b), A.mult)
+                    mm([(yy, M(ID), S("wd", a, b)), (yy, M(N8192), um)])
+                    act(S("win", Y1 + B + a, Y1 + B + b), yy, F.Relu)
                 else:
-                    ts(gg, S("s1", a, b), 135.5, A.is_lt)
-                    tt(S("yon", ZB + P + a, ZB + P + b), gg, S("wd", a, b), A.mult)
-                    tt(S("tt", a, b), gg, S("dlw", a, b), A.mult)
-                    tt(S("tt", P + a, P + b), gg, S("s2", a, b), A.mult)
+                    mm([(ev, M(ON80), S("ca", a, b)), (ev, M(ON16), S("cb", a, b)), (ev, M(ONES), S("cc", a, b)), (en, M(ID), S("ii", a, b)),
+                        (yy, M(ID), S("wd", a, b))], stop=False)
+                    mm([(x, M(N8192), um) for x in (yy, ev, en)], start=False)
+                    act(S("tt", a, b), ev, F.Relu)
+                    act(S("tt", P + a, P + b), en, F.Relu, bias=128.0 + n0)
+                    act(S("yon", ZB + P + a, ZB + P + b), yy, F.Relu)
             if t == 0:
                 c0, n = CUT[-1], KB + 16 - CUT[-1]
                 mm([(ps(7, r, 128, 16, n=n), S("win", Y1 + 16 * c0 + r, WEND, 16), S("st", 0, 8)) for r in range(16)])
                 ts(dk(len(CUT), n), ps(7, 0, 128, n=n), 1407.5, A.is_lt, EPS, A.add)
-                mm([(ps(6, 0, 16), W(P8, r), S("made", r, P, 16)) for r in range(16)])
-                ts(R("mw"), ps(6, 0, 16), 1 / 128, A.mult)
+                mm([(ps(6, 0, 16), W(P8, r), S("win", Y1 + B + r, WEND, 16)) for r in range(16)])
+                ts(R("mw"), ps(6, 0, 16), 0.5, A.is_gt)
                 for h, src in ((0, "dl"), (1, "nw")):
                     tt(S("e1", 192 * h + KB, 192 * h + KB + 16), R("mw"), R(src), A.mult)
                     cp(R("eu", h, slice(KB, KB + 16)), S("e1", 192 * h + KB, 192 * h + KB + 16))
             else:
                 dma(T.yl[:, 0:n0], S("bl", 0, n0), lat=3000.0)
-                dma(T.yl[:, n0:C], R("tv"), eng="a")
+                dma(T.yl[:, n0:C], R("tv"))
                 dma(T.yy[:, B:B + 2 * P], S("yon", ZB, ZB + 2 * P), eng="a")
                 for h in range(2):
-                    dma(T.ye[h::2, B + P:B + 2 * P], S("tt", P * h, P * h + P, part=slice(0, 128, 16)), eng="a")
-        if t == 1:
-            act(R("s2"), R("xi"), bias=float(n0))
+                    dma(T.ye[h::2, B + P:B + 2 * P], S("tt", P * h, P * h + P, part=slice(0, 128, 16)), eng="sa"[h])
         late.append(slot_tail)
     late[1]()
 
@@ -722,17 +793,27 @@ def emit(ops, queue, T):
         if a["e"] != b["e"] or a["kind"] != "c" or b["kind"] != "c":
             return False
         return a["e"] == "p" or not (meet(a["tw"], b["tr"] + b["tw"]) or meet(a["tr"], b["tw"]))
-    succ = [[] for _ in range(n)]
+    above, full = [0] * n, list(deps)
     for k in range(n):
+        a = 0
         for j in deps[k]:
+            a |= above[j]
+        above[k] = a | sum(1 << j for j in deps[k])
+        deps[k] = set(j for j in deps[k] if not a >> j & 1)
+    back = [[(j, ops[j]["lat"], 0.0 if free_edge(j, k) else 1.0) for j in deps[k]] + [(j, 0.0, 0.0) for j in ops[k].get("after", [])] for k in range(n)]
+    succ, gap = [[] for _ in range(n)], [[] for _ in range(n)]
+    for k in range(n):
+        for j, l, h in back[k]:
             succ[j].append(k)
+            gap[j].append(l + h * HOP)
     tail = [0.0] * n
     for k in range(n - 1, -1, -1):
         tail[k] = ops[k]["cost"] + ops[k]["lat"] + ops[k].get("lead", 0.0) + max([HOP + tail[j] for j in succ[k]] + [0.0])
-    gap = [[ops[k]["lat"] + (0.0 if free_edge(k, j) else HOP) for j in succ[k]] for k in range(n)]
+
+    cost0, eng = [o["cost"] for o in ops], [o["e"] for o in ops]
 
     def plan(pri, look):
-        left = [len(d) for d in deps]
+        left = [len(d) for d in back]
         ready = {e: [] for e in queue}
         at = [0.0] * n
         for k in range(n):
@@ -740,38 +821,54 @@ def emit(ops, queue, T):
                 ready[ops[k]["e"]].append(k)
         free = {e: 0.0 for e in queue}
         order, start, end = [], [0.0] * n, 0.0
+        pick, stale = {}, set(queue)
         while len(order) < n:
-            best = None
-            for e in queue:
-                if ready[e]:
-                    now = max(free[e], min(at[k] for k in ready[e]))
-                    k = max((k for k in ready[e] if at[k] <= now + 40), key=lambda k: pri[k])
-                    soon = [j for j in ready[e] if now + 40 < at[j] < now + look * ops[k]["cost"] and pri[j] > pri[k] + ops[k]["cost"]]
+            for e in stale:
+                rd = ready[e]
+                if not rd:
+                    pick.pop(e, None)
+                    continue
+                k = rd[0]
+                if len(rd) > 1:
+                    now = max(free[e], min([at[x] for x in rd]))
+                    k = max([x for x in rd if at[x] <= now + 40], key=lambda x: pri[x])
+                    soon = [j for j in rd if now + 40 < at[j] < now + look * cost0[k] and pri[j] > pri[k] + cost0[k]]
                     if soon:
-                        j = max(soon, key=lambda j: pri[j])
-                        fit = [x for x in ready[e] if max(at[x], now) + ops[x]["cost"] <= at[j] + 60]
+                        j = max(soon, key=lambda x: pri[x])
+                        fit = [x for x in rd if max(at[x], now) + cost0[x] <= at[j] + 60]
                         k = max(fit, key=lambda x: pri[x]) if fit else j
-                    st = max(free[e], at[k])
-                    if best is None or st < best[0]:
-                        best = (st, k)
-            st, k = best
-            e = ops[k]["e"]
+                pick[e] = (max(free[e], at[k]), k)
+            st, k = min(pick.values())
+            e = eng[k]
+            stale = {e}
             ready[e].remove(k)
             order.append(k)
             start[k] = st
-            free[e] = st + ops[k]["cost"]
-            end = max(end, free[e] + ops[k]["lat"])
+            f = free[e] = st + cost0[k]
+            end = max(end, f + ops[k]["lat"])
             for j, gp in zip(succ[k], gap[k]):
-                at[j] = max(at[j], free[e] + gp)
+                if f + gp > at[j]:
+                    at[j] = f + gp
                 left[j] -= 1
                 if left[j] == 0:
-                    ready[ops[j]["e"]].append(j)
+                    ready[eng[j]].append(j)
+                    stale.add(eng[j])
         return end, order, start
 
     plan0 = plan
-    back = [[(j, ops[j]["lat"], 0.0 if free_edge(j, k) else 1.0) for j in deps[k]] for k in range(n)]
-    cases = [([o["cost"] + dg * o["ng"] + ds * o["ns"] + fx + (pe - 1.0) * o["cost"] * (o["e"] == "p") for o in ops], hop, lat)
-             for dg, ds, fx, pe, hop, lat in CASES]
+
+    def priced(o, cy, ga, sc, fv, fa, pe, first):
+        if o["kind"] != "c":
+            return o["cost"] + first * (o["kind"] == "r2")
+        if o["ng"] or o["ns"]:
+            return 55.0 + cy * (ga * o["ng"] + sc * o["ns"])
+        fix, new = {"v": (30, fv), "a": (70, fa), "g": (150, 150), "p": (0, 0)}[o["e"]]
+        if o["e"] != "p" and any(x[0][:4] == "bank" for x in o["wr"]):
+            new += PSX
+        return new + (o["cost"] - fix) * (2 * pe if o["e"] == "p" else cy)
+    cases = [([w * priced(o, cy, ga, sc, fv, fa, pe, first) for o in ops], [(k, w * o["lat"] * lat) for k, o in enumerate(ops) if o["lat"]],
+              [[(j, w * (l * (lat if ops[j]["kind"] == "d" else rem) + h * hop)) for j, l, h in b] for b in back])
+             for w, cy, ga, sc, fv, fa, pe, hop, lat, rem, first in CASES]
 
     def plan(pri, look):
         end, order, start = plan0(pri, look)
@@ -780,59 +877,149 @@ def emit(ops, queue, T):
             free = {e: 0.0 for e in queue}
             last = 0.0
             for k in order:
-                s = free[ops[k]["e"]]
-                for j, l, h in back[k]:
-                    x = fin[j] + l * lat + h * hop
+                s = free[eng[k]]
+                for j, d in lat[k]:
+                    x = fin[j] + d
                     if x > s:
                         s = x
-                fin[k] = free[ops[k]["e"]] = s + cost[k]
-                if ops[k]["lat"]:
-                    last = max(last, fin[k] + ops[k]["lat"] * lat)
-            end += last
+                fin[k] = free[eng[k]] = s + cost[k]
+            end += max([fin[k] + d for k, d in hop])
         return end / (1 + len(cases)), order, start
+
+    slack = [0.0]
+
+    def judge(order, a=0, old=None, first=0):
+        end, crit, state = 0.0, [], {}
+        prev0 = {e: -1 for e in queue}
+        for k in order[:a]:
+            prev0[eng[k]] = k
+        rest = order[a:]
+        for i in [first] + [x for x in range(len(cases)) if x != first]:
+            cost, hop, lat = cases[i]
+            fin, why = (old[i][0][:], old[i][1][:]) if old else ([0.0] * n, [-1] * n)
+            prev = dict(prev0)
+            for k in rest:
+                p = prev[eng[k]]
+                s = fin[p] if p >= 0 else 0.0
+                w = -2 - p
+                for j, d in lat[k]:
+                    if fin[j] + d > s:
+                        s = fin[j] + d
+                        w = j
+                fin[k] = s + cost[k]
+                why[k] = w
+                prev[eng[k]] = k
+            last, k = max([(fin[k] + d, k) for k, d in hop])
+            if old and i == first and last > old[i][2] + 2 * slack[0]:
+                return 1e18, None, None
+            state[i] = (fin, why, last)
+            end += last
+            while k != -1:
+                w = why[k]
+                if w < -1:
+                    crit.append((-2 - w, k, i))
+                    w = -2 - w
+                k = w
+        return end / len(cases), crit, state
+
+    def improve(order, tries, rng):
+        pre = [set(j for j, l, h in b) for b in back]
+        post = [set() for _ in range(n)]
+        for k in range(n):
+            for j in pre[k]:
+                post[j].add(k)
+        end, crit, state = judge(order)
+        top = (end, order)
+        for trial in range(tries):
+            slack[0] = TEMP * max(0.0, 1.0 - 1.15 * trial / tries)
+            p, k, case = crit[rng.randint(len(crit))]
+            e, far = eng[k], rng.randint(1, FAR) if trial % 2 else 1
+            if trial % 4 < 2:
+                b = a = order.index(k)
+                while a > 0 and far:
+                    a -= 1
+                    far -= eng[order[a]] == e
+                need, qs, go = set(pre[k]), set(), [k]
+                for x in order[b - 1:a - 1 if a else None:-1]:
+                    if x in need or eng[x] in qs:
+                        go.append(x)
+                        need |= pre[x]
+                        qs.add(eng[x])
+                if go[-1] == order[a]:
+                    continue
+                gs = set(go)
+                new = order[:a] + go[::-1] + [x for x in order[a:b] if x not in gs] + order[b + 1:]
+            else:
+                b = a = order.index(p)
+                while b < n - 1 and far:
+                    b += 1
+                    far -= eng[order[b]] == e
+                need, qs, go = set(post[p]), set(), [p]
+                for x in order[a + 1:b + 1]:
+                    if x in need or eng[x] in qs:
+                        go.append(x)
+                        need |= post[x]
+                        qs.add(eng[x])
+                if go[-1] == order[b]:
+                    continue
+                gs = set(go)
+                new = order[:a] + [x for x in order[a + 1:b + 1] if x not in gs] + go + order[b + 1:]
+            e2, c2, s2 = judge(new, a, state, case)
+            if e2 <= end + slack[0] * rng.rand() ** 2:
+                end, crit, order, state = e2, c2, new, s2
+                if end < top[0]:
+                    top = (end, order)
+        return top
 
     rng = np.random.RandomState(7)
     base = np.array([tail[k] + (1e6 if ops[k]["kind"] != "c" else 0.0) - 1e-3 * k for k in range(n)])
     if n not in PLANS:
-        best = None
-        for trial in range(20):
-            pri, look = base + (0.0, 100.0, 400.0, 1200.0)[trial // 5] * rng.rand(n), (0.0, 0.3, 0.5, 0.7, 0.9)[trial % 5]
-            end = plan(list(pri), look)[0]
-            if best is None or end < best[0]:
-                best = (end, pri, look)
-        for trial in range(TRIES):
-            pri = best[1].copy()
-            a = rng.randint(n)
-            if trial % 2:
-                pri[a:a + rng.randint(1, 40)] += rng.randn() * 3000.0
-            else:
-                pri[a:a + 120] += rng.randn(len(pri[a:a + 120])) * 500.0
-            look = best[2] if trial % 7 else rng.rand()
-            end = plan(list(pri), look)[0]
-            if end <= best[0]:
-                best = (end, pri, look)
-        PLANS[n] = best
-    end, order, start = plan(list(PLANS[n][1]), PLANS[n][2])
-    for k in range(n):
-        ops[k]["st"] = start[k]
+        found = []
+        for start in range(STARTS):
+            best = None
+            for trial in range(20):
+                pri, look = base + (0.0, 100.0, 400.0, 1200.0)[trial // 5] * rng.rand(n), (0.0, 0.3, 0.5, 0.7, 0.9)[trial % 5]
+                end = plan(list(pri), look)[0]
+                if best is None or end < best[0]:
+                    best = (end, pri, look)
+            for trial in range(TRIES):
+                pri = best[1].copy()
+                a = rng.randint(n)
+                if trial % 2:
+                    pri[a:a + rng.randint(1, 40)] += rng.randn() * 3000.0
+                else:
+                    pri[a:a + 120] += rng.randn(len(pri[a:a + 120])) * 500.0
+                look = best[2] if trial % 7 else rng.rand()
+                end = plan(list(pri), look)[0]
+                if end <= best[0]:
+                    best = (end, pri, look)
+            found.append(improve(plan(list(best[1]), best[2])[1], MOVES // 40, rng))
+        PLANS[n] = improve(min(found)[1], MOVES, rng)
+    end, order = PLANS[n]
+    DBG.update(ops=ops, order=order, cases=cases, eng=eng)
     pos = {k: i for i, k in enumerate(order)}
     need = [False] * n
     waits = [[] for _ in range(n)]
     seen = {e: {} for e in queue}
+    known = {}
     for k in order:
         e = ops[k]["e"]
         last = {}
-        for j in deps[k]:
+        for j in full[k]:
             key = ops[j]["e"] if ops[j]["kind"] == "c" else j
             if free_edge(j, k):
                 continue
             if key not in last or pos[j] > pos[last[key]]:
                 last[key] = j
-        for key, j in last.items():
+        for key, j in sorted(last.items(), key=lambda x: -pos[x[1]]):
             if seen[e].get(key, -1) < pos[j]:
                 seen[e][key] = pos[j]
                 need[j] = True
                 waits[k].append(j)
+                for x, p in known[j].items() if ops[j]["kind"] in "cd" else ():
+                    if seen[e].get(x, -1) < p:
+                        seen[e][x] = p
+        known[k] = dict(seen[e])
     sig = {}
     cnt = {e: 0 for e in queue}
     nd = 0

import numpy as np
from concourse.bass import DstId, RemoteDMATransfer
from concourse.mybir import AluOpType as A, AxisListType as AX, ActivationFunctionType as F

V, B, P, C, GH = 1024, 2768, 256, 1536, 336
THETA, DELTA = (465, 580), (7, 9)
CW = C + GH
LO, HZ, HA = 16, 16 + CW, 16 + 4992
XA, YN, Y0 = HZ, HA + C - B, HA + CW
Y1, WEND = Y0 + B, Y0 + B + B + P
KB = 173
MAG = 1.5 * 2 ** 23
CUT = (0, 128)
ZB = 16 * (KB - CUT[-1])
EPS = 2.0 ** -13
NB = 16 * (KB + 16)

bf, f4, i4, u2 = "bfloat16", "float32", "int32", "uint16"
SB = {
    "win": ([WEND], bf), "lw": ([2 * CW], bf), "ax": ([1280], bf), "xb": ([1280], bf), "wb": ([2], bf),
    "yo": ([16, KB], bf), "yon": ([ZB + 512], bf), "bli": ([V], i4), "bl": ([C], f4),
    "eni": ([2 * KB], i4), "e0": ([384], f4), "e1": ([384], f4), "e2": ([384], f4), "eu": ([2, 192], u2), "ofs": ([384], u2),
    "cod": ([192], bf),
    "sni": ([24], i4), "snf": ([144], f4), "snu": ([72], u2), "mk": ([GH], f4), "gm": ([GH], f4), "ow": ([72], u2), "owt": ([136], f4),
    "sb0": ([GH], bf), "sb1": ([GH], bf), "land0": ([GH], bf), "land1": ([GH], bf), "flo": ([GH], bf),
    "sx0": ([GH], bf), "sx1": ([GH], bf), "lx0": ([GH], bf), "lx1": ([GH], bf), "mk2": ([GH], bf),
    "tu": ([NB + 16], bf), "t00": ([NB], bf), "t01": ([NB], bf), "wa": ([NB], bf),
    "r00": ([NB], bf), "r01": ([NB], bf), "r10": ([NB], bf), "r11": ([NB], bf),
    "dkt": ([len(CUT) + 1, 128], bf), "rr": ([256], f4), "ppt": ([len(CUT), 256], bf), "ut": ([128], bf), "nnt": ([256], bf), "oa": ([128], f4),
    "gs": ([4096], bf), "jb": ([192], f4), "jb1": ([192], f4), "dlw": ([P], f4),
    "cs": ([32], f4), "ci": ([8], i4), "cand": ([80], bf), "cum": ([80], bf), "dvb": ([80], bf), "dv": ([80], bf), "dv1": ([80], f4), "dv2": ([80], f4),
    "sou": ([32], u2), "dl": ([16], f4), "dlu": ([16], u2), "mw": ([16], f4), "nw": ([16], f4),
    "hd": ([P], bf), "wd": ([P], bf), "bta": ([P], bf), "btz": ([P], bf), "inv": ([2, P], bf), "nd": ([2, P], f4), "dvu": ([P], u2),
    "s1": ([P], f4), "s2": ([P], f4), "tt": ([512], f4), "tv": ([P], f4), "em": ([3, P], bf), "made": ([P], bf), "ii": ([P], bf),
    "fv": ([2, P], f4), "fn": ([2, P], f4),
    "prf": ([16], f4), "tr": ([32], f4), "trt": ([32], f4), "d2": ([V], bf),
    "xi": ([256], f4), "gi": ([128], f4), "wt": ([16, 128], bf), "bm": ([3, 144], bf), "idf": ([128], f4),
    "xs": ([80], f4), "pn": ([P], bf), "mt": ([29, 128], bf), "um": ([P], bf), "c768": ([P], bf), "st": ([104], bf), "sw": ([32], bf), "sk": ([4, 8], bf), "g8": ([104], f4), "ex": ([P], bf),
    "tin": ([5, 2, 16], bf), "tin2": ([32], bf), "tct": ([160], bf), "tbt": ([32], bf), "ca": ([P], bf), "cb": ([P], bf), "cc": ([P], bf),
    "ib": ([P], bf), "tb": ([16], f4), "pw": ([16], f4), "pw2": ([16], f4), "ones": ([1024], bf),
}
SCRATCH = {k: ("sbuf", [128] + s, d) for k, (s, d) in SB.items()}
for _k in range(4, 8):
    SCRATCH["ps%d" % _k] = ("psum", [128, 512], "float32")
for _k in (0, 2):
    SCRATCH["ps%d" % _k] = ("psum", [128, 1024], "float32")
NDMA = 48
SEMAPHORES = ["qv", "qa", "qp", "qg", "arr0", "arr1", "out0", "out1", "arr2", "arr3", "out2", "out3"] + ["d%d" % k for k in range(NDMA)]
HOP = 200.0
TRIES = 100
PLANS = {}
DBG = {}
MOVES = 100000
STARTS = 1
FAR = 8
TTG = 1.6
CASES = ((1.0, 1.0, 1.3, 3.0, 30.0, 70.0, 0.45, 170.0, 1.0, 1.0, 0.0), (1.0, 1.0, 1.1, 1.8, 30.0, 70.0, 0.5, 300.0, 1.4, 1.4, 1500.0),
         (1.0, 1.0, 2.05, 5.8, 10.0, 50.0, 0.5, 100.0, 0.8, 0.8, -1500.0), (1.0, 1.0, 1.4, 3.8, 60.0, 100.0, 0.75, 250.0, 1.2, 1.2, 0.0))
PLAIN = ((4, 5), (4, 5))
RV00 = ((0, 0), (0, 0))
RV01 = ((0, 0), (0, 0))
RVAH = ((0, 0), (0, 0))
GU = (32, 64, 64, 32)
GSV = ((1, 3, 5), (1, 3, 5))
PIECES = ((0, 128), (128, 192), (192, 256))
AW = 64
PW = 32
PSX = 0.0
TEMP = 300.0
LOV = (0, 0)
LWV = ((0, 1), (0, 1))
FIRST = 1500.0
WEAVE = 3
BOOST = 4000.0
TAILS = (((0, 256),), ((0, 128), (128, 256)))
WG = ()
ORD1 = ((0, 1), (0, 1))
ORD2 = ((0, 1), (0, 1))
HHA = ((), ())


def rank_program(g, core, T, topo):
    q = T.rank_of(core)
    if q is None:
        return
    N = len(T.cores)
    ops = []
    queue = {"v": g.vector, "a": g.scalar, "p": g.tensor, "g": g, "s": g.sync}

    def R(name, *ix, part=None):
        shape = SCRATCH[name][1][1:]
        ix = list(ix) + [slice(None)] * (len(shape) - len(ix))
        lo = hi = 0
        n = 1
        for d, i in enumerate(ix):
            st = 1
            for s in shape[d + 1:]:
                st *= s
            rg = range(shape[d])[i] if isinstance(i, slice) else range(i, i + 1)
            lo += rg[0] * st
            hi += rg[-1] * st
            n *= len(rg)
        ap = T[name][tuple([part if part is not None else slice(None)] + ix)]
        return (ap, name, lo, hi + 1, n, 2 if SCRATCH[name][2] in (bf, u2) else 4)

    def S(name, a, b, st=1, part=None):
        return R(name, slice(a, b, st), part=part)

    def IND(w, o):
        return (w[0].indirect(o[0]), w[1], w[2], w[3], 16 * o[4], w[5], o)

    def op(eng, fn, cost, rd, wr, lat=0.0, kind="c"):
        rd = [x for x in rd if isinstance(x, tuple)]
        rd = rd + [x[6] for x in rd + wr if len(x) > 6]
        ops.append({"e": eng, "fn": fn, "cost": cost, "lat": lat, "kind": kind,
                    "ng": sum(x[4] for x in rd if len(x) > 6), "ns": sum(x[4] for x in wr if len(x) > 6),
                    "tr": [x[1:4] for x in rd], "tw": [x[1:4] for x in wr],
                    "rd": [x[1:4] for x in rd],
                    "wr": [x[1:4] for x in wr] + [("bank" + x[1], x[2] // 512, (x[3] - 1) // 512 + 1) for x in rd + wr if x[1].startswith("ps")]})

    def ap(x):
        return x[0] if isinstance(x, tuple) else x

    def vcost(o, i, two=False):
        if len(o) > 6:
            return 60 + 3.8 * o[4]
        if len(i) > 6:
            return 60 + (TTG if two else 1.6) * o[4]
        return 30 + max(64, o[4] * (2 if two else 0.5 if o[5] == 2 and i[5] == 2 else 1))

    def ts(o, i, s1, o0, s2=None, o1=None):
        if o1 is None:
            op("v", lambda e: e.tensor_scalar(o[0], i[0], ap(s1), None, o0), vcost(o, i), [i, s1], [o])
        else:
            op("v", lambda e: e.tensor_scalar(o[0], i[0], ap(s1), ap(s2), o0, o1), vcost(o, i), [i, s1, s2], [o])

    def tt(o, a, b, f):
        two = not (a[1].startswith("ps") or b[1].startswith("ps"))
        op("v", lambda e: e.tensor_tensor(o[0], a[0], b[0], f), vcost(o, a, two) if two else 30 + max(64, o[4]), [a, b], [o])

    def cp(o, i):
        op("v", lambda e: e.tensor_copy(o[0], i[0]), vcost(o, i), [i], [o])

    def ms(o, c):
        op("v", lambda e: e.memset(o[0], c), vcost(o, o), [], [o])

    def act(o, i, f=F.Identity, bias=0.0, scale=1.0, acc=None):
        if acc is None:
            op("a", lambda e: e.activation(o[0], i[0], f, bias=ap(bias), scale=ap(scale)),
               70 + o[4] * (1.6 if len(i) > 6 else 1.0), [i, bias, scale], [o])
        else:
            op("a", lambda e: e.activation(o[0], i[0], f, bias=ap(bias), scale=ap(scale), accum_out=acc[0]), 100 + o[4], [i, bias, scale], [o, acc])

    def mm(items, start=True, stop=True):
        def fn(e):
            r = None
            for k, (o, l, x) in enumerate(items):
                r = e.matmul(o[0], l[0], x[0], start and k == 0, stop and k == len(items) - 1)
            return r
        cost = sum(max(min(64, l[4]), x[4]) * (2.0 if x[5] == 4 else 0.5) for o, l, x in items)
        op("p", fn, cost, [x for o, l, x in items] + [l for o, l, x in items], [o for o, l, x in items])

    def iota(o, pat, base, cm, small=True):
        if small:
            op("g", lambda e: e.iota(o[0], pat, base, cm, allow_small_or_imprecise_dtypes=True), 150 + 2 * o[4], [], [o])
        else:
            op("g", lambda e: e.iota(o[0], pat, base, cm), 150 + 2 * o[4], [], [o])

    def dma(o, i, eng="s", lat=2200.0, tag=None):
        w = [(o[0], o[1], o[2] * o[5] // 16 * 16 // o[5], -(-o[3] * o[5] // 16) * 16 // o[5])] if isinstance(o, tuple) else []
        op(eng, lambda e: e.dma_start(ap(o), ap(i)), 80, [i], w, lat=lat, kind="d")
        ops[-1]["tag"] = tag

    (ID, NI, I255, IBIG, ON128, NIH, IA, IZ, IN0, IN1, IK2, IK3, ONES, TRI, A1, NA1, O8192, A3, CV, N8192, P8192, K8, ON17, ON16, NON,
     N255, KD, ON80, IH) = range(29)

    def M(k, n=128, m=None):
        return R("mt", k, slice(0, n if m is None else m), part=slice(0, n))

    def W(kind, r):
        return R("bm", kind, slice(15 - r, 143 - r))
    P8, WS, W256 = 0, 1, 2
    G8 = S("st", 0, 8)

    def col(k):
        return S("cs", k, k + 1)
    PC, FC, GC, G15, PWC, RC, MA, MZ, WSC, TH, UO = [col(k) for k in range(11)]
    WB = S("wb", 0, 1)

    def ps(k, a=0, b=512, st=1, n=None):
        if k in (1, 3):
            k, a, b = k - 1, a + 512, b + 512
        return S("ps%d" % k, a, b, st, part=None if n is None else slice(0, n))

    def chunks_of(t):
        return list(zip(CUT, CUT[1:] + (KB + 16 * t,)))

    def dk(k, n):
        return R("dkt", k, part=slice(0, n))

    for h in range(2):
        dma(S("eni", KB * h, KB * h + KB), T.en0[h::2, :], eng="sa"[h], lat=2500.0, tag="e")
        ops[-1]["lead"] = 9000.0
    dma(S("sni", 0, 21), T.snd[:, :], lat=2400.0)
    ops[-1]["lead"] = 9000.0
    yn = lambda a, b: S("win", YN + a, YN + b)
    XS = lambda t, a, b: S("win", XA + a, XA + b) if t == 0 else S("xb", a, b)
    dma(yn(0, B // 2), T.y0[:, 0:B // 2], lat=3000.0, tag="y")
    dma(yn(B // 2, B), T.y0[:, B // 2:B], eng="a", lat=3400.0, tag="y")
    dma(XS(0, 0, V), T.x0[:, :], lat=3600.0)
    for k, j in ((2, 0), (3, 2), (4, 1), (5, 3)):
        ops[k]["after"] = [j]

    iota(R("xi"), [[1, 256]], 0, 0)
    iota(S("ci", 0, 1), [[0, 1]], 0, 1, small=False)
    iota(R("gi"), [[1, 8], [0, 16]], 0, 0)
    iota(R("g8"), [[0, 13], [1, 8]], 0, 0)
    ms(R("ones"), 1.0)
    for h in (0, 8):
        op("g", lambda e, h=h: e.affine_select(T.wt[:, h:h + 8], T.ones[:], [[-1, 8], [-16, 8], [0, 16]], A.is_equal, 0.0, -h, 1), 2250,
           [R("ones")], [R("wt", slice(h, h + 8))])
    iota(R("ib"), [[1, P]], 0, 0)
    cp(PC, S("ci", 0, 1))
    ts(S("ci", 1, 2), S("ci", 0, 1), 15, A.bitwise_and)
    ts(S("ci", 2, 3), S("ci", 0, 1), 4, A.arith_shift_right)
    cp(S("cs", 1, 3), S("ci", 1, 3))
    ts(G15, GC, 16.0, A.mult, 15.0, A.add)
    x144, x8 = S("xi", 0, 144), S("xi", 0, 8)
    ts(R("bm", P8), x144, G15, A.is_equal, 8.0, A.mult)
    ts(M(ONES), R("gi"), GC, A.is_equal)
    ts(M(ID), S("xi", 0, 128), PC, A.is_equal)
    op("g", lambda e: e.affine_select(M(TRI)[0], M(ONES)[0], [[1, 128]], A.is_gt, 0.0, 0, -1), 430, [M(ONES)], [M(TRI)])
    act(R("bm", W256), R("bm", P8), scale=32.0)
    ts(R("tb"), S("xi", 0, 16), FC, A.is_equal)
    ts(S("owt", 128, 136), x8, GC, A.is_equal)
    ts(R("st"), R("g8"), GC, A.is_equal, 8.0, A.mult)
    for a, b, c in ((1, 2, 0.0), (2, 3, -1.0), (4, 5, -1.0), (8, 11, -1.0), (11, 12, 0.0))[:5 if any(RV00[0] + RV00[1] + RV01[0] + RV01[1]) else 3]:
        act(S("st", 8 * a, 8 * b), S("st", 8 * a, 8 * b), scale=c)
    for k, c in enumerate((64.0, 80.0, 16.0, 1.0 / 16)):
        act(R("sk", k), G8, scale=c)
    act(S("s2", 0, 192), S("xi", 0, 192), bias=FC, scale=16.0)
    act(R("nw"), S("s2", 0, 16), bias=float(V))
    ts(col(18), FC, 14.5, A.is_lt)
    ts(S("ci", 3, 4), S("ci", 0, 1), 16, A.bitwise_and)
    cp(col(19), S("ci", 3, 4))
    ms(R("tin2"), 512.0)
    act(R("jb1"), S("s2", 0, 192), bias=float(Y1 - LO))
    act(R("jb"), S("s2", 0, 192), bias=float(Y0 - LO))
    act(M(NIH), M(ID), scale=-0.5)
    act(M(IH), M(ID), scale=0.5)
    act(M(K8), M(ID), scale=-1.0, bias=64.0)
    act(R("idf"), M(ID))
    for m, c in ((O8192, 8192.0), (ON16, 16.0), (ON17, 17.0), (NON, -1.0), (ON128, -128.0), (ON80, 80.0)):
        act(M(m), M(ONES), scale=c)
    tt(M(A3), M(ID), M(TRI), A.subtract)
    act(M(A3), M(A3), scale=262144.0)
    tt(M(A1), M(A3), M(O8192), A.subtract)
    act(M(NA1), M(A1), scale=-1.0)
    ms(R("pw2"), 2.0)
    ms(R("prf"), 0.0)
    op("v", lambda e: e.tensor_tensor_scan(T.pw[:], T.pw2[:], T.prf[:], 0.5, A.mult, A.add), 100, [R("pw2"), R("prf")], [R("pw")])
    tt(R("pw"), R("pw"), R("tb"), A.mult)
    op("v", lambda e: e.tensor_reduce(PWC[0], T.pw[:], AX.X, A.add), 100, [R("pw")], [PWC])
    ts(MA, FC, 7.5, A.is_lt, 0.25, A.mult)
    ts(MZ, FC, 7.5, A.is_gt, 0.25, A.mult)
    ts(col(11), PWC, MA, A.mult, -16.0, A.mult)
    ts(col(13), PWC, MZ, A.mult, 1.0 / 16, A.mult)
    ts(S("sw", 0, 8), x8, GC, A.is_equal, col(11), A.mult)
    ts(S("sw", 8, 16), x8, GC, A.is_equal, col(13), A.mult)
    act(S("sw", 16, 32), S("sw", 0, 16), scale=-1.0)
    ts(col(12), MZ, 1020.0, A.mult, 1.0, A.add)
    op("v", lambda e: e.reciprocal(RC[0], PWC[0]), 200, [PWC], [RC])
    ts(RC, RC, col(12), A.mult, 0.5, A.mult)
    act(R("s1"), R("xi"), bias=-0.5 + 2.0 ** -10, scale=RC)
    ts(R("tv"), R("s1"), MAG, A.add, -MAG, A.add)
    tt(R("made"), R("tv"), R("s1"), A.is_lt)
    act(R("bta"), R("made"), scale=MA)
    act(R("btz"), R("made"), scale=MZ)
    ts(R("bm", WS), x144, G15, A.is_equal, S("tb", 0, 1), A.mult)
    ms(S("win", 0, 16), 0.0)
    ms(S("lw", V, V + 128), 0.0)
    for k in range(4):
        act(col(24 + k), (MA, MZ)[k % 2], scale=-1.0, bias=float(DELTA[k // 2]))
    ms(S("e1", KB, 192), 0.0)
    ms(S("e1", 192 + KB, 384), 0.0)

    sn = lambda k: S("snf", 24 * k, 24 * k + 21)
    nlow = 3 * (N - 1 - q)
    ts(sn(4), S("xi", 0, 21), nlow - 0.5, A.is_gt, float(KB), A.mult)
    ts(sn(5), S("xi", 0, 21), nlow - 0.5, A.is_gt, 192.0 - KB, A.mult)
    ts(S("snu", 24, 45), S("sni", 0, 21), 1.0 / KB, A.mult, -0.5 + 0.5 / KB, A.add)
    tt(sn(4), sn(4), S("sni", 0, 21), A.add)
    ts(sn(2), S("snu", 24, 45), -float(KB), A.mult)
    tt(sn(2), sn(2), sn(4), A.add)
    cp(S("snu", 0, 21), sn(2))
    tt(sn(5), sn(5), sn(2), A.add)
    cp(S("snu", 48, 69), sn(5))
    act(R("mk"), IND(R("tb"), S("snu", 24, 45)))
    for k, (c0, c1) in enumerate(chunks_of(0)):
        n = c1 - c0
        pb = (7, 5)[k % 2]
        mm([(ps(pb, r, 128, 16, n=n), yn(KB * r + c0, KB * r + c1), G8) for r in range(16)])
        ts(dk(k, n), ps(pb, 0, 128, n=n), 1407.5, A.is_lt, EPS, A.add)
    for h in range(2):
        cp(S("e0", 192 * h, 192 * h + KB), S("eni", KB * h, KB * h + KB))
    cp(R("eu", slice(None), slice(0, KB)), R("eni"))
    dma(R("bli"), T.bl0[:, :], lat=3000.0)
    ops[-1]["rd"].append(dk(0, 1)[1:4])
    for r in range(16):
        o, i = S("win", Y0 + r, Y0 + B, 16), yn(KB * r, KB * r + KB)
        if r in WG:
            op("g", lambda e, o=o, i=i: e.affine_select(o[0], i[0], [[0, KB]], A.is_ge, 0.0, 0, 0), 520, [i], [o])
        else:
            (cp if r % WEAVE == 1 else act)(o, i)
        ops[-1]["tag"] = "weave"
    cp(S("bl", 0, V), R("bli"))
    ts(R("d2"), yn(0, V), 1028.5, A.add)

    def own_cells(t):
        tt(R("gm"), IND(R("eni") if t == 0 else R("e1"), S("snu", 48 * t, 48 * t + 21)), R("mk"), A.mult)
        pb = 2 if t == 0 else 5
        mm([(ps(pb, r, 128, 16, n=21), S("gm", r, GH, 16), S("owt", 128, 136)) for r in range(16)])
        act(S("owt", 0, 128, part=slice(0, 21)), ps(pb, 0, 128, n=21))
        mm([(ps(pb, 0, 21), S("owt", 0, 128, part=slice(0, 21)), S("idf", 0, 21, part=slice(0, 21)))])
        K = 64 + 16 * t
        own = ps(pb, 0, 21)
        cp(S("ow", 0, 21), own)
        ts(S("ow", 24, 45), own, 1.0 / K, A.mult, -0.5 + 0.5 / K, A.add)
        ts(sn(2), S("ow", 24, 45), -float(K), A.mult)
        tt(sn(3), own, sn(2), A.add)
        cp(S("ow", 48, 69), sn(3))
        act(R("mk2"), IND(R("tb"), S("ow", 24, 45)))
        act(R("sx%d" % t), IND(XS(t, 0, V + P * t), S("ow", 0, 21)))
        send("sx%d" % t, "lx%d" % t, 2 + t)
        dl = float(DELTA[t])
        for h, H in enumerate((HA, HZ)):
            ts(S("win", H + C, H + CW), R("lx%d" % t), 63.0 - dl, A.min, col(24 + 2 * t + h), A.add)
        act(R("flo"), R("lx%d" % t), F.Abs, bias=-31.5)

    def send(sb, land, k):
        def fn(e):
            trs = []
            for d in range(1, N):
                dst = T.cores[(q + d) % N]
                rid, pid, _ = topo.addr(dst)
                en = topo.engines(core, dst)
                mask = (1 << en[2 * (d - 1)]) | (1 << en[2 * (d - 1) + 1])
                trs.append(RemoteDMATransfer(dst_ids=[DstId(rid=rid, pnc=pid)], dma_engine_mask=mask, remote_sem=T.sem["arr%d" % k],
                                             src=T[sb][:, 48 * (d - 1):48 * d], dst=T[land][:, 48 * (N - 1 - d):48 * (N - d)]))
            e.remote_dma_fused(trs, local_sem=T.sem["out%d" % k])
        op("g", fn, 300 + FIRST * (k == 2), [R(sb)], [R(land)], lat=2500.0, kind="r%d" % k)

    def banks_of(t):
        rb = 8 if t == 0 else 6
        return [(r0, min(16, r0 + rb)) for r0 in range(0, 16, rb)]

    def cell_sums(t):
        K, Ct = 64 + 16 * t, V + P * t
        act(S("ax", 0, Ct), XS(t, 0, Ct), F.Abs, bias=-31.5)
        pb = 6 + t
        mm([(ps(pb, 0, K), W(P8, r), XS(t, K * r, K * r + K)) for r in range(16)])
        if t == 0:
            act(S("xs", 0, K), ps(pb, 0, K), scale=(1 - EPS) / 8, bias=(0.5 - 8.0 * THETA[0] - 4 * 8320.0) * (1 - EPS) / 8 - B)
        else:
            act(S("xs", 0, K), ps(pb, 0, K), bias=0.5 - 124.0 - 8.0 * THETA[1] - 4 * 8320.0)

    def cell_preload(t, ks=(0, 1)):
        K = 64 + 16 * t
        for k in ks:
            r0, r1 = banks_of(t)[k]
            w = (r1 - r0) * K
            mm([(ps(k, 0, w), M(NIH), XS(t, K * r0, K * r1))], stop=False)
            mm([(ps(3 + k, 0, w), M(IH), S("ax", K * r0, K * r1))], stop=False)

    def old_live(u):
        o = ps(7, 384, 512)
        mm([(o, M(ID), M(O8192))], stop=False)
        mm([(o, S("ones", 0, 128, part=slice(0, c1 - c0)), dk(k, c1 - c0)) for k, (c0, c1) in enumerate(chunks_of(0))], start=False)
        act(S("tt", 0, 128), o, F.Relu, bias=-8192.0, acc=col(15))
        if u is TH:
            ts(WB, col(15), -2.0 / (1 - EPS), A.mult, 8320.0 - 31.0 + 2.0 * B / (1 - EPS), A.add)
            ts(S("xs", 0, 64), S("xs", 0, 64), col(15), A.add, -2.0 / (1 - EPS), A.mult)
        else:
            ts(u, col(15), 8.0 / (1 - EPS), A.mult, 124.0 - 8.0 * B / (1 - EPS), A.add)

    own_cells(0)
    cell_sums(0)
    cell_preload(0)
    old_live(TH)
    for m, c in ((NI, -1.0), (IBIG, 131072.0), (IK2, -16384.0), (N8192, -8192.0), (IK3, -24576.0), (IA, float(HA - LO)), (IZ, float(HZ - LO)), (I255, 255 / 512),
                 (N255, -255 / 512), (IN0, float(V)), (IN1, float(V + P)), (KD, 255.0), (P8192, 8192.0), (CV, -33.0 * 2 ** 19)):
        if m != N255 or any(RVAH[0] + RVAH[1]):
            op("g", lambda e, m=m, c=c: e.affine_select(M(m)[0], T.lw[:, V:V + 128], [[-1, 128]], A.not_equal, c, 0, 1), 430,
               [S("lw", V, V + 128), R("sx0")], [M(m)])
    late = []
    for t in range(2):
        Ct, K, NC = V + P * t, 64 + 16 * t, KB + 16 * t
        n0, dl = V + P * t, float(DELTA[t])
        E, En = "e%d" % t, "e%d" % (t + 1)
        YB = Y0 if t == 0 else Y1
        ts(S("cand", 0, K), S("xs", 0, K), WB, A.is_lt)
        op("v", lambda e, K=K: e.tensor_tensor_scan(T.cum[:, 0:K], T.ones[:, 0:K], T.cand[:, 0:K], 0.0, A.mult, A.subtract), 100,
           [S("ones", 0, K), R("cand")], [R("cum")])
        ts(S("dv2", 0, K), S("cand", 0, K), -1024.0, A.mult, 767.5, A.add)
        off, cnt = ps(7, 300, 301), ps(7, 301, 302)
        mm([(off, M(TRI), S("cum", K - 1, K)), (cnt, M(NON), S("cum", K - 1, K))])
        tt(S("dv1", 0, K), S("dv2", 0, K), S("cum", 0, K), A.subtract)
        ts(S("dv", 0, K), S("dv1", 0, K), off, A.is_lt, dl / 2, A.mult)
        tt(R("sb%d" % t), IND(S("dv", 0, K), S("ow", 48, 69)), R("mk2"), A.mult)
        send("sb%d" % t, "land%d" % t, t)
        ts(S("dvb", 0, K), S("dv1", 0, K), off, A.is_lt, -64 * dl, A.mult)
        ts(S("cs", 28, 30), ps(7, 300, 302), -1.0, A.mult)

        def low(o, p, on_v):
            if on_v:
                ts(o, p, -1.0, A.mult, 0.0, A.max)
            else:
                act(o, p, F.Relu, scale=-1.0)

        def width(o, p, on_v):
            if on_v:
                ts(o, p, 64.5 * dl - 15.75, A.add, 0.0, A.max)
            else:
                act(o, p, F.Relu, bias=64.5 * dl - 15.75)
        for k, (r0, r1) in enumerate(banks_of(t)):
            w = (r1 - r0) * K
            for kk_, nm in ((k, "dv"), (3 + k, "dvb")):
                mm([(ps(kk_, K * (r - r0), K * (r - r0 + 1)), R("wt", r), S(nm, 0, K)) for r in range(r0, r1)], start=False)
            low(S("lw", K * r0, K * r1), ps(k, 0, w), False)
            width(S("lw", CW + K * r0, CW + K * r1), ps(3 + k, 0, w), k in LWV[t])
        sb, land = "sb%d" % t, "land%d" % t
        nk = K // 16
        place = lambda o, i: act(o, i, scale=-1.0, bias=col(28))
        for h in range(2):
            place(R("tin", slice(0, nk), h), S("cum", 0, K))
            place(S("tin2", 16 * h, 16 * h + nk - 1), S("cum", 15, K - 1, 16))
        place(col(17), S("cum", K - 1, K))
        act(R("ex"), R("ib"), F.Relu, bias=col(29))
        ts(R("inv", t), R("ib"), cnt, A.is_ge, 2.0 ** -7, A.add)
        if t == 1:
            late[0]()
            iota(S("lw", CW + Ct, CW + C), [[0, C - Ct]], DELTA[1], 0)
        f0, f1 = ps(2, 0, GH), ps(5, 0, GH)
        mm([(f0, M(NIH), R("lx%d" % t))], stop=False)
        mm([(f1, M(IH), R("flo"))], stop=False)
        mm([(f0, M(ONES), R(land))], start=False)
        mm([(f1, M(ON128), R(land))], start=False)
        low(S("lw", C, CW), f0, True)
        width(S("lw", CW + C, 2 * CW), f1, False)
        if t == 0:
            for nm, a, b, st, v in (("lw", V + 128, C, 0, 0), ("lw", CW + V, CW + C, 0, DELTA[0]), ("win", LO + V, LO + C, 0, 0), ("win", HZ + V, HZ + C, 0, 0), ("bl", V, C, 0, -1), ("yon", 0, ZB, 0, 0),
                                    ("tu", B, NB + 16, 0, 0), ("win", HZ + CW, YN, 0, 0), ("ii", 0, P, 1, -128),
                                    ("c768", 0, 128, 0, -768), ("c768", 128, 256, 0, 768)):
                iota(S(nm, a, b), [[st, b - a]], v, 0)
                ops[-1]["rd"].append(R(sb)[1:4])
        for a, b in ((0, Ct // 2), (Ct // 2, Ct), (C, CW)):
            if LOV[t]:
                ts(S("win", LO + a, LO + b), S("lw", a, b), 2.0, A.mult)
            else:
                act(S("win", LO + a, LO + b), S("lw", a, b), scale=2.0)
        op("v", lambda e, nk=nk: e.transpose(T.tct[:, 0:32 * nk], T.tin[:, 0:nk]), 30 + 16 * nk, [R("tin")], [R("tct")])
        op("v", lambda e: e.transpose(T.tbt[:], T.tin2[:]), 94, [R("tin2")], [R("tbt")])
        ts(R("ca"), R("ib"), col(17), A.is_ge, col(18), A.mult)
        pa_ = ps(7, 0, 16)
        mm([(pa_, W(P8, r), S("ca", r, P, 16)) for r in range(16)])
        ts(S("sou", 0, 16), pa_, 0.125, A.mult, col(19), A.add)
        mm([(pa_, W(P8, r), S("ca", r, P, 16)) for r in range(16)], stop=False)
        tt(R("cb"), IND(R("tbt"), S("sou", 0, 16)), R("ib"), A.is_le)
        mm([(pa_, W(W256, r), S("cb", r, P, 16)) for r in range(16)], start=False)
        ts(S("sou", 16, 32), pa_, 0.125, A.mult, col(19), A.add)
        tt(R("cc"), IND(S("tct", 0, 32 * nk), S("sou", 16, 32)), R("ib"), A.is_le)
        mm([(ps(7, 128 + r, 256, 16, n=16), S(nm, r, P, 16), w_) for nm, w_ in (("ca", R("sk", t)), ("cb", R("sk", 2)), ("ex", R("sk", 3)), ("cc", G8))
            for r in range(16)])
        act(S("owt", 0, 128, part=slice(0, 16)), ps(7, 128, 256, n=16), scale=0.125)
        mm([(pa_, S("owt", 0, 128, part=slice(0, 16)), S("idf", 0, 16, part=slice(0, 16)))])
        cp(R("dlu"), pa_)
        if t == 0:
            act(R("dl"), pa_)
        act(R("wd"), IND(S("lw", CW, CW + C), R("dlu")), scale=-2.0, bias=2 * dl)
        tt(R("hd"), IND(S("win", LO, LO + C), R("dlu")), R("wd"), A.add)
        act(R("nd", 1), IND(R("bl"), R("dlu")))
        ts(R("dvu"), R("nd", 1), 8.0, A.add)
        tt(IND(S("win", HA, HA + C), R("dlu")), R("hd"), R("bta"), A.add)
        tt(IND(S("win", HZ, HZ + C), R("dlu")), R("hd"), R("btz"), A.add)
        ops[-1]["lead"] = ops[-2]["lead"] = BOOST
        iota(R("nd", 0), [[1, P]], B + P * t, 0)
        ops[-1]["rd"].append(R(sb)[1:4])
        if t == 1:
            dma(T.yx[:, 0:Ct], S("win", LO, LO + Ct))
            dma(T.yx[:, Ct:C], R("hd"))
        if t == 0:
            for a, b in ((0, 512), (512, V)):
                mm([(ps(7), M(ID), S("win", LO + a, LO + b)), (ps(7), M(ID), yn(a, b)), (ps(7), M(NI), S("d2", a, b))])
                act(S("xb", a, b), ps(7), F.Relu, bias=1029.0)
            o = ps(7, 0, P)
            mm([(o, M(ID), R("hd")), (o, M(ID), yn(0, P)), (o, M(NI), S("d2", 0, P)), (o, M(N8192), R("inv", 0))])
            act(S("xb", V, V + P), o, F.Relu, bias=1093.0)
            ts(R("xb"), R("xb"), 63.0, A.min)
            cell_sums(1)
            mm([(ps(7, P, 2 * P), M(ONES), R("wd"))])
            ts(R("pn"), ps(7, P, 2 * P), 175.5, A.is_lt, -1024.0, A.mult)

        chunks = chunks_of(t)
        loh, wh = S("lw", 0, CW), S("lw", CW, 2 * CW)
        awin, zwin = S("win", LO, Y1 if t == 0 else WEND), S("win", 0, HZ + CW)
        U = lambda nm, a, b: S(nm, 16 * a, 16 * b)
        EU = lambda h, a, b: R("eu", h, slice(a, b))
        rot = [0]

        def units(c0, c1, w=32):
            return [(a, min(c1, a + w)) for a in range(c0, c1, w)]

        def bank(w):
            if w > 512:
                rot[0] += rot[0] % 2 + 2
                return ps(rot[0] % 4, 0, w)
            rot[0] += 1
            return ps((rot[0] + 1) % 4, 0, w)

        def adds(a, b, terms):
            p = bank(16 * (b - a))
            for x, y in units(a, b):
                mm([(S(p[1], p[2] + 16 * (x - a), p[2] + 16 * (y - a)), M(m), S(nm, o + 16 * x, o + 16 * y)) for m, nm, o in terms])
            return p

        def relu2(o, i, on_v):
            if on_v:
                ts(o, i, 0.0, A.max, 2.0, A.mult)
            else:
                act(o, i, F.Relu, scale=2.0)

        def phase1(k):
            c0, c1 = chunks[k]
            n, sc = c1 - c0, 5 - k % 2
            plain = lambda a: a // 32 in PLAIN[t]
            d_ = dk(len(CUT) if t == 1 and k == len(CUT) - 1 else k, n)
            mm([(ps(sc, 128 * j, 128 * j + 128, n=n), M(m, n), d_) for j, m in enumerate((IBIG, IK2, N8192, IK3))], stop=False)

            def sums(nm, k0, k1, w0, stop=False):
                mm([(ps(sc, 128 * k0 + r, 128 * k1, 16, n=n), S(nm, 16 * c0 + r, 16 * c1, 16), S("st", 8 * w0, 8 * (w0 + k1 - k0)))
                    for r in range(16)], start=False, stop=stop)
            big = units(c0, c1, GU[1])
            if k == ORD1[t][0]:
                big = units(c0, min(c1, c0 + GU[1]), GU[0]) + big[1:]
            for a, b in big:
                tt(U("tu", a, b), IND(loh, EU(0, a, b)), S("win", YB + 16 * a, YB + 16 * b), A.subtract)
                act(U("wa", a, b), IND(wh, EU(0, a, b)))
                tt(U("t00", a, b), IND(loh, EU(1, a, b)), U("tu", a, b), A.add)
                for a, b in [(a, b)] if plain(a) == plain(b - 1) else units(a, b):
                    if plain(a):
                        act(U("t01", a, b), IND(wh, EU(1, a, b)))
                    else:
                        tt(U("t01", a, b), IND(wh, EU(1, a, b)), U("t00", a, b), A.subtract)
            for a, b in units(c0, c1, AW):
                if RV00[t][k]:
                    relu2(U("r00", a, b), U("t00", a, b), a - c0 < 32 * RV00[t][k])
                else:
                    act(U("r00", a, b), U("t00", a, b), F.Abs)
                for a, b in [(a, b)] if plain(a) == plain(b - 1) else units(a, b):
                    if not plain(a):
                        act(U("r01", a, b), U("t01", a, b), F.Abs, bias=-dl)
            for a, b in units(c0, c1, PW):
                act(U("r10", a, b), adds(a, b, ((ID, "t00", 0), (NI, "wa", 0))), F.Abs, bias=dl)
                for a, b in [(a, b)] if plain(a) == plain(b - 1) else units(a, b):
                    if plain(a):
                        act(U("r01", a, b), adds(a, b, ((ID, "t00", 0), (NI, "t01", 0))), F.Abs, bias=dl)
                    act(U("r11", a, b), adds(a, b, ((NI, "t00", 0),) * plain(a) + ((ID, "t01", 0), (ID, "wa", 0))), F.Abs, bias=-2 * dl)
            if RV00[t][k]:
                sums("t00", 1, 4, 8)
            sums("r00", 1, 4, 5)
            sums("r01", 0, 3, 0)
            sums("r10", 0, 2, 3)
            sums("r11", 3, 4, 2, stop=True)

        def decide(k):
            c0, c1 = chunks[k]
            n, sc = c1 - c0, 5 - k % 2
            pn_ = slice(0, n)
            oa, oz = ps(6, 256, 256 + n), ps(6, 384, 384 + n)
            mm([(oa, R("idf"), S(E, c0, c1)), (oz, R("idf"), S(E, 192 + c0, 192 + c1))], stop=False)
            act(S("rr", 0, 256, part=pn_), ps(sc, 128, 384, n=n), F.Relu)
            tt(ps(6, 0, 128, n=n), ps(sc, 384, 512, n=n), S("rr", 128, 256, part=pn_), A.max)
            tt(ps(6, 128, 256, n=n), ps(sc, 384, 512, n=n), S("rr", 0, 128, part=pn_), A.max)
            act(S("ut", 0, 128, part=pn_), ps(sc, 0, 128, n=n), F.Relu, bias=-8.0 * (9600, 12000)[t])
            tt(R("ppt", k, part=pn_), ps(6, 0, 256, n=n), S("rr", 0, 256, part=pn_), A.is_gt)
            pz, pa, ut = R("ppt", k, slice(0, 128), part=pn_), R("ppt", k, slice(128, 256), part=pn_), S("ut", 0, 128, part=pn_)
            mm([(oa, ut, M(ID, n)), (oz, ut, M(NI, n))], start=False, stop=False)
            mm([(oa, pa, M(IA, n)), (oz, pz, M(IZ, n))], start=False)
            tt(S("oa", 0, n), oa, S("jb" if t == 0 else "jb1", c0, c1), A.min)
            cp(S("ofs", c0, c1), S("oa", 0, n))
            ts(S("ofs", 192 + c0, 192 + c1), oz, 16.0, A.add)

        def phase2(k):
            c0, c1 = chunks[k]
            n, sc = c1 - c0, 5 - k % 2
            GA, DD, HH, AH = "r00", "r01", "r10", "r11"
            big = units(c0, c1, GU[2])
            if k == ORD2[t][0]:
                big = units(c0, min(c1, c0 + GU[2]), 32) + big[1:]
            else:
                big = big[:-1] + units(big[-1][0], c1, GU[3])
            for a, b in big:
                act(U(GA, a, b), IND(awin, S("ofs", a, b)))
                tt(U(DD, a, b), IND(zwin, S("ofs", 192 + a, 192 + b)), U(GA, a, b), A.subtract)
                if a // 32 in HHA[t]:
                    act(U(HH, a, b), U(DD, a, b), bias=192.0)
                else:
                    ts(U(HH, a, b), U(DD, a, b), 192.0, A.add)
            onv = lambda a: False
            for a, b in big if k == ORD2[t][-1] else units(c0, c1, AW):
                act(U(AH, a, b), U(HH, a, b), F.Abs, bias=-192.0)
            mm([(ps(sc, 128, 384, n=n), M(KD, n), S("c768", 0, 256, part=slice(0, n)))] + [(ps(sc, 128 + r, 384, 16, n=n), S(nm, 16 * c0 + r, 16 * c1, 16), S("sw", w0, w0 + 16)) for nm, w0 in ((DD, 0), (HH, 16)) for r in range(16)])
            act(S("nnt", 0, 256, part=slice(0, n)), ps(sc, 128, 384, n=n))
            ys = lambda r, m=n: ps(9 - sc if k == ORD2[t][-1] else sc, r, 128, 16, n=m)

            def woven(a, b, o):
                ts(o, adds(a, b, ((I255, "win", YB), (I255, AH, 0))), MAG, A.add, -MAG, A.add)
            if t == 0:
                for a, b in big if k == ORD2[t][-1] else units(c0, c1, PW):
                    woven(a, b, S("win", Y1 + 16 * a, Y1 + 16 * b))
                mm([(ys(r), S("win", Y1 + 16 * c0 + r, Y1 + 16 * c1, 16), S("st", 0, 8)) for r in range(16)])
            else:
                cb = min(c1, KB)
                m = cb - c0
                rb = 8 if m <= 64 or PW > 32 and m == 128 else 4
                if cb < c1:
                    woven(cb, c1, S("yon", ZB, ZB + P))
                    mm([(ys(r), S("yon", r, 16 * n, 16), S("st", 0, 8)) for r in range(16)], stop=False)
                for r0 in range(0, 16, rb):
                    p = bank(rb * m)
                    its = []
                    for r in range(r0, r0 + rb):
                        oo = S(p[1], p[2] + m * (r - r0), p[2] + m * (r - r0 + 1))
                        its += [(oo, M(I255), S("win", Y1 + 16 * c0 + r, Y1 + 16 * cb, 16)), (oo, M(I255), S(AH, 16 * c0 + r, 16 * cb, 16))]
                    for x in range(0, 2 * rb, 2 * min(rb, 512 // m)):
                        mm(its[x:x + 2 * min(rb, 512 // m)])
                    ts(R("yo", slice(r0, r0 + rb), slice(c0, cb)), p, MAG, A.add, -MAG, A.add)
                    mm([(ys(r, m), R("yo", r, slice(c0, cb)), S("st", 0, 8)) for r in range(r0, r0 + rb)], start=r0 == 0 and cb == c1, stop=r0 + rb == 16)

        def post(k):
            c0, c1 = chunks[k]
            n, sc = c1 - c0, 5 - k % 2
            pn_ = slice(0, n)
            na, nz = S("nnt", 0, 128, part=pn_), S("nnt", 128, 256, part=pn_)
            pz, pa = R("ppt", k, slice(0, 128), part=pn_), R("ppt", k, slice(128, 256), part=pn_)
            IN = IN0 if t == 0 else IN1
            rr = lambda h: ps(6, 256 + 128 * h, 256 + 128 * h + n)
            mm([(rr(0), pa, M(IN, n)), (rr(1), pz, M(IN, n)), (rr(0), na, M(ID, n)), (rr(1), nz, M(ID, n))])
            for h in range(2):
                ne = S(En, 192 * h + c0, 192 * h + c1)
                tt(ne, rr(h), S(E, 192 * h + c0, 192 * h + c1), A.max)
                if t == 0:
                    cp(EU(h, c0, c1), ne)
            cd = ps(sc if k == ORD2[t][-1] else 6, 0, n)
            mm([(cd, pa, M(KD, n)), (cd, pz, M(KD, n)), (cd, na, M(ID, n)), (cd, nz, M(ID, n))], stop=False)
            ts(dk(k, n), ps(9 - sc if k == ORD2[t][-1] else sc, 0, 128, n=n), 1407.5, A.is_lt, EPS, A.add)
            mm([(cd, dk(k, n), M(N8192, n))], start=False)
            act(S("cod", c0, c1), cd, bias=-382.0)

        for k in ORD1[t]:
            phase1(k)
            decide(k)
        for k in ORD2[t]:
            phase2(k)
            post(k)
        iota(S("tu", 0, 8), [[0, 8]], -8192, 0)
        dma(S("tu", 8, 8 + B, part=slice(0, 128, 16)), S("cod", 0, KB))

        if t == 0:
            own_cells(1)
            cell_preload(1, (0, 1))
            old_live(UO)
        else:
            mm([(ps(0, r, P, 16), R("wt", r), S("cod", KB, NC)) for r in range(16)])
            act(S("tu", 8 + B, 8 + B + P), ps(0, 0, P))
            dma(T.yy[:, 0:B], R("yo"))
            ops[-1]["rd"].append(S("tu", 16, 32)[1:4])
            for h in range(2):
                dma(T.ye[h::2, 0:B], S("e2", 192 * h, 192 * h + KB))
                ops[-1]["rd"].append(S("tu", 16, 32)[1:4])
                cp(S("tr", 16 * h, 16 * h + 16), S("e2", 192 * h + KB, 192 * h + NC))
            op("v", lambda e: e.transpose(T.trt[:], T.tr[:]), 100, [R("tr")], [R("trt")])
            for a in range(4):
                for gp in range(2):
                    dma(T.ye[4 * a + 2 * gp:4 * a + 2 * gp + 2, B:B + P], S("trt", 16 * gp, 16 * gp + 16, part=slice(32 * a, 32 * a + 32)))
                    ops[-1]["rd"].append(S("tu", 16, 32)[1:4])
        iw = R("tu")
        EM = lambda x, a, b: R("em", x, slice(a, b))
        for pb, (a, b) in zip((6, 7, 2 + 4 * t), PIECES):
            oo = ps(pb, 0, b - a)
            for k in range(a // 64, b // 64):
                for u in (2 * k, 2 * k + 1):
                    (cp if u in GSV[t] else act)(S("gs", 512 * u, 512 * u + 512), IND(iw, S("dvu", 32 * u, 32 * u + 32)))
                mm([(ps(pb, 64 * k - a, 64 * k - a + 64), W(WS, s), S("gs", 1024 * k + s, 1024 * k + 1024, 16)) for s in range(16)],
                   start=k == a // 64, stop=k == b // 64 - 1)
            tt(EM(0, a, b), oo, S("ii", a, b), A.is_equal)
            ts(EM(1, a, b), oo, 127.5, A.is_gt)
            ts(EM(2, a, b), oo, -2000.0, A.is_lt)
            if t == 0:
                h = a // 128
                g2, g3 = lambda a, b: ps(5, a % 128, a % 128 + b - a), lambda a, b: ps(5, 128 + a % 128, 128 + a % 128 + b - a)
                if a % 128 == 0:
                    mm([(g2(a, a + 128), M(ID), S("pn", a, a + 128)), (g3(a, a + 128), M(NI), S("pn", a, a + 128)),
                        (g3(a, a + 128), M(ONES), S("ones", 0, 128))], stop=False)
                for x in range(2):
                    mm([(g2(a, b), M(ONES), EM(x, a, b)), (g3(a, b), M(NON), EM(x, a, b))], start=False, stop=False)
                mm([(g2(a, b), M(ONES), EM(2, a, b))], start=False, stop=b % 128 == 0)
                if b % 128 == 0:
                    act(S("tt", 0, 256), ps(5, 0, 256), F.Sign, bias=-0.5, acc=col(22 + h))
                    if h:
                        ts(WB, col(23), col(20), A.add)
                        ts(R("xs"), R("xs"), col(23), A.add)
                    else:
                        ts(UO, col(22), -4.0, A.mult, UO, A.add)
                        ts(col(20), UO, -0.25, A.mult, 8320.0, A.add)
                        ts(R("xs"), R("xs"), UO, A.add, -0.25, A.mult)
        if t == 0:
            cell_preload(1, (2,))

        def slot_tail(t=t, n0=n0):
            for x, (a, b) in enumerate(TAILS[t]):
                w = b - a
                bv, bn, bg = (4, 4, 6) if t == 0 else (x % 2, 2 + x % 2, 4 + x % 2)
                e0, e1, e2, on = EM(0, a, b), EM(1, a, b), EM(2, a, b), S("ones", 0, w)
                f, fk = ps(bv, 0, w), ps(bv, w, 2 * w)
                inv = R("inv", t, slice(a, b))
                mm([(f, M(CV), inv), (fk, M(K8), on)], stop=False)
                mm([(f, M(A1), e0), (fk, M(N8192), e0), (f, M(A1), e1), (fk, M(N8192), e1), (f, M(A3), e2), (fk, M(N8192), e2)], start=False)
                tt(R("fv", slice(None), slice(a, b)), ps(bv, 0, 2 * w), R("nd", slice(None), slice(a, b)), A.min)
                tt(IND(R("bl"), S("dlu", a // 16, b // 16)), R("fv", 0, slice(a, b)), R("fv", 1, slice(a, b)), A.max)
                f, fk = ps(bn, 0, w), ps(bn, w, 2 * w)
                mm([(f, M(CV), inv), (f, M(A1), on), (fk, M(NI), on)], stop=False)
                mm([(f, M(NA1), e0), (fk, M(P8192), e0), (f, M(NA1), e1), (fk, M(P8192), e1), (f, M(O8192), e2)], start=False)
                tt(R("fn", slice(None), slice(a, b)), ps(bn, 0, 2 * w), R("nd", slice(None), slice(a, b)), A.min)
                tt(S("bl", n0 + a, n0 + b) if t == 0 else S("tv", a, b), R("fn", 0, slice(a, b)), R("fn", 1, slice(a, b)), A.max)
                gg = ps(bg, 0, w)
                mm([(gg, M(N8192), inv), (gg, M(ON17), e0), (gg, M(ON17), e1), (gg, M(ONES), e2)])
                act(S("s1", a, b), gg, F.Abs, bias=-72.0)
                um = S("um", a, b)
                act(um, S("s1", a, b), F.Relu, bias=-135.0)
                yy, ev, en = gg, ps(bg, 256, 256 + w // 2 * (t + 1)), ps(bg, 384, 384 + w // 2 * (t + 1))
                if t == 0:
                    mm([(yy, M(ID), S("wd", a, b)), (yy, M(N8192), um)])
                    act(S("win", Y1 + B + a, Y1 + B + b), yy, F.Relu)
                else:
                    mm([(ev, M(ON80), S("ca", a, b)), (ev, M(ON16), S("cb", a, b)), (ev, M(ONES), S("cc", a, b)), (en, M(ID), S("ii", a, b)),
                        (yy, M(ID), S("wd", a, b))], stop=False)
                    mm([(x, M(N8192), um) for x in (yy, ev, en)], start=False)
                    act(S("tt", a, b), ev, F.Relu)
                    act(S("tt", P + a, P + b), en, F.Relu, bias=128.0 + n0)
                    act(S("yon", ZB + P + a, ZB + P + b), yy, F.Relu)
            if t == 0:
                c0, n = CUT[-1], KB + 16 - CUT[-1]
                mm([(ps(7, r, 128, 16, n=n), S("win", Y1 + 16 * c0 + r, WEND, 16), S("st", 0, 8)) for r in range(16)])
                ts(dk(len(CUT), n), ps(7, 0, 128, n=n), 1407.5, A.is_lt, EPS, A.add)
                mm([(ps(6, 0, 16), W(P8, r), S("win", Y1 + B + r, WEND, 16)) for r in range(16)])
                ts(R("mw"), ps(6, 0, 16), 0.5, A.is_gt)
                for h, src in ((0, "dl"), (1, "nw")):
                    tt(S("e1", 192 * h + KB, 192 * h + KB + 16), R("mw"), R(src), A.mult)
                    cp(R("eu", h, slice(KB, KB + 16)), S("e1", 192 * h + KB, 192 * h + KB + 16))
            else:
                dma(T.yl[:, 0:n0], S("bl", 0, n0), lat=3000.0)
                dma(T.yl[:, n0:C], R("tv"))
                dma(T.yy[:, B:B + 2 * P], S("yon", ZB, ZB + 2 * P), eng="a")
                for h in range(2):
                    dma(T.ye[h::2, B + P:B + 2 * P], S("tt", P * h, P * h + P, part=slice(0, 128, 16)), eng="sa"[h])
        late.append(slot_tail)
    late[1]()

    emit(ops, queue, T)


def emit(ops, queue, T):
    n = len(ops)
    hist = {}
    deps = [set() for _ in range(n)]
    for k, o in enumerate(ops):
        for acc, wr in ((o["rd"], False), (o["wr"], True)):
            for name, lo, hi in acc:
                for j, l2, h2, w2 in hist.get(name, []):
                    if j != k and (wr or w2) and l2 < hi and lo < h2 and not (o.get("tag") and o.get("tag") == ops[j].get("tag")):
                        deps[k].add(j)
        for name, lo, hi in o["wr"]:
            hist[name] = [x for x in hist.get(name, []) if o.get("tag") or not (lo <= x[1] and x[2] <= hi)] + [(k, lo, hi, True)]
        for name, lo, hi in o["rd"]:
            hist.setdefault(name, []).append((k, lo, hi, False))

    def meet(u, v):
        return any(x[0] == y[0] and x[1] < y[2] and y[1] < x[2] for x in u for y in v)

    def free_edge(j, k):
        a, b = ops[j], ops[k]
        if a["e"] != b["e"] or a["kind"] != "c" or b["kind"] != "c":
            return False
        return a["e"] == "p" or not (meet(a["tw"], b["tr"] + b["tw"]) or meet(a["tr"], b["tw"]))
    above, full = [0] * n, list(deps)
    for k in range(n):
        a = 0
        for j in deps[k]:
            a |= above[j]
        above[k] = a | sum(1 << j for j in deps[k])
        deps[k] = set(j for j in deps[k] if not a >> j & 1)
    back = [[(j, ops[j]["lat"], 0.0 if free_edge(j, k) else 1.0) for j in deps[k]] + [(j, 0.0, 0.0) for j in ops[k].get("after", [])] for k in range(n)]
    succ, gap = [[] for _ in range(n)], [[] for _ in range(n)]
    for k in range(n):
        for j, l, h in back[k]:
            succ[j].append(k)
            gap[j].append(l + h * HOP)
    tail = [0.0] * n
    for k in range(n - 1, -1, -1):
        tail[k] = ops[k]["cost"] + ops[k]["lat"] + ops[k].get("lead", 0.0) + max([HOP + tail[j] for j in succ[k]] + [0.0])

    cost0, eng = [o["cost"] for o in ops], [o["e"] for o in ops]

    def plan(pri, look):
        left = [len(d) for d in back]
        ready = {e: [] for e in queue}
        at = [0.0] * n
        for k in range(n):
            if left[k] == 0:
                ready[ops[k]["e"]].append(k)
        free = {e: 0.0 for e in queue}
        order, start, end = [], [0.0] * n, 0.0
        pick, stale = {}, set(queue)
        while len(order) < n:
            for e in stale:
                rd = ready[e]
                if not rd:
                    pick.pop(e, None)
                    continue
                k = rd[0]
                if len(rd) > 1:
                    now = max(free[e], min([at[x] for x in rd]))
                    k = max([x for x in rd if at[x] <= now + 40], key=lambda x: pri[x])
                    soon = [j for j in rd if now + 40 < at[j] < now + look * cost0[k] and pri[j] > pri[k] + cost0[k]]
                    if soon:
                        j = max(soon, key=lambda x: pri[x])
                        fit = [x for x in rd if max(at[x], now) + cost0[x] <= at[j] + 60]
                        k = max(fit, key=lambda x: pri[x]) if fit else j
                pick[e] = (max(free[e], at[k]), k)
            st, k = min(pick.values())
            e = eng[k]
            stale = {e}
            ready[e].remove(k)
            order.append(k)
            start[k] = st
            f = free[e] = st + cost0[k]
            end = max(end, f + ops[k]["lat"])
            for j, gp in zip(succ[k], gap[k]):
                if f + gp > at[j]:
                    at[j] = f + gp
                left[j] -= 1
                if left[j] == 0:
                    ready[eng[j]].append(j)
                    stale.add(eng[j])
        return end, order, start

    plan0 = plan

    def priced(o, cy, ga, sc, fv, fa, pe, first):
        if o["kind"] != "c":
            return o["cost"] + first * (o["kind"] == "r2")
        if o["ng"] or o["ns"]:
            return 55.0 + cy * (ga * o["ng"] + sc * o["ns"])
        fix, new = {"v": (30, fv), "a": (70, fa), "g": (150, 150), "p": (0, 0)}[o["e"]]
        if o["e"] != "p" and any(x[0][:4] == "bank" for x in o["wr"]):
            new += PSX
        return new + (o["cost"] - fix) * (2 * pe if o["e"] == "p" else cy)
    cases = [([w * priced(o, cy, ga, sc, fv, fa, pe, first) for o in ops], [(k, w * o["lat"] * lat) for k, o in enumerate(ops) if o["lat"]],
              [[(j, w * (l * (lat if ops[j]["kind"] == "d" else rem) + h * hop)) for j, l, h in b] for b in back])
             for w, cy, ga, sc, fv, fa, pe, hop, lat, rem, first in CASES]

    def plan(pri, look):
        end, order, start = plan0(pri, look)
        for cost, hop, lat in cases:
            fin = [0.0] * n
            free = {e: 0.0 for e in queue}
            last = 0.0
            for k in order:
                s = free[eng[k]]
                for j, d in lat[k]:
                    x = fin[j] + d
                    if x > s:
                        s = x
                fin[k] = free[eng[k]] = s + cost[k]
            end += max([fin[k] + d for k, d in hop])
        return end / (1 + len(cases)), order, start

    slack = [0.0]

    def judge(order, a=0, old=None, first=0):
        end, crit, state = 0.0, [], {}
        prev0 = {e: -1 for e in queue}
        for k in order[:a]:
            prev0[eng[k]] = k
        rest = order[a:]
        for i in [first] + [x for x in range(len(cases)) if x != first]:
            cost, hop, lat = cases[i]
            fin, why = (old[i][0][:], old[i][1][:]) if old else ([0.0] * n, [-1] * n)
            prev = dict(prev0)
            for k in rest:
                p = prev[eng[k]]
                s = fin[p] if p >= 0 else 0.0
                w = -2 - p
                for j, d in lat[k]:
                    if fin[j] + d > s:
                        s = fin[j] + d
                        w = j
                fin[k] = s + cost[k]
                why[k] = w
                prev[eng[k]] = k
            last, k = max([(fin[k] + d, k) for k, d in hop])
            if old and i == first and last > old[i][2] + 2 * slack[0]:
                return 1e18, None, None
            state[i] = (fin, why, last)
            end += last
            while k != -1:
                w = why[k]
                if w < -1:
                    crit.append((-2 - w, k, i))
                    w = -2 - w
                k = w
        return end / len(cases), crit, state

    def improve(order, tries, rng):
        pre = [set(j for j, l, h in b) for b in back]
        post = [set() for _ in range(n)]
        for k in range(n):
            for j in pre[k]:
                post[j].add(k)
        end, crit, state = judge(order)
        top = (end, order)
        for trial in range(tries):
            slack[0] = TEMP * max(0.0, 1.0 - 1.15 * trial / tries)
            p, k, case = crit[rng.randint(len(crit))]
            e, far = eng[k], rng.randint(1, FAR) if trial % 2 else 1
            if trial % 4 < 2:
                b = a = order.index(k)
                while a > 0 and far:
                    a -= 1
                    far -= eng[order[a]] == e
                need, qs, go = set(pre[k]), set(), [k]
                for x in order[b - 1:a - 1 if a else None:-1]:
                    if x in need or eng[x] in qs:
                        go.append(x)
                        need |= pre[x]
                        qs.add(eng[x])
                if go[-1] == order[a]:
                    continue
                gs = set(go)
                new = order[:a] + go[::-1] + [x for x in order[a:b] if x not in gs] + order[b + 1:]
            else:
                b = a = order.index(p)
                while b < n - 1 and far:
                    b += 1
                    far -= eng[order[b]] == e
                need, qs, go = set(post[p]), set(), [p]
                for x in order[a + 1:b + 1]:
                    if x in need or eng[x] in qs:
                        go.append(x)
                        need |= post[x]
                        qs.add(eng[x])
                if go[-1] == order[b]:
                    continue
                gs = set(go)
                new = order[:a] + [x for x in order[a + 1:b + 1] if x not in gs] + go + order[b + 1:]
            e2, c2, s2 = judge(new, a, state, case)
            if e2 <= end + slack[0] * rng.rand() ** 2:
                end, crit, order, state = e2, c2, new, s2
                if end < top[0]:
                    top = (end, order)
        return top

    rng = np.random.RandomState(7)
    base = np.array([tail[k] + (1e6 if ops[k]["kind"] != "c" else 0.0) - 1e-3 * k for k in range(n)])
    if n not in PLANS:
        found = []
        for start in range(STARTS):
            best = None
            for trial in range(20):
                pri, look = base + (0.0, 100.0, 400.0, 1200.0)[trial // 5] * rng.rand(n), (0.0, 0.3, 0.5, 0.7, 0.9)[trial % 5]
                end = plan(list(pri), look)[0]
                if best is None or end < best[0]:
                    best = (end, pri, look)
            for trial in range(TRIES):
                pri = best[1].copy()
                a = rng.randint(n)
                if trial % 2:
                    pri[a:a + rng.randint(1, 40)] += rng.randn() * 3000.0
                else:
                    pri[a:a + 120] += rng.randn(len(pri[a:a + 120])) * 500.0
                look = best[2] if trial % 7 else rng.rand()
                end = plan(list(pri), look)[0]
                if end <= best[0]:
                    best = (end, pri, look)
            found.append(improve(plan(list(best[1]), best[2])[1], MOVES // 40, rng))
        PLANS[n] = improve(min(found)[1], MOVES, rng)
    end, order = PLANS[n]
    DBG.update(ops=ops, order=order, cases=cases, eng=eng)
    pos = {k: i for i, k in enumerate(order)}
    need = [False] * n
    waits = [[] for _ in range(n)]
    seen = {e: {} for e in queue}
    known = {}
    for k in order:
        e = ops[k]["e"]
        last = {}
        for j in full[k]:
            key = ops[j]["e"] if ops[j]["kind"] == "c" else j
            if free_edge(j, k):
                continue
            if key not in last or pos[j] > pos[last[key]]:
                last[key] = j
        for key, j in sorted(last.items(), key=lambda x: -pos[x[1]]):
            if seen[e].get(key, -1) < pos[j]:
                seen[e][key] = pos[j]
                need[j] = True
                waits[k].append(j)
                for x, p in known[j].items() if ops[j]["kind"] in "cd" else ():
                    if seen[e].get(x, -1) < p:
                        seen[e][x] = p
        known[k] = dict(seen[e])
    sig = {}
    cnt = {e: 0 for e in queue}
    nd = 0
    ends = []
    for k in order:
        o = ops[k]
        e = queue[o["e"]]
        for j in waits[k]:
            e.wait_ge(*sig[j])
        r = o["fn"](e)
        if o["kind"] == "d":
            s = T.sem["d%d" % nd]
            nd += 1
            r.then_inc(s, 16)
            sig[k] = (s, 16)
            if not need[k]:
                ends.append(sig[k])
        elif o["kind"] == "c":
            if need[k]:
                cnt[o["e"]] += 1
                s = T.sem["q" + o["e"]]
                r.then_inc(s, 1)
                sig[k] = (s, cnt[o["e"]])
        else:
            sig[k] = (T.sem["arr" + o["kind"][1]], 14)
            ends.append((T.sem["out" + o["kind"][1]], 14))
    for s in ends:
        queue["s"].wait_ge(*s)
    return end
